import numpy as np
import ml_dtypes


def mxq(x, axis, fmt="e4m3"):
    dtype, down = {"e4m3": (ml_dtypes.float8_e4m3fn, 7), "e5m2": (ml_dtypes.float8_e5m2, 14)}[fmt]
    v = np.moveaxis(np.asarray(x, np.float32).astype(ml_dtypes.bfloat16).astype(np.float64), axis, -1)
    blocks = v.reshape(v.shape[:-1] + (-1, 32))
    amax = np.abs(blocks).max(-1, keepdims=True)
    byte = np.maximum(np.where(amax > 0, np.frexp(amax)[1] - 1 + 127, 0) - down, 1)
    scale = np.exp2(byte - 127.0)
    codes = (blocks / scale).astype(np.float32).astype(dtype).astype(np.float64)
    return np.moveaxis((codes * scale).reshape(v.shape), -1, axis)


WIDE = False


def mx_kscale(k):
    if not WIDE:
        return np.ones(k)
    levels = np.array([24, -24, 12, -12, 0])
    if k % 512:
        return np.exp2(np.random.permutation(np.resize(levels, k // 32))).repeat(32)
    a = np.empty((k // 512, 16))
    for p in range(k // 512):
        a[p, :8] = np.random.permutation(np.resize(levels, 8))
        for g in range(8):
            far = levels[np.abs(levels - a[p, g]) >= 10]
            a[p, g + 8] = far[np.random.randint(len(far))]
    return np.exp2(a.ravel()).repeat(32)


def f64(x):
    return np.asarray(x).astype(np.float64)


def striped(idx):
    return np.tile(idx.reshape(-1, 16).T, (8, 1)).astype(np.uint16)


def unstriped(offs):
    return offs[:16].T.reshape(-1).astype(np.int64)


E2M1 = np.array([0.0, 0.5, 1.0, 1.5, 2.0, 3.0, 4.0, 6.0, -0.0, -0.5, -1.0, -1.5, -2.0, -3.0, -4.0, -6.0])


def pack_weight(w, fmt):
    k, n = w.shape
    w = f64(np.asarray(w, np.float32).astype(ml_dtypes.bfloat16)).reshape(k // 32, 32, n)
    amax = np.abs(w).max(1)
    if fmt == "e4m3":
        byte = np.frexp(amax)[1] - 1 + 127 - 7
    else:
        mant, ex = np.frexp(amax / 6.0)
        byte = np.where(mant > 0.5, ex, ex - 1) + 127
    byte = np.clip(np.where(amax > 0, byte, 1), 1, 254)
    scaled = (w * np.exp2(127.0 - byte)[:, None, :]).reshape(k, n).astype(np.float32)
    by_word = np.ascontiguousarray(scaled.reshape(k // 512, 128, 4, n).transpose(0, 1, 3, 2))
    if fmt == "e4m3":
        words = by_word.astype(ml_dtypes.float8_e4m3fn).view(np.uint8)
    else:
        c = by_word.astype(ml_dtypes.float4_e2m1fn).view(np.uint8) & 0xF
        words = (c[..., 0::2] | (c[..., 1::2] << 4)).reshape(k // 512, 128, 2 * n)
    return np.ascontiguousarray(words), np.ascontiguousarray(byte.astype(np.uint8).reshape(k // 512, 16, n))


def unpack_weight(words, scales, fmt):
    g, _, n = scales.shape
    words = np.ascontiguousarray(words).reshape(g, 128, n, -1)
    if fmt == "e4m3":
        vals = words.view(ml_dtypes.float8_e4m3fn).astype(np.float64)
    else:
        nib = np.empty((g, 128, n, 4), np.uint8)
        nib[..., 0::2] = words & 0xF
        nib[..., 1::2] = words >> 4
        vals = E2M1[nib]
    vals = vals * np.repeat(np.exp2(scales.astype(np.float64) - 127.0), 8, axis=1)[..., None]
    return vals.transpose(0, 1, 3, 2).reshape(g * 512, n)


def silu(f):
    return f / (1.0 + np.exp(-np.maximum(f, -700.0)))


K, L, N, T, J = 512, 512, 1024, 2048, 1024


def setup_inputs():
    n = np.random.standard_normal
    s = mx_kscale(K)[:, None]
    s2 = mx_kscale(L)[:, None]
    p_tab = pack_weight(n((K, T)) * s, "e4m3")
    p_wt4 = pack_weight(n((K, N)) / np.sqrt(K) / s, "e2m1")
    p_wx = pack_weight(n((L, N)) / np.sqrt(L) / s2, "e2m1")
    return {
        "tab_words": p_tab[0],
        "tab_scales": p_tab[1],
        "wt4_words": p_wt4[0],
        "wt4_scales": p_wt4[1],
        "wtd": (0.4 * (n((K, N)) / np.sqrt(K) / s)).astype(np.float32),
        "x": (n((L, J)) * s2).astype(np.float32),
        "wx_words": p_wx[0],
        "wx_scales": p_wx[1],
        "b": (0.3 * n(N)).astype(np.float32),
        "offs": striped(np.random.permutation(T)[:J]),
    }


def reference(tab_words, tab_scales, wt4_words, wt4_scales, wtd, x, wx_words, wx_scales, b, offs):
    idx = unstriped(offs)
    tab_ = unpack_weight(tab_words, tab_scales, "e4m3")[:, idx]
    wt4_ = unpack_weight(wt4_words, wt4_scales, "e2m1")
    wtd_ = mxq(f64(wtd), 0, "e4m3")
    x_q_ = mxq(f64(x), 0, "e4m3")
    x_r_ = mxq(f64(x) - x_q_, 0, "e4m3")
    wx_ = unpack_weight(wx_words, wx_scales, "e2m1")
    y = wt4_.T @ tab_ + wtd_.T @ tab_ + wx_.T @ x_q_ + wx_.T @ x_r_
    return silu(y + f64(b)[:, None])

@@ -1,0 +1,266 @@
+from contextlib import ExitStack
+
+import concourse.mybir as mybir
+from concourse.masks import make_identity
+
+K, L, N, T, J = 512, 512, 1024, 2048, 1024
+FLOPS = 4 * 2 * K * N * J + 2 * L * L * J
+
+F32 = mybir.dt.float32
+BF16 = mybir.dt.bfloat16
+I32 = mybir.dt.int32
+U32 = mybir.dt.uint32
+U16 = mybir.dt.uint16
+U8 = mybir.dt.uint8
+FP8X4 = mybir.dt.float8_e4m3fn_x4
+FP4X4 = mybir.dt.float4_e2m1fn_x4
+SILU = mybir.ActivationFunctionType.Silu
+SUB = mybir.AluOpType.subtract
+
+P = 128
+PACK = 4
+HALF = 512
+CHUNK = 256
+RUN = 4
+WARM_PASSES = 18
+
+
+def by_runs_packed(ap):
+    return ap.rearrange("p (c i) t -> p c t i", i=RUN)
+
+
+def by_runs_planes(ap):
+    return ap.rearrange("p t (c i) -> p c t i", i=RUN)
+
+
+def tile_list_tiert_xdl_silu_kernel(
+    tc, tab_words, tab_scales, wt4_words, wt4_scales, wtd, x, wx_words, wx_scales, b, offs, out
+):
+    nc = tc.nc
+    with ExitStack() as ctx:
+        keep = ctx.enter_context(tc.tile_pool(name="keep", bufs=1))
+        alias = ctx.enter_context(tc.tile_pool(name="alias", bufs=1))
+        res_pool = ctx.enter_context(tc.tile_pool(name="res", bufs=6))
+        psum = ctx.enter_context(tc.psum_pool(name="psum", bufs=1))
+
+        def bank(i):
+            return psum.tile([P, HALF], F32, name="bank%d" % i)
+
+        offsets = keep.tile([P, J // 16], U16, name="offsets")
+        tab_w = keep.tile([P, T], I32, name="tab_w", align_bytes=64)
+        tab_s = keep.tile([P, T], U8, name="tab_s", align_bytes=64)
+        wt4_w = keep.tile([P, 2 * N], U8, name="wt4_w", align_bytes=64)
+        wt4_s = keep.tile([P, N], U8, name="wt4_s", align_bytes=64)
+        wx_w = keep.tile([P, 2 * N], U8, name="wx_w", align_bytes=64)
+        wx_s = keep.tile([P, N], U8, name="wx_s", align_bytes=64)
+        x_raw = [keep.tile([P, PACK, CHUNK], F32, name="x_raw%d" % c, align_bytes=64) for c in range(J // CHUNK)]
+        d_raw = [keep.tile([P, PACK, CHUNK], F32, name="d_raw%d" % c, align_bytes=64) for c in range(N // CHUNK)]
+        d_bf = [keep.tile([P, CHUNK, PACK], BF16, name="d_bf%d" % c, align_bytes=64) for c in range(N // CHUNK)]
+        r_bf = [keep.tile([P, CHUNK, PACK], BF16, name="r_bf%d" % c, align_bytes=64) for c in (0, 2, 3)]
+        r_bf.insert(1, alias.tile([P, CHUNK, PACK], BF16, name="r_bf1", align_bytes=64, offset=0))
+        xq_w = [keep.tile([P, HALF], U32, name="xq_w%d" % h, align_bytes=64) for h in range(2)]
+        xq_s = [keep.tile([P, HALF], U8, name="xq_s%d" % h, align_bytes=64) for h in range(2)]
+        xr_w = [keep.tile([P, HALF], U32, name="xr_w%d" % h, align_bytes=64) for h in range(2)]
+        xr_s = [keep.tile([P, HALF], U8, name="xr_s%d" % h, align_bytes=64) for h in range(2)]
+        wd_w = [keep.tile([P, CHUNK], U32, name="wd_w%d" % c, align_bytes=64) for c in range(N // CHUNK)]
+        wd_s = [keep.tile([P, CHUNK], U8, name="wd_s%d" % c, align_bytes=64) for c in range(N // CHUNK)]
+        got_w, got_s = [], []
+        ident = keep.tile([P, P], F32, name="ident")
+        id_bf = keep.tile([P, PACK - 1, P * PACK], BF16, name="x_bf0", align_bytes=64)
+        diag = keep.tile([P, PACK * P + PACK], BF16, name="diag", align_bytes=64)
+        id_w = [keep.tile([P, P], U32, name="id_w%d" % t, align_bytes=64) for t in range(PACK)]
+        id_s = [keep.tile([P, P], U8, name="id_s%d" % t, align_bytes=64) for t in range(PACK)]
+        b_rows = keep.tile([P, P], F32, name="b_rows")
+        b_early = keep.tile([P, N // P], F32, name="b_early")
+        warm = keep.tile([P, 8], F32, name="warm")
+
+        x_v = x.rearrange("(p t) j -> p t j", t=PACK)
+        d_v = wtd.rearrange("(p t) n -> p t n", t=PACK)
+
+        def load_scales(queue, plane, rows):
+            for r in range(4):
+                queue.dma_start(out=plane[r:P:32, :].bitcast(I32), in_=rows[0, r:16:4, :].bitcast(I32))
+
+        def load_chunk(dst, src, c):
+            nc.sync.dma_start(out=dst[c][:], in_=src[:, :, c * CHUNK : (c + 1) * CHUNK])
+
+        def pack(engine, dst, src):
+            if engine == "vector":
+                nc.vector.tensor_copy(out=by_runs_packed(dst[:]), in_=by_runs_planes(src[:]))
+            else:
+                nc.scalar.copy(out=by_runs_packed(dst[:]), in_=by_runs_planes(src[:]))
+
+        def quant(words, scales, src, c):
+            per_tile = words[0].shape[1] // CHUNK
+            i, lo = c // per_tile, (c % per_tile) * CHUNK
+            nc.vector.quantize_mx(
+                out=words[i][:, lo : lo + CHUNK].bitcast(FP8X4),
+                scales=scales[i][:, lo : lo + CHUNK],
+                in_=src[c][:].rearrange("p c t -> p (c t)"),
+            )
+
+        def dequant(dst, jj):
+            h, cols = jj // 4, slice((jj % 4) * P, (jj % 4 + 1) * P)
+            for t in range(PACK):
+                m = slice(t * P, (t + 1) * P)
+                nc.tensor.matmul_mx(
+                    out=dst[:, m], lhsT=id_w[t][:].bitcast(FP8X4), lhsT_scale=id_s[t][:],
+                    rhs=xq_w[h][:, cols].bitcast(FP8X4), rhs_scale=xq_s[h][:, cols], start=True, stop=True,
+                )
+
+        def residual(src, jj):
+            c, lo = jj // 2, (jj % 2) * P
+            nc.vector.tensor_tensor(
+                out=by_runs_packed(r_bf[c][:, lo : lo + P, :]),
+                in0=by_runs_planes(x_raw[c][:, :, lo : lo + P]),
+                in1=src[:].rearrange("p (t c i) -> p c t i", t=PACK, i=RUN),
+                op=SUB,
+            )
+
+        def gather(h):
+            lst = offsets[:, h * (HALF // 16) : (h + 1) * (HALF // 16)]
+            nc.vector.tensor_copy(out=got_w[h][:], in_=tab_w[:].bitcast(U32).indirect(lst))
+            nc.vector.tensor_copy(out=got_s[h][:], in_=tab_s[:].indirect(lst))
+
+        def mm(acc, kind, n, h, start, stop):
+            m = slice(n * P, (n + 1) * P)
+            m2 = slice(2 * n * P, 2 * (n + 1) * P)
+            md = slice((n % 2) * P, (n % 2 + 1) * P)
+            if kind == "wt4":
+                w, ws, a, s = wt4_w[:, m2].bitcast(FP4X4), wt4_s[:, m], got_w[h][:], got_s[h][:]
+            elif kind == "wtd":
+                w, ws, a, s = wd_w[n // 2][:, md].bitcast(FP8X4), wd_s[n // 2][:, md], got_w[h][:], got_s[h][:]
+            elif kind == "xq":
+                w, ws, a, s = wx_w[:, m2].bitcast(FP4X4), wx_s[:, m], xq_w[h][:], xq_s[h][:]
+            else:
+                w, ws, a, s = wx_w[:, m2].bitcast(FP4X4), wx_s[:, m], xr_w[h][:], xr_s[h][:]
+            nc.tensor.matmul_mx(
+                out=acc[:], lhsT=w, lhsT_scale=ws, rhs=a.bitcast(FP8X4), rhs_scale=s, start=start, stop=stop
+            )
+
+        def finish(acc, n, h):
+            res = res_pool.tile([P, HALF], F32, name="res")
+            nc.scalar.activation(out=res[:], in_=acc[:], func=SILU, bias=b_cols[:, n : n + 1])
+            nc.sync.dma_start(out=out[n * P : (n + 1) * P, h * HALF : (h + 1) * HALF], in_=res[:])
+
+        nc.gpsimd.memset(diag[:].bitcast(I32), 0)
+        nc.gpsimd.affine_select(
+            out=diag[:], in_=diag[:], pattern=[[1, PACK * P + PACK]], compare_op=mybir.AluOpType.not_equal,
+            fill=1.0, base=-(PACK - 1), channel_multiplier=-PACK,
+        )
+        make_identity(nc, ident[:])
+        last = PACK - 1
+        nc.vector.quantize_mx(out=id_w[last][:].bitcast(FP8X4), scales=id_s[last][:], in_=diag[:, 0 : P * PACK])
+        nc.vector.memset(warm[:], 0.0)
+        nc.scalar.activation(out=warm[:], in_=warm[:], func=SILU)
+        nc.vector.memset(b_rows[:], 0.0)
+        nc.vector.memset(wx_s[:].bitcast(I32), 0)
+        nc.vector.memset(tab_s[:].bitcast(I32), 0)
+        nc.vector.memset(wt4_s[:].bitcast(I32), 0)
+
+        load_chunk(x_raw, x_v, 0)
+        nc.sync.dma_start(out=b_rows[0 : N // P, :], in_=b.rearrange("(c p) -> c p", p=P))
+        load_chunk(x_raw, x_v, 1)
+        nc.sync.dma_start(out=wx_w[:].bitcast(I32), in_=wx_words[0].bitcast(I32))
+        load_scales(nc.sync, wx_s, wx_scales)
+        nc.sync.dma_start(out=tab_w[:], in_=tab_words[0].rearrange("p n t -> p (n t)").bitcast(I32))
+        load_scales(nc.sync, tab_s, tab_scales)
+        nc.sync.dma_start(offsets[:], offs)
+        nc.sync.dma_start(out=wt4_w[:].bitcast(I32), in_=wt4_words[0].bitcast(I32))
+        load_chunk(d_raw, d_v, 0)
+        load_scales(nc.sync, wt4_s, wt4_scales)
+        load_chunk(d_raw, d_v, 1)
+        load_chunk(d_raw, d_v, 2)
+        load_chunk(d_raw, d_v, 3)
+        load_chunk(x_raw, x_v, 2)
+        load_chunk(x_raw, x_v, 3)
+
+        for t in range(last):
+            nc.vector.tensor_copy(out=id_bf[:, t, :], in_=diag[:, last - t : last - t + P * PACK])
+        for t in range(last):
+            nc.vector.quantize_mx(out=id_w[t][:].bitcast(FP8X4), scales=id_s[t][:], in_=id_bf[:, t, :])
+        idle = bank(3)
+        for i in range(WARM_PASSES):
+            nc.tensor.matmul_mx(
+                out=idle[:, (i % PACK) * P : (i % PACK + 1) * P],
+                lhsT=id_w[last][:].bitcast(FP8X4), lhsT_scale=id_s[last][:],
+                rhs=id_w[last][:].bitcast(FP8X4), rhs_scale=id_s[last][:], start=True, stop=True,
+            )
+        b_t = bank(3)
+        nc.tensor.transpose(b_t[:, 0:P], b_rows[:], ident[:])
+        nc.scalar.copy(out=b_early[:], in_=b_t[:, 0 : N // P])
+
+        x_bf = [keep.tile([P, CHUNK, PACK], BF16, name="x_bf0", align_bytes=64)]
+        pack("vector", x_bf[0], x_raw[0])
+        quant(xq_w, xq_s, x_bf, 0)
+        x_bf.append(keep.tile([P, CHUNK, PACK], BF16, name="x_bf0", align_bytes=64))
+        pack("scalar", x_bf[1], x_raw[1])
+        back = [bank(4 + jj) for jj in range(4)]
+        dequant(back[0], 0)
+        dequant(back[1], 1)
+        residual(back[0], 0)
+        quant(xq_w, xq_s, x_bf, 1)
+        residual(back[1], 1)
+        dequant(back[2], 2)
+        dequant(back[3], 3)
+        acc = [bank(n) for n in range(4)]
+        for n in range(4):
+            mm(acc[n], "xq", n, 0, True, False)
+        residual(back[2], 2)
+        quant(xr_w, xr_s, r_bf, 0)
+        residual(back[3], 3)
+        quant(xr_w, xr_s, r_bf, 1)
+        acc += [bank(n) for n in range(4, 8)]
+        for n in range(4, 8):
+            mm(acc[n], "xq", n, 0, True, False)
+        for n in range(8):
+            mm(acc[n], "xr", n, 0, False, False)
+        got_w.append(alias.tile([P, HALF], U32, name="got_w0", align_bytes=64, offset=1536))
+        got_s.append(alias.tile([P, HALF], U8, name="got_s0", align_bytes=64, offset=0))
+        gather(0)
+        for n in range(8):
+            mm(acc[n], "wt4", n, 0, False, False)
+        for c in range(4):
+            pack("scalar", d_bf[c], d_raw[c])
+            quant(wd_w, wd_s, d_bf, c)
+        got_w.append(keep.tile([P, HALF], U32, name="d_bf0", align_bytes=64))
+        got_s.append(keep.tile([P, HALF], U8, name="d_bf2", align_bytes=64))
+        gather(1)
+        b_cols = keep.tile([P, N // P], F32, name="d_raw3", align_bytes=64)
+        nc.scalar.copy(out=b_cols[:], in_=b_early[:])
+        for n in range(8):
+            mm(acc[n], "wtd", n, 0, False, True)
+            finish(acc[n], n, 0)
+
+        x_bf.append(keep.tile([P, CHUNK, PACK], BF16, name="d_bf3", align_bytes=64))
+        pack("vector", x_bf[2], x_raw[2])
+        back = [bank(4 + jj) for jj in range(4)]
+        quant(xq_w, xq_s, x_bf, 2)
+        dequant(back[0], 4)
+        dequant(back[1], 5)
+        x_bf.append(keep.tile([P, CHUNK, PACK], BF16, name="d_bf3", align_bytes=64))
+        pack("vector", x_bf[3], x_raw[3])
+        quant(xq_w, xq_s, x_bf, 3)
+        dequant(back[2], 6)
+        dequant(back[3], 7)
+        for jj in range(3):
+            residual(back[jj], 4 + jj)
+        quant(xr_w, xr_s, r_bf, 2)
+        residual(back[3], 7)
+        quant(xr_w, xr_s, r_bf, 3)
+        acc = [bank(n) for n in range(4)]
+        for n in range(4):
+            mm(acc[n], "wt4", n, 1, True, False)
+            mm(acc[n], "wtd", n, 1, False, False)
+        for n in range(4):
+            mm(acc[n], "xq", n, 1, False, False)
+        for n in range(4):
+            mm(acc[n], "xr", n, 1, False, True)
+            finish(acc[n], n, 1)
+        for n in range(4, 8):
+            acc.append(bank(n))
+            mm(acc[n], "wt4", n, 1, True, False)
+            mm(acc[n], "wtd", n, 1, False, False)
+            mm(acc[n], "xq", n, 1, False, False)
+            mm(acc[n], "xr", n, 1, False, True)
+            finish(acc[n], n, 1)

@@ -22,6 +22,7 @@ PACK = 4
 HALF = 512
 CHUNK = 256
 RUN = 4
+HEAD_SPLIT = 160
 WARM_PASSES = 18
 
 
@@ -84,11 +85,11 @@ def tile_list_tiert_xdl_silu_kernel(
         def load_chunk(dst, src, c):
             nc.sync.dma_start(out=dst[c][:], in_=src[:, :, c * CHUNK : (c + 1) * CHUNK])
 
-        def pack(engine, dst, src):
-            if engine == "vector":
-                nc.vector.tensor_copy(out=by_runs_packed(dst[:]), in_=by_runs_planes(src[:]))
-            else:
-                nc.scalar.copy(out=by_runs_packed(dst[:]), in_=by_runs_planes(src[:]))
+        def pack(dst, src, split):
+            if split > 0:
+                nc.vector.tensor_copy(out=by_runs_packed(dst[:, 0:split, :]), in_=by_runs_planes(src[:, :, 0:split]))
+            if split < CHUNK:
+                nc.scalar.copy(out=by_runs_packed(dst[:, split:CHUNK, :]), in_=by_runs_planes(src[:, :, split:CHUNK]))
 
         def quant(words, scales, src, c):
             per_tile = words[0].shape[1] // CHUNK
@@ -122,26 +123,28 @@ def tile_list_tiert_xdl_silu_kernel(
             nc.vector.tensor_copy(out=got_w[h][:], in_=tab_w[:].bitcast(U32).indirect(lst))
             nc.vector.tensor_copy(out=got_s[h][:], in_=tab_s[:].indirect(lst))
 
-        def mm(acc, kind, n, h, start, stop):
+        def mm(acc, kind, n, h, start, stop, lo=0, width=HALF):
             m = slice(n * P, (n + 1) * P)
             m2 = slice(2 * n * P, 2 * (n + 1) * P)
             md = slice((n % 2) * P, (n % 2 + 1) * P)
             if kind == "wt4":
-                w, ws, a, s = wt4_w[:, m2].bitcast(FP4X4), wt4_s[:, m], got_w[h][:], got_s[h][:]
+                w, ws, a, s = wt4_w[:, m2].bitcast(FP4X4), wt4_s[:, m], got_w[h], got_s[h]
             elif kind == "wtd":
-                w, ws, a, s = wd_w[n // 2][:, md].bitcast(FP8X4), wd_s[n // 2][:, md], got_w[h][:], got_s[h][:]
+                w, ws, a, s = wd_w[n // 2][:, md].bitcast(FP8X4), wd_s[n // 2][:, md], got_w[h], got_s[h]
             elif kind == "xq":
-                w, ws, a, s = wx_w[:, m2].bitcast(FP4X4), wx_s[:, m], xq_w[h][:], xq_s[h][:]
+                w, ws, a, s = wx_w[:, m2].bitcast(FP4X4), wx_s[:, m], xq_w[h], xq_s[h]
             else:
-                w, ws, a, s = wx_w[:, m2].bitcast(FP4X4), wx_s[:, m], xr_w[h][:], xr_s[h][:]
+                w, ws, a, s = wx_w[:, m2].bitcast(FP4X4), wx_s[:, m], xr_w[h], xr_s[h]
             nc.tensor.matmul_mx(
-                out=acc[:], lhsT=w, lhsT_scale=ws, rhs=a.bitcast(FP8X4), rhs_scale=s, start=start, stop=stop
+                out=acc[:, 0:width], lhsT=w, lhsT_scale=ws,
+                rhs=a[:, lo : lo + width].bitcast(FP8X4), rhs_scale=s[:, lo : lo + width], start=start, stop=stop,
             )
 
-        def finish(acc, n, h):
-            res = res_pool.tile([P, HALF], F32, name="res")
-            nc.scalar.activation(out=res[:], in_=acc[:], func=SILU, bias=b_cols[:, n : n + 1])
-            nc.sync.dma_start(out=out[n * P : (n + 1) * P, h * HALF : (h + 1) * HALF], in_=res[:])
+        def finish(acc, n, h, lo=0, width=HALF):
+            res = res_pool.tile([P, width], F32, name="res")
+            nc.scalar.activation(out=res[:], in_=acc[:, 0:width], func=SILU, bias=b_cols[:, n : n + 1])
+            j0 = h * HALF + lo
+            nc.sync.dma_start(out=out[n * P : (n + 1) * P, j0 : j0 + width], in_=res[:])
 
         nc.gpsimd.memset(diag[:].bitcast(I32), 0)
         nc.gpsimd.affine_select(
@@ -168,8 +171,8 @@ def tile_list_tiert_xdl_silu_kernel(
         nc.sync.dma_start(offsets[:], offs)
         nc.sync.dma_start(out=wt4_w[:].bitcast(I32), in_=wt4_words[0].bitcast(I32))
         load_chunk(d_raw, d_v, 0)
-        load_scales(nc.sync, wt4_s, wt4_scales)
         load_chunk(d_raw, d_v, 1)
+        load_scales(nc.sync, wt4_s, wt4_scales)
         load_chunk(d_raw, d_v, 2)
         load_chunk(d_raw, d_v, 3)
         load_chunk(x_raw, x_v, 2)
@@ -191,18 +194,18 @@ def tile_list_tiert_xdl_silu_kernel(
         nc.scalar.copy(out=b_early[:], in_=b_t[:, 0 : N // P])
 
         x_bf = [keep.tile([P, CHUNK, PACK], BF16, name="x_bf0", align_bytes=64)]
-        pack("vector", x_bf[0], x_raw[0])
+        pack(x_bf[0], x_raw[0], HEAD_SPLIT)
         quant(xq_w, xq_s, x_bf, 0)
         x_bf.append(keep.tile([P, CHUNK, PACK], BF16, name="x_bf0", align_bytes=64))
-        pack("scalar", x_bf[1], x_raw[1])
+        pack(x_bf[1], x_raw[1], HEAD_SPLIT)
         back = [bank(4 + jj) for jj in range(4)]
         dequant(back[0], 0)
         dequant(back[1], 1)
-        residual(back[0], 0)
         quant(xq_w, xq_s, x_bf, 1)
-        residual(back[1], 1)
         dequant(back[2], 2)
         dequant(back[3], 3)
+        residual(back[0], 0)
+        residual(back[1], 1)
         acc = [bank(n) for n in range(4)]
         for n in range(4):
             mm(acc[n], "xq", n, 0, True, False)
@@ -221,7 +224,7 @@ def tile_list_tiert_xdl_silu_kernel(
         for n in range(8):
             mm(acc[n], "wt4", n, 0, False, False)
         for c in range(4):
-            pack("scalar", d_bf[c], d_raw[c])
+            pack(d_bf[c], d_raw[c], 0)
             quant(wd_w, wd_s, d_bf, c)
         got_w.append(keep.tile([P, HALF], U32, name="d_bf0", align_bytes=64))
         got_s.append(keep.tile([P, HALF], U8, name="d_bf2", align_bytes=64))
@@ -233,34 +236,28 @@ def tile_list_tiert_xdl_silu_kernel(
             finish(acc[n], n, 0)
 
         x_bf.append(keep.tile([P, CHUNK, PACK], BF16, name="d_bf3", align_bytes=64))
-        pack("vector", x_bf[2], x_raw[2])
-        back = [bank(4 + jj) for jj in range(4)]
+        pack(x_bf[2], x_raw[2], CHUNK)
         quant(xq_w, xq_s, x_bf, 2)
+        back = [bank(0), bank(1)]
         dequant(back[0], 4)
         dequant(back[1], 5)
         x_bf.append(keep.tile([P, CHUNK, PACK], BF16, name="d_bf3", align_bytes=64))
-        pack("vector", x_bf[3], x_raw[3])
+        pack(x_bf[3], x_raw[3], CHUNK)
+        residual(back[0], 4)
         quant(xq_w, xq_s, x_bf, 3)
-        dequant(back[2], 6)
-        dequant(back[3], 7)
-        for jj in range(3):
-            residual(back[jj], 4 + jj)
+        residual(back[1], 5)
+        back = [bank(0), bank(1)]
+        dequant(back[0], 6)
+        dequant(back[1], 7)
         quant(xr_w, xr_s, r_bf, 2)
-        residual(back[3], 7)
+        residual(back[0], 6)
+        residual(back[1], 7)
         quant(xr_w, xr_s, r_bf, 3)
-        acc = [bank(n) for n in range(4)]
-        for n in range(4):
-            mm(acc[n], "wt4", n, 1, True, False)
-            mm(acc[n], "wtd", n, 1, False, False)
-        for n in range(4):
-            mm(acc[n], "xq", n, 1, False, False)
-        for n in range(4):
-            mm(acc[n], "xr", n, 1, False, True)
-            finish(acc[n], n, 1)
-        for n in range(4, 8):
-            acc.append(bank(n))
-            mm(acc[n], "wt4", n, 1, True, False)
-            mm(acc[n], "wtd", n, 1, False, False)
-            mm(acc[n], "xq", n, 1, False, False)
-            mm(acc[n], "xr", n, 1, False, True)
-            finish(acc[n], n, 1)
+        pieces = [(n, (n + 2) % 8, 0, HALF) for n in range(7)] + [(7, 1 + i, i * P, P) for i in range(4)]
+        for n, i, lo, width in pieces:
+            last_acc = bank(i)
+            mm(last_acc, "wt4", n, 1, True, False, lo, width)
+            mm(last_acc, "wtd", n, 1, False, False, lo, width)
+            mm(last_acc, "xq", n, 1, False, False, lo, width)
+            mm(last_acc, "xr", n, 1, False, True, lo, width)
+            finish(last_acc, n, 1, lo, width)

@@ -48,29 +48,29 @@ def tile_list_tiert_xdl_silu_kernel(
             return psum.tile([P, HALF], F32, name="bank%d" % i)
 
         offsets = keep.tile([P, J // 16], U16, name="offsets")
-        tab_w = keep.tile([P, T], I32, name="tab_w", align_bytes=64)
-        tab_s = keep.tile([P, T], U8, name="tab_s", align_bytes=64)
-        wt4_w = keep.tile([P, 2 * N], U8, name="wt4_w", align_bytes=64)
-        wt4_s = keep.tile([P, N], U8, name="wt4_s", align_bytes=64)
-        wx_w = keep.tile([P, 2 * N], U8, name="wx_w", align_bytes=64)
-        wx_s = keep.tile([P, N], U8, name="wx_s", align_bytes=64)
-        x_raw = [keep.tile([P, PACK, CHUNK], F32, name="x_raw%d" % c, align_bytes=64) for c in range(J // CHUNK)]
-        d_raw = [keep.tile([P, PACK, CHUNK], F32, name="d_raw%d" % c, align_bytes=64) for c in range(N // CHUNK)]
-        d_bf = [keep.tile([P, CHUNK, PACK], BF16, name="d_bf%d" % c, align_bytes=64) for c in range(N // CHUNK)]
-        r_bf = [keep.tile([P, CHUNK, PACK], BF16, name="r_bf%d" % c, align_bytes=64) for c in (0, 2, 3)]
-        r_bf.insert(1, alias.tile([P, CHUNK, PACK], BF16, name="r_bf1", align_bytes=64, offset=0))
-        xq_w = [keep.tile([P, HALF], U32, name="xq_w%d" % h, align_bytes=64) for h in range(2)]
-        xq_s = [keep.tile([P, HALF], U8, name="xq_s%d" % h, align_bytes=64) for h in range(2)]
-        xr_w = [keep.tile([P, HALF], U32, name="xr_w%d" % h, align_bytes=64) for h in range(2)]
-        xr_s = [keep.tile([P, HALF], U8, name="xr_s%d" % h, align_bytes=64) for h in range(2)]
-        wd_w = [keep.tile([P, CHUNK], U32, name="wd_w%d" % c, align_bytes=64) for c in range(N // CHUNK)]
-        wd_s = [keep.tile([P, CHUNK], U8, name="wd_s%d" % c, align_bytes=64) for c in range(N // CHUNK)]
+        tab_w = keep.tile([P, T], I32, name="tab_w", align_bytes=256)
+        tab_s = keep.tile([P, T], U8, name="tab_s", align_bytes=256)
+        wt4_w = keep.tile([P, 2 * N], U8, name="wt4_w", align_bytes=256)
+        wt4_s = keep.tile([P, N], U8, name="wt4_s", align_bytes=256)
+        wx_w = keep.tile([P, 2 * N], U8, name="wx_w", align_bytes=256)
+        wx_s = keep.tile([P, N], U8, name="wx_s", align_bytes=256)
+        x_raw = [keep.tile([P, PACK, CHUNK], F32, name="x_raw%d" % c, align_bytes=256) for c in range(J // CHUNK)]
+        d_raw = [keep.tile([P, PACK, CHUNK], F32, name="d_raw%d" % c, align_bytes=256) for c in range(N // CHUNK)]
+        d_bf = [keep.tile([P, CHUNK, PACK], BF16, name="d_bf%d" % c, align_bytes=256) for c in range(N // CHUNK)]
+        r_bf = [keep.tile([P, CHUNK, PACK], BF16, name="r_bf%d" % c, align_bytes=256) for c in (0, 2, 3)]
+        r_bf.insert(1, alias.tile([P, CHUNK, PACK], BF16, name="r_bf1", align_bytes=256, offset=0))
+        xq_w = [keep.tile([P, HALF], U32, name="xq_w%d" % h, align_bytes=256) for h in range(2)]
+        xq_s = [keep.tile([P, HALF], U8, name="xq_s%d" % h, align_bytes=256) for h in range(2)]
+        xr_w = [keep.tile([P, HALF], U32, name="xr_w%d" % h, align_bytes=256) for h in range(2)]
+        xr_s = [keep.tile([P, HALF], U8, name="xr_s%d" % h, align_bytes=256) for h in range(2)]
+        wd_w = [keep.tile([P, CHUNK], U32, name="wd_w%d" % c, align_bytes=256) for c in range(N // CHUNK)]
+        wd_s = [keep.tile([P, CHUNK], U8, name="wd_s%d" % c, align_bytes=256) for c in range(N // CHUNK)]
         got_w, got_s = [], []
         ident = keep.tile([P, P], F32, name="ident")
-        id_bf = keep.tile([P, PACK - 1, P * PACK], BF16, name="x_bf0", align_bytes=64)
-        diag = keep.tile([P, PACK * P + PACK], BF16, name="diag", align_bytes=64)
-        id_w = [keep.tile([P, P], U32, name="id_w%d" % t, align_bytes=64) for t in range(PACK)]
-        id_s = [keep.tile([P, P], U8, name="id_s%d" % t, align_bytes=64) for t in range(PACK)]
+        id_bf = keep.tile([P, PACK - 1, P * PACK], BF16, name="x_bf0", align_bytes=256)
+        diag = keep.tile([P, PACK * P + PACK], BF16, name="diag", align_bytes=256)
+        id_w = [keep.tile([P, P], U32, name="id_w%d" % t, align_bytes=256) for t in range(PACK)]
+        id_s = [keep.tile([P, P], U8, name="id_s%d" % t, align_bytes=256) for t in range(PACK)]
         b_rows = keep.tile([P, P], F32, name="b_rows")
         b_early = keep.tile([P, N // P], F32, name="b_early")
         warm = keep.tile([P, 8], F32, name="warm")
@@ -112,9 +112,9 @@ def tile_list_tiert_xdl_silu_kernel(
         def residual(src, jj):
             c, lo = jj // 2, (jj % 2) * P
             nc.vector.tensor_tensor(
-                out=by_runs_packed(r_bf[c][:, lo : lo + P, :]),
-                in0=by_runs_planes(x_raw[c][:, :, lo : lo + P]),
-                in1=src[:].rearrange("p (t c i) -> p c t i", t=PACK, i=RUN),
+                out=r_bf[c][:, lo : lo + P, :],
+                in0=x_raw[c][:, :, lo : lo + P].rearrange("p t j -> p j t"),
+                in1=src[:].rearrange("p (t j) -> p j t", t=PACK),
                 op=SUB,
             )
 
@@ -123,7 +123,7 @@ def tile_list_tiert_xdl_silu_kernel(
             nc.vector.tensor_copy(out=got_w[h][:], in_=tab_w[:].bitcast(U32).indirect(lst))
             nc.vector.tensor_copy(out=got_s[h][:], in_=tab_s[:].indirect(lst))
 
-        def mm(acc, kind, n, h, start, stop, lo=0, width=HALF):
+        def mm(acc, kind, n, h, start, stop):
             m = slice(n * P, (n + 1) * P)
             m2 = slice(2 * n * P, 2 * (n + 1) * P)
             md = slice((n % 2) * P, (n % 2 + 1) * P)
@@ -136,13 +136,12 @@ def tile_list_tiert_xdl_silu_kernel(
             else:
                 w, ws, a, s = wx_w[:, m2].bitcast(FP4X4), wx_s[:, m], xr_w[h], xr_s[h]
             nc.tensor.matmul_mx(
-                out=acc[:, 0:width], lhsT=w, lhsT_scale=ws,
-                rhs=a[:, lo : lo + width].bitcast(FP8X4), rhs_scale=s[:, lo : lo + width], start=start, stop=stop,
+                out=acc[:], lhsT=w, lhsT_scale=ws, rhs=a[:].bitcast(FP8X4), rhs_scale=s[:], start=start, stop=stop
             )
 
         def finish(acc, n, h, lo=0, width=HALF):
             res = res_pool.tile([P, width], F32, name="res")
-            nc.scalar.activation(out=res[:], in_=acc[:, 0:width], func=SILU, bias=b_cols[:, n : n + 1])
+            nc.scalar.activation(out=res[:], in_=acc[:, lo : lo + width], func=SILU, bias=b_cols[:, n : n + 1])
             j0 = h * HALF + lo
             nc.sync.dma_start(out=out[n * P : (n + 1) * P, j0 : j0 + width], in_=res[:])
 
@@ -171,8 +170,8 @@ def tile_list_tiert_xdl_silu_kernel(
         nc.sync.dma_start(offsets[:], offs)
         nc.sync.dma_start(out=wt4_w[:].bitcast(I32), in_=wt4_words[0].bitcast(I32))
         load_chunk(d_raw, d_v, 0)
-        load_chunk(d_raw, d_v, 1)
         load_scales(nc.sync, wt4_s, wt4_scales)
+        load_chunk(d_raw, d_v, 1)
         load_chunk(d_raw, d_v, 2)
         load_chunk(d_raw, d_v, 3)
         load_chunk(x_raw, x_v, 2)
@@ -193,10 +192,10 @@ def tile_list_tiert_xdl_silu_kernel(
         nc.tensor.transpose(b_t[:, 0:P], b_rows[:], ident[:])
         nc.scalar.copy(out=b_early[:], in_=b_t[:, 0 : N // P])
 
-        x_bf = [keep.tile([P, CHUNK, PACK], BF16, name="x_bf0", align_bytes=64)]
+        x_bf = [keep.tile([P, CHUNK, PACK], BF16, name="x_bf0", align_bytes=256)]
         pack(x_bf[0], x_raw[0], HEAD_SPLIT)
         quant(xq_w, xq_s, x_bf, 0)
-        x_bf.append(keep.tile([P, CHUNK, PACK], BF16, name="x_bf0", align_bytes=64))
+        x_bf.append(keep.tile([P, CHUNK, PACK], BF16, name="x_bf0", align_bytes=256))
         pack(x_bf[1], x_raw[1], HEAD_SPLIT)
         back = [bank(4 + jj) for jj in range(4)]
         dequant(back[0], 0)
@@ -218,30 +217,30 @@ def tile_list_tiert_xdl_silu_kernel(
             mm(acc[n], "xq", n, 0, True, False)
         for n in range(8):
             mm(acc[n], "xr", n, 0, False, False)
-        got_w.append(alias.tile([P, HALF], U32, name="got_w0", align_bytes=64, offset=1536))
-        got_s.append(alias.tile([P, HALF], U8, name="got_s0", align_bytes=64, offset=0))
+        got_w.append(alias.tile([P, HALF], U32, name="got_w0", align_bytes=256, offset=1536))
+        got_s.append(alias.tile([P, HALF], U8, name="got_s0", align_bytes=256, offset=0))
         gather(0)
         for n in range(8):
             mm(acc[n], "wt4", n, 0, False, False)
         for c in range(4):
             pack(d_bf[c], d_raw[c], 0)
             quant(wd_w, wd_s, d_bf, c)
-        got_w.append(keep.tile([P, HALF], U32, name="d_bf0", align_bytes=64))
-        got_s.append(keep.tile([P, HALF], U8, name="d_bf2", align_bytes=64))
+        got_w.append(keep.tile([P, HALF], U32, name="d_bf0", align_bytes=256))
+        got_s.append(keep.tile([P, HALF], U8, name="d_bf2", align_bytes=256))
         gather(1)
-        b_cols = keep.tile([P, N // P], F32, name="d_raw3", align_bytes=64)
+        b_cols = keep.tile([P, N // P], F32, name="d_raw3", align_bytes=256)
         nc.scalar.copy(out=b_cols[:], in_=b_early[:])
         for n in range(8):
             mm(acc[n], "wtd", n, 0, False, True)
             finish(acc[n], n, 0)
 
-        x_bf.append(keep.tile([P, CHUNK, PACK], BF16, name="d_bf3", align_bytes=64))
+        x_bf.append(keep.tile([P, CHUNK, PACK], BF16, name="d_bf3", align_bytes=256))
         pack(x_bf[2], x_raw[2], CHUNK)
         quant(xq_w, xq_s, x_bf, 2)
         back = [bank(0), bank(1)]
         dequant(back[0], 4)
         dequant(back[1], 5)
-        x_bf.append(keep.tile([P, CHUNK, PACK], BF16, name="d_bf3", align_bytes=64))
+        x_bf.append(keep.tile([P, CHUNK, PACK], BF16, name="d_bf3", align_bytes=256))
         pack(x_bf[3], x_raw[3], CHUNK)
         residual(back[0], 4)
         quant(xq_w, xq_s, x_bf, 3)
@@ -253,11 +252,14 @@ def tile_list_tiert_xdl_silu_kernel(
         residual(back[0], 6)
         residual(back[1], 7)
         quant(xr_w, xr_s, r_bf, 3)
-        pieces = [(n, (n + 2) % 8, 0, HALF) for n in range(7)] + [(7, 1 + i, i * P, P) for i in range(4)]
-        for n, i, lo, width in pieces:
-            last_acc = bank(i)
-            mm(last_acc, "wt4", n, 1, True, False, lo, width)
-            mm(last_acc, "wtd", n, 1, False, False, lo, width)
-            mm(last_acc, "xq", n, 1, False, False, lo, width)
-            mm(last_acc, "xr", n, 1, False, True, lo, width)
-            finish(last_acc, n, 1, lo, width)
+        for n in range(8):
+            acc = bank((n + 2) % 8)
+            mm(acc, "wt4", n, 1, True, False)
+            mm(acc, "wtd", n, 1, False, False)
+            mm(acc, "xq", n, 1, False, False)
+            mm(acc, "xr", n, 1, False, True)
+            if n < 7:
+                finish(acc, n, 1)
+            else:
+                finish(acc, n, 1, 0, CHUNK)
+                finish(acc, n, 1, CHUNK, CHUNK)

@@ -15,22 +15,27 @@ U8 = mybir.dt.uint8
 FP8X4 = mybir.dt.float8_e4m3fn_x4
 FP4X4 = mybir.dt.float4_e2m1fn_x4
 SILU = mybir.ActivationFunctionType.Silu
-SUB = mybir.AluOpType.subtract
 
 P = 128
 PACK = 4
 HALF = 512
 CHUNK = 256
+TILES = N // P
 RUN = 4
-HEAD_SPLIT = 160
+ALIGN = 64
+RESULT_BUFS = 6
 WARM_PASSES = 18
+X_ON_VECTOR = (160, 96, CHUNK, CHUNK)
+EARLY_TILES = 2
+BACK_BANKS = (1, 2)
+SECOND_BANKS = (0, 3, 4, 5, 6, 7, 1, 2)
 
 
-def by_runs_packed(ap):
+def packed_by_runs(ap):
     return ap.rearrange("p (c i) t -> p c t i", i=RUN)
 
 
-def by_runs_planes(ap):
+def planes_by_runs(ap):
     return ap.rearrange("p t (c i) -> p c t i", i=RUN)
 
 
@@ -40,226 +45,231 @@ def tile_list_tiert_xdl_silu_kernel(
     nc = tc.nc
     with ExitStack() as ctx:
         keep = ctx.enter_context(tc.tile_pool(name="keep", bufs=1))
-        alias = ctx.enter_context(tc.tile_pool(name="alias", bufs=1))
-        res_pool = ctx.enter_context(tc.tile_pool(name="res", bufs=6))
+        shared = ctx.enter_context(tc.tile_pool(name="shared", bufs=1))
+        results = ctx.enter_context(tc.tile_pool(name="results", bufs=RESULT_BUFS))
         psum = ctx.enter_context(tc.psum_pool(name="psum", bufs=1))
 
         def bank(i):
             return psum.tile([P, HALF], F32, name="bank%d" % i)
 
+        def tiles(name, count, shape, dtype):
+            return [keep.tile(shape, dtype, name="%s%d" % (name, i), align_bytes=ALIGN) for i in range(count)]
+
         offsets = keep.tile([P, J // 16], U16, name="offsets")
-        tab_w = keep.tile([P, T], I32, name="tab_w", align_bytes=256)
-        tab_s = keep.tile([P, T], U8, name="tab_s", align_bytes=256)
-        wt4_w = keep.tile([P, 2 * N], U8, name="wt4_w", align_bytes=256)
-        wt4_s = keep.tile([P, N], U8, name="wt4_s", align_bytes=256)
-        wx_w = keep.tile([P, 2 * N], U8, name="wx_w", align_bytes=256)
-        wx_s = keep.tile([P, N], U8, name="wx_s", align_bytes=256)
-        x_raw = [keep.tile([P, PACK, CHUNK], F32, name="x_raw%d" % c, align_bytes=256) for c in range(J // CHUNK)]
-        d_raw = [keep.tile([P, PACK, CHUNK], F32, name="d_raw%d" % c, align_bytes=256) for c in range(N // CHUNK)]
-        d_bf = [keep.tile([P, CHUNK, PACK], BF16, name="d_bf%d" % c, align_bytes=256) for c in range(N // CHUNK)]
-        r_bf = [keep.tile([P, CHUNK, PACK], BF16, name="r_bf%d" % c, align_bytes=256) for c in (0, 2, 3)]
-        r_bf.insert(1, alias.tile([P, CHUNK, PACK], BF16, name="r_bf1", align_bytes=256, offset=0))
-        xq_w = [keep.tile([P, HALF], U32, name="xq_w%d" % h, align_bytes=256) for h in range(2)]
-        xq_s = [keep.tile([P, HALF], U8, name="xq_s%d" % h, align_bytes=256) for h in range(2)]
-        xr_w = [keep.tile([P, HALF], U32, name="xr_w%d" % h, align_bytes=256) for h in range(2)]
-        xr_s = [keep.tile([P, HALF], U8, name="xr_s%d" % h, align_bytes=256) for h in range(2)]
-        wd_w = [keep.tile([P, CHUNK], U32, name="wd_w%d" % c, align_bytes=256) for c in range(N // CHUNK)]
-        wd_s = [keep.tile([P, CHUNK], U8, name="wd_s%d" % c, align_bytes=256) for c in range(N // CHUNK)]
-        got_w, got_s = [], []
-        ident = keep.tile([P, P], F32, name="ident")
-        id_bf = keep.tile([P, PACK - 1, P * PACK], BF16, name="x_bf0", align_bytes=256)
-        diag = keep.tile([P, PACK * P + PACK], BF16, name="diag", align_bytes=256)
-        id_w = [keep.tile([P, P], U32, name="id_w%d" % t, align_bytes=256) for t in range(PACK)]
-        id_s = [keep.tile([P, P], U8, name="id_s%d" % t, align_bytes=256) for t in range(PACK)]
+        tab_w = keep.tile([P, T], I32, name="tab_w", align_bytes=ALIGN)
+        tab_s = keep.tile([P, T], U8, name="tab_s", align_bytes=ALIGN)
+        wt4_w = keep.tile([P, 2 * N], U8, name="wt4_w", align_bytes=ALIGN)
+        wt4_s = keep.tile([P, N], U8, name="wt4_s", align_bytes=ALIGN)
+        wx_w = keep.tile([P, 2 * N], U8, name="wx_w", align_bytes=ALIGN)
+        wx_s = keep.tile([P, N], U8, name="wx_s", align_bytes=ALIGN)
+        x_raw = [keep.tile([P, PACK, CHUNK], F32, name="x_raw%d" % c, align_bytes=ALIGN) for c in (0, 2, 3)]
+        x_raw.insert(1, shared.tile([P, PACK, CHUNK], F32, name="x_raw1", align_bytes=ALIGN, offset=0))
+        wtd_raw = tiles("wtd_raw", N // CHUNK, [P, PACK, CHUNK], F32)
+        wtd_bf = tiles("wtd_bf", N // CHUNK, [P, CHUNK, PACK], BF16)
+        rest_bf = tiles("rest_bf", J // CHUNK, [P, CHUNK, PACK], BF16)
+        xq_w, xq_s = tiles("xq_w", 2, [P, HALF], U32), tiles("xq_s", 2, [P, HALF], U8)
+        xr_w, xr_s = tiles("xr_w", 2, [P, HALF], U32), tiles("xr_s", 2, [P, HALF], U8)
+        wtd_w, wtd_s = tiles("wtd_w", N // CHUNK, [P, CHUNK], U32), tiles("wtd_s", N // CHUNK, [P, CHUNK], U8)
+        eye_w, eye_s = tiles("eye_w", PACK, [P, P], U32), tiles("eye_s", PACK, [P, P], U8)
+        eye_f32 = keep.tile([P, P], F32, name="eye_f32")
+        eye_bf = keep.tile([P, PACK - 1, P * PACK], BF16, name="staging", align_bytes=ALIGN)
+        diagonal = keep.tile([P, P * PACK + PACK], BF16, name="diagonal", align_bytes=ALIGN)
         b_rows = keep.tile([P, P], F32, name="b_rows")
-        b_early = keep.tile([P, N // P], F32, name="b_early")
-        warm = keep.tile([P, 8], F32, name="warm")
+        b_cols = keep.tile([P, TILES], F32, name="b_cols")
+        table_warm = keep.tile([P, 8], F32, name="table_warm")
+        x_bf, got_w, got_s = [], [], []
 
-        x_v = x.rearrange("(p t) j -> p t j", t=PACK)
-        d_v = wtd.rearrange("(p t) n -> p t n", t=PACK)
+        x_planes = x.rearrange("(p t) j -> p t j", t=PACK)
+        wtd_planes = wtd.rearrange("(p t) n -> p t n", t=PACK)
 
-        def load_scales(queue, plane, rows):
+        def load_scales(plane, rows):
             for r in range(4):
-                queue.dma_start(out=plane[r:P:32, :].bitcast(I32), in_=rows[0, r:16:4, :].bitcast(I32))
+                nc.sync.dma_start(out=plane[r:P:32, :].bitcast(I32), in_=rows[0, r:16:4, :].bitcast(I32))
 
-        def load_chunk(dst, src, c):
-            nc.sync.dma_start(out=dst[c][:], in_=src[:, :, c * CHUNK : (c + 1) * CHUNK])
+        def load_chunk(raw, planes, c):
+            nc.sync.dma_start(out=raw[c][:], in_=planes[:, :, c * CHUNK : (c + 1) * CHUNK])
 
-        def pack(dst, src, split):
-            if split > 0:
-                nc.vector.tensor_copy(out=by_runs_packed(dst[:, 0:split, :]), in_=by_runs_planes(src[:, :, 0:split]))
-            if split < CHUNK:
-                nc.scalar.copy(out=by_runs_packed(dst[:, split:CHUNK, :]), in_=by_runs_planes(src[:, :, split:CHUNK]))
+        def round_chunk(dst, src, on_vector):
+            if on_vector > 0:
+                nc.vector.tensor_copy(out=packed_by_runs(dst[:, 0:on_vector, :]), in_=planes_by_runs(src[:, :, 0:on_vector]))
+            if on_vector < CHUNK:
+                nc.scalar.copy(out=packed_by_runs(dst[:, on_vector:CHUNK, :]), in_=planes_by_runs(src[:, :, on_vector:CHUNK]))
 
-        def quant(words, scales, src, c):
-            per_tile = words[0].shape[1] // CHUNK
-            i, lo = c // per_tile, (c % per_tile) * CHUNK
+        def quantise_chunk(words, scales, src, c):
+            i, lo = divmod(c * CHUNK, words[0].shape[1])
             nc.vector.quantize_mx(
                 out=words[i][:, lo : lo + CHUNK].bitcast(FP8X4),
                 scales=scales[i][:, lo : lo + CHUNK],
                 in_=src[c][:].rearrange("p c t -> p (c t)"),
             )
 
-        def dequant(dst, jj):
-            h, cols = jj // 4, slice((jj % 4) * P, (jj % 4 + 1) * P)
+        def round_x(c, buffer):
+            x_bf.append(keep.tile([P, CHUNK, PACK], BF16, name=buffer, align_bytes=ALIGN))
+            round_chunk(x_bf[c], x_raw[c], X_ON_VECTOR[c])
+
+        def dequantise(dst, piece):
+            h, lo = divmod(piece * P, HALF)
             for t in range(PACK):
-                m = slice(t * P, (t + 1) * P)
                 nc.tensor.matmul_mx(
-                    out=dst[:, m], lhsT=id_w[t][:].bitcast(FP8X4), lhsT_scale=id_s[t][:],
-                    rhs=xq_w[h][:, cols].bitcast(FP8X4), rhs_scale=xq_s[h][:, cols], start=True, stop=True,
+                    out=dst[:, t * P : (t + 1) * P],
+                    lhsT=eye_w[t][:].bitcast(FP8X4), lhsT_scale=eye_s[t][:],
+                    rhs=xq_w[h][:, lo : lo + P].bitcast(FP8X4), rhs_scale=xq_s[h][:, lo : lo + P],
+                    start=True, stop=True,
                 )
 
-        def residual(src, jj):
-            c, lo = jj // 2, (jj % 2) * P
+        def residual(back, piece):
+            c, lo = divmod(piece * P, CHUNK)
             nc.vector.tensor_tensor(
-                out=r_bf[c][:, lo : lo + P, :],
-                in0=x_raw[c][:, :, lo : lo + P].rearrange("p t j -> p j t"),
-                in1=src[:].rearrange("p (t j) -> p j t", t=PACK),
-                op=SUB,
+                out=packed_by_runs(rest_bf[c][:, lo : lo + P, :]),
+                in0=planes_by_runs(x_raw[c][:, :, lo : lo + P]),
+                in1=back[:].rearrange("p (t c i) -> p c t i", t=PACK, i=RUN),
+                op=mybir.AluOpType.subtract,
             )
 
         def gather(h):
-            lst = offsets[:, h * (HALF // 16) : (h + 1) * (HALF // 16)]
-            nc.vector.tensor_copy(out=got_w[h][:], in_=tab_w[:].bitcast(U32).indirect(lst))
-            nc.vector.tensor_copy(out=got_s[h][:], in_=tab_s[:].indirect(lst))
+            entries = offsets[:, h * (HALF // 16) : (h + 1) * (HALF // 16)]
+            nc.vector.tensor_copy(out=got_w[h][:], in_=tab_w[:].bitcast(U32).indirect(entries))
+            nc.vector.tensor_copy(out=got_s[h][:], in_=tab_s[:].indirect(entries))
 
-        def mm(acc, kind, n, h, start, stop):
-            m = slice(n * P, (n + 1) * P)
-            m2 = slice(2 * n * P, 2 * (n + 1) * P)
-            md = slice((n % 2) * P, (n % 2 + 1) * P)
-            if kind == "wt4":
-                w, ws, a, s = wt4_w[:, m2].bitcast(FP4X4), wt4_s[:, m], got_w[h], got_s[h]
-            elif kind == "wtd":
-                w, ws, a, s = wd_w[n // 2][:, md].bitcast(FP8X4), wd_s[n // 2][:, md], got_w[h], got_s[h]
-            elif kind == "xq":
-                w, ws, a, s = wx_w[:, m2].bitcast(FP4X4), wx_s[:, m], xq_w[h], xq_s[h]
+        def product(acc, term, n, h, start, stop):
+            rows = slice(n * P, (n + 1) * P)
+            fp4_bytes = slice(2 * n * P, 2 * (n + 1) * P)
+            c, lo = divmod(n * P, CHUNK)
+            if term == "wt4":
+                w, w_s, a, a_s = wt4_w[:, fp4_bytes].bitcast(FP4X4), wt4_s[:, rows], got_w[h], got_s[h]
+            elif term == "wtd":
+                w, w_s, a, a_s = wtd_w[c][:, lo : lo + P].bitcast(FP8X4), wtd_s[c][:, lo : lo + P], got_w[h], got_s[h]
+            elif term == "xq":
+                w, w_s, a, a_s = wx_w[:, fp4_bytes].bitcast(FP4X4), wx_s[:, rows], xq_w[h], xq_s[h]
             else:
-                w, ws, a, s = wx_w[:, m2].bitcast(FP4X4), wx_s[:, m], xr_w[h], xr_s[h]
+                w, w_s, a, a_s = wx_w[:, fp4_bytes].bitcast(FP4X4), wx_s[:, rows], xr_w[h], xr_s[h]
             nc.tensor.matmul_mx(
-                out=acc[:], lhsT=w, lhsT_scale=ws, rhs=a[:].bitcast(FP8X4), rhs_scale=s[:], start=start, stop=stop
+                out=acc[:], lhsT=w, lhsT_scale=w_s, rhs=a[:].bitcast(FP8X4), rhs_scale=a_s[:], start=start, stop=stop
             )
 
-        def finish(acc, n, h, lo=0, width=HALF):
-            res = res_pool.tile([P, width], F32, name="res")
+        def finish(acc, n, h, lo, width):
+            res = results.tile([P, width], F32, name="res")
             nc.scalar.activation(out=res[:], in_=acc[:, lo : lo + width], func=SILU, bias=b_cols[:, n : n + 1])
             j0 = h * HALF + lo
             nc.sync.dma_start(out=out[n * P : (n + 1) * P, j0 : j0 + width], in_=res[:])
 
-        nc.gpsimd.memset(diag[:].bitcast(I32), 0)
-        nc.gpsimd.affine_select(
-            out=diag[:], in_=diag[:], pattern=[[1, PACK * P + PACK]], compare_op=mybir.AluOpType.not_equal,
-            fill=1.0, base=-(PACK - 1), channel_multiplier=-PACK,
-        )
-        make_identity(nc, ident[:])
         last = PACK - 1
-        nc.vector.quantize_mx(out=id_w[last][:].bitcast(FP8X4), scales=id_s[last][:], in_=diag[:, 0 : P * PACK])
-        nc.vector.memset(warm[:], 0.0)
-        nc.scalar.activation(out=warm[:], in_=warm[:], func=SILU)
+        nc.gpsimd.memset(diagonal[:].bitcast(I32), 0)
+        nc.gpsimd.affine_select(
+            out=diagonal[:], in_=diagonal[:], pattern=[[1, P * PACK + PACK]], compare_op=mybir.AluOpType.not_equal,
+            fill=1.0, base=-last, channel_multiplier=-PACK,
+        )
+        make_identity(nc, eye_f32[:])
+        nc.vector.quantize_mx(out=eye_w[last][:].bitcast(FP8X4), scales=eye_s[last][:], in_=diagonal[:, 0 : P * PACK])
+
+        nc.vector.memset(table_warm[:], 0.0)
+        nc.scalar.activation(out=table_warm[:], in_=table_warm[:], func=SILU)
+
         nc.vector.memset(b_rows[:], 0.0)
         nc.vector.memset(wx_s[:].bitcast(I32), 0)
         nc.vector.memset(tab_s[:].bitcast(I32), 0)
         nc.vector.memset(wt4_s[:].bitcast(I32), 0)
 
-        load_chunk(x_raw, x_v, 0)
-        nc.sync.dma_start(out=b_rows[0 : N // P, :], in_=b.rearrange("(c p) -> c p", p=P))
-        load_chunk(x_raw, x_v, 1)
+        load_chunk(x_raw, x_planes, 0)
+        nc.sync.dma_start(out=b_rows[0:TILES, :], in_=b.rearrange("(c p) -> c p", p=P))
+        load_chunk(x_raw, x_planes, 1)
+        load_scales(wx_s, wx_scales)
         nc.sync.dma_start(out=wx_w[:].bitcast(I32), in_=wx_words[0].bitcast(I32))
-        load_scales(nc.sync, wx_s, wx_scales)
         nc.sync.dma_start(out=tab_w[:], in_=tab_words[0].rearrange("p n t -> p (n t)").bitcast(I32))
-        load_scales(nc.sync, tab_s, tab_scales)
+        load_scales(tab_s, tab_scales)
         nc.sync.dma_start(offsets[:], offs)
+        load_chunk(wtd_raw, wtd_planes, 0)
         nc.sync.dma_start(out=wt4_w[:].bitcast(I32), in_=wt4_words[0].bitcast(I32))
-        load_chunk(d_raw, d_v, 0)
-        load_scales(nc.sync, wt4_s, wt4_scales)
-        load_chunk(d_raw, d_v, 1)
-        load_chunk(d_raw, d_v, 2)
-        load_chunk(d_raw, d_v, 3)
-        load_chunk(x_raw, x_v, 2)
-        load_chunk(x_raw, x_v, 3)
+        load_chunk(wtd_raw, wtd_planes, 1)
+        load_scales(wt4_s, wt4_scales)
+        load_chunk(wtd_raw, wtd_planes, 2)
+        load_chunk(x_raw, x_planes, 2)
+        load_chunk(x_raw, x_planes, 3)
+        load_chunk(wtd_raw, wtd_planes, 3)
 
         for t in range(last):
-            nc.vector.tensor_copy(out=id_bf[:, t, :], in_=diag[:, last - t : last - t + P * PACK])
+            nc.vector.tensor_copy(out=eye_bf[:, t, :], in_=diagonal[:, last - t : last - t + P * PACK])
         for t in range(last):
-            nc.vector.quantize_mx(out=id_w[t][:].bitcast(FP8X4), scales=id_s[t][:], in_=id_bf[:, t, :])
+            nc.vector.quantize_mx(out=eye_w[t][:].bitcast(FP8X4), scales=eye_s[t][:], in_=eye_bf[:, t, :])
+
         idle = bank(3)
         for i in range(WARM_PASSES):
             nc.tensor.matmul_mx(
                 out=idle[:, (i % PACK) * P : (i % PACK + 1) * P],
-                lhsT=id_w[last][:].bitcast(FP8X4), lhsT_scale=id_s[last][:],
-                rhs=id_w[last][:].bitcast(FP8X4), rhs_scale=id_s[last][:], start=True, stop=True,
+                lhsT=eye_w[last][:].bitcast(FP8X4), lhsT_scale=eye_s[last][:],
+                rhs=eye_w[last][:].bitcast(FP8X4), rhs_scale=eye_s[last][:],
+                start=True, stop=True,
             )
-        b_t = bank(3)
-        nc.tensor.transpose(b_t[:, 0:P], b_rows[:], ident[:])
-        nc.scalar.copy(out=b_early[:], in_=b_t[:, 0 : N // P])
 
-        x_bf = [keep.tile([P, CHUNK, PACK], BF16, name="x_bf0", align_bytes=256)]
-        pack(x_bf[0], x_raw[0], HEAD_SPLIT)
-        quant(xq_w, xq_s, x_bf, 0)
-        x_bf.append(keep.tile([P, CHUNK, PACK], BF16, name="x_bf0", align_bytes=256))
-        pack(x_bf[1], x_raw[1], HEAD_SPLIT)
-        back = [bank(4 + jj) for jj in range(4)]
-        dequant(back[0], 0)
-        dequant(back[1], 1)
-        quant(xq_w, xq_s, x_bf, 1)
-        dequant(back[2], 2)
-        dequant(back[3], 3)
+        b_turned = bank(3)
+        nc.tensor.transpose(b_turned[:, 0:P], b_rows[:], eye_f32[:])
+        nc.scalar.copy(out=b_cols[:], in_=b_turned[:, 0:TILES])
+
+        round_x(0, "staging")
+        quantise_chunk(xq_w, xq_s, x_bf, 0)
+        round_x(1, "staging")
+        back = [bank(4 + piece) for piece in range(4)]
+        dequantise(back[0], 0)
+        dequantise(back[1], 1)
+        quantise_chunk(xq_w, xq_s, x_bf, 1)
+        dequantise(back[2], 2)
+        dequantise(back[3], 3)
         residual(back[0], 0)
         residual(back[1], 1)
-        acc = [bank(n) for n in range(4)]
+        sums = [bank(n) for n in range(4)]
         for n in range(4):
-            mm(acc[n], "xq", n, 0, True, False)
+            product(sums[n], "xq", n, 0, True, False)
         residual(back[2], 2)
-        quant(xr_w, xr_s, r_bf, 0)
         residual(back[3], 3)
-        quant(xr_w, xr_s, r_bf, 1)
-        acc += [bank(n) for n in range(4, 8)]
-        for n in range(4, 8):
-            mm(acc[n], "xq", n, 0, True, False)
-        for n in range(8):
-            mm(acc[n], "xr", n, 0, False, False)
-        got_w.append(alias.tile([P, HALF], U32, name="got_w0", align_bytes=256, offset=1536))
-        got_s.append(alias.tile([P, HALF], U8, name="got_s0", align_bytes=256, offset=0))
-        gather(0)
-        for n in range(8):
-            mm(acc[n], "wt4", n, 0, False, False)
-        for c in range(4):
-            pack(d_bf[c], d_raw[c], 0)
-            quant(wd_w, wd_s, d_bf, c)
-        got_w.append(keep.tile([P, HALF], U32, name="d_bf0", align_bytes=256))
-        got_s.append(keep.tile([P, HALF], U8, name="d_bf2", align_bytes=256))
-        gather(1)
-        b_cols = keep.tile([P, N // P], F32, name="d_raw3", align_bytes=256)
-        nc.scalar.copy(out=b_cols[:], in_=b_early[:])
-        for n in range(8):
-            mm(acc[n], "wtd", n, 0, False, True)
-            finish(acc[n], n, 0)
+        quantise_chunk(xr_w, xr_s, rest_bf, 0)
+        quantise_chunk(xr_w, xr_s, rest_bf, 1)
+        sums += [bank(n) for n in range(4, TILES)]
+        for n in range(4, TILES):
+            product(sums[n], "xq", n, 0, True, False)
+        for n in range(TILES):
+            product(sums[n], "xr", n, 0, False, False)
 
-        x_bf.append(keep.tile([P, CHUNK, PACK], BF16, name="d_bf3", align_bytes=256))
-        pack(x_bf[2], x_raw[2], CHUNK)
-        quant(xq_w, xq_s, x_bf, 2)
-        back = [bank(0), bank(1)]
-        dequant(back[0], 4)
-        dequant(back[1], 5)
-        x_bf.append(keep.tile([P, CHUNK, PACK], BF16, name="d_bf3", align_bytes=256))
-        pack(x_bf[3], x_raw[3], CHUNK)
+        got_w.append(shared.tile([P, HALF], U32, name="got_w0", align_bytes=ALIGN, offset=0))
+        got_s.append(shared.tile([P, HALF], U8, name="got_s0", align_bytes=ALIGN, offset=4 * HALF))
+        gather(0)
+        for c in range(N // CHUNK):
+            round_chunk(wtd_bf[c], wtd_raw[c], 0)
+            quantise_chunk(wtd_w, wtd_s, wtd_bf, c)
+        got_w.append(keep.tile([P, HALF], U32, name="wtd_raw0", align_bytes=ALIGN))
+        got_s.append(keep.tile([P, HALF], U8, name="wtd_raw1", align_bytes=ALIGN))
+        gather(1)
+        for n in range(EARLY_TILES):
+            product(sums[n], "wt4", n, 0, False, False)
+            product(sums[n], "wtd", n, 0, False, True)
+            finish(sums[n], n, 0, 0, HALF)
+        for n in range(EARLY_TILES, TILES):
+            product(sums[n], "wt4", n, 0, False, False)
+        for n in range(EARLY_TILES, TILES):
+            product(sums[n], "wtd", n, 0, False, True)
+            finish(sums[n], n, 0, 0, HALF)
+
+        round_x(2, "x_bf2")
+        quantise_chunk(xq_w, xq_s, x_bf, 2)
+        back = [bank(i) for i in BACK_BANKS]
+        dequantise(back[0], 4)
+        dequantise(back[1], 5)
+        round_x(3, "x_bf3")
         residual(back[0], 4)
-        quant(xq_w, xq_s, x_bf, 3)
+        quantise_chunk(xq_w, xq_s, x_bf, 3)
         residual(back[1], 5)
-        back = [bank(0), bank(1)]
-        dequant(back[0], 6)
-        dequant(back[1], 7)
-        quant(xr_w, xr_s, r_bf, 2)
+        back = [bank(i) for i in BACK_BANKS]
+        dequantise(back[0], 6)
+        dequantise(back[1], 7)
         residual(back[0], 6)
         residual(back[1], 7)
-        quant(xr_w, xr_s, r_bf, 3)
-        for n in range(8):
-            acc = bank((n + 2) % 8)
-            mm(acc, "wt4", n, 1, True, False)
-            mm(acc, "wtd", n, 1, False, False)
-            mm(acc, "xq", n, 1, False, False)
-            mm(acc, "xr", n, 1, False, True)
-            if n < 7:
-                finish(acc, n, 1)
-            else:
-                finish(acc, n, 1, 0, CHUNK)
-                finish(acc, n, 1, CHUNK, CHUNK)
+        quantise_chunk(xr_w, xr_s, rest_bf, 2)
+        quantise_chunk(xr_w, xr_s, rest_bf, 3)
+        for n in range(TILES):
+            acc = bank(SECOND_BANKS[n])
+            product(acc, "wt4", n, 1, True, False)
+            product(acc, "wtd", n, 1, False, False)
+            product(acc, "xq", n, 1, False, False)
+            product(acc, "xr", n, 1, False, True)
+            width = HALF if n < TILES - 1 else HALF // 2
+            for lo in range(0, HALF, width):
+                finish(acc, n, 1, lo, width)

@@ -21,11 +21,14 @@ PACK = 4
 HALF = 512
 CHUNK = 256
 TILES = N // P
-RUN = 4
+RUN = 2
 ALIGN = 64
 RESULT_BUFS = 6
-WARM_PASSES = 18
-X_ON_VECTOR = (160, 96, CHUNK, CHUNK)
+WARM_WIDTHS = (128, 128, 128, 128, 256, 256, 256, 256, 256)
+X_ON_VECTOR = (160, 96, 256, 256)
+WTD_ON_VECTOR = (0, 0, 0, 0)
+X_LOADS = (256, 256, 256, 256,)
+WTD_LOADS = (256, 256, 256, 256,)
 EARLY_TILES = 2
 BACK_BANKS = (1, 2)
 SECOND_BANKS = (0, 3, 4, 5, 6, 7, 1, 2)
@@ -62,22 +65,25 @@ def tile_list_tiert_xdl_silu_kernel(
         wt4_s = keep.tile([P, N], U8, name="wt4_s", align_bytes=ALIGN)
         wx_w = keep.tile([P, 2 * N], U8, name="wx_w", align_bytes=ALIGN)
         wx_s = keep.tile([P, N], U8, name="wx_s", align_bytes=ALIGN)
-        x_raw = [keep.tile([P, PACK, CHUNK], F32, name="x_raw%d" % c, align_bytes=ALIGN) for c in (0, 2, 3)]
-        x_raw.insert(1, shared.tile([P, PACK, CHUNK], F32, name="x_raw1", align_bytes=ALIGN, offset=0))
-        wtd_raw = tiles("wtd_raw", N // CHUNK, [P, PACK, CHUNK], F32)
-        wtd_bf = tiles("wtd_bf", N // CHUNK, [P, CHUNK, PACK], BF16)
-        rest_bf = tiles("rest_bf", J // CHUNK, [P, CHUNK, PACK], BF16)
+        x_loaded = [keep.tile([P, PACK, w], F32, name="x_raw%d" % i, align_bytes=ALIGN) for i, w in enumerate(X_LOADS) if i != 1]
+        x_loaded.insert(1, shared.tile([P, PACK, X_LOADS[1]], F32, name="x_raw1", align_bytes=ALIGN, offset=0))
+        wtd_loaded = [keep.tile([P, PACK, w], F32, name="wtd_raw%d" % i, align_bytes=ALIGN) for i, w in enumerate(WTD_LOADS)]
+        x_raw = [t[:, :, lo : lo + CHUNK] for t in x_loaded for lo in range(0, t.shape[2], CHUNK)]
+        wtd_raw = [t[:, :, lo : lo + CHUNK] for t in wtd_loaded for lo in range(0, t.shape[2], CHUNK)]
         xq_w, xq_s = tiles("xq_w", 2, [P, HALF], U32), tiles("xq_s", 2, [P, HALF], U8)
         xr_w, xr_s = tiles("xr_w", 2, [P, HALF], U32), tiles("xr_s", 2, [P, HALF], U8)
         wtd_w, wtd_s = tiles("wtd_w", N // CHUNK, [P, CHUNK], U32), tiles("wtd_s", N // CHUNK, [P, CHUNK], U8)
-        eye_w, eye_s = tiles("eye_w", PACK, [P, P], U32), tiles("eye_s", PACK, [P, P], U8)
+        eye_words = keep.tile([P, PACK * P], U32, name="eye_words", align_bytes=ALIGN)
+        eye_scales = keep.tile([P, PACK * P], U8, name="eye_scales", align_bytes=ALIGN)
+        eye_w = [eye_words[:, t * P : (t + 1) * P] for t in range(PACK)]
+        eye_s = [eye_scales[:, t * P : (t + 1) * P] for t in range(PACK)]
         eye_f32 = keep.tile([P, P], F32, name="eye_f32")
         eye_bf = keep.tile([P, PACK - 1, P * PACK], BF16, name="staging", align_bytes=ALIGN)
         diagonal = keep.tile([P, P * PACK + PACK], BF16, name="diagonal", align_bytes=ALIGN)
-        b_rows = keep.tile([P, P], F32, name="b_rows")
+        b_rows = keep.tile([P, P], F32, name="b_rows", align_bytes=ALIGN)
         b_cols = keep.tile([P, TILES], F32, name="b_cols")
         table_warm = keep.tile([P, 8], F32, name="table_warm")
-        x_bf, got_w, got_s = [], [], []
+        x_bf, wtd_bf, rest_bf, got_w, got_s, back, sums = {}, {}, {}, {}, {}, {}, {}
 
         x_planes = x.rearrange("(p t) j -> p t j", t=PACK)
         wtd_planes = wtd.rearrange("(p t) n -> p t n", t=PACK)
@@ -86,8 +92,9 @@ def tile_list_tiert_xdl_silu_kernel(
             for r in range(4):
                 nc.sync.dma_start(out=plane[r:P:32, :].bitcast(I32), in_=rows[0, r:16:4, :].bitcast(I32))
 
-        def load_chunk(raw, planes, c):
-            nc.sync.dma_start(out=raw[c][:], in_=planes[:, :, c * CHUNK : (c + 1) * CHUNK])
+        def load_columns(loaded, planes, widths, i):
+            lo = sum(widths[:i])
+            nc.sync.dma_start(out=loaded[i][:], in_=planes[:, :, lo : lo + widths[i]])
 
         def round_chunk(dst, src, on_vector):
             if on_vector > 0:
@@ -103,16 +110,12 @@ def tile_list_tiert_xdl_silu_kernel(
                 in_=src[c][:].rearrange("p c t -> p (c t)"),
             )
 
-        def round_x(c, buffer):
-            x_bf.append(keep.tile([P, CHUNK, PACK], BF16, name=buffer, align_bytes=ALIGN))
-            round_chunk(x_bf[c], x_raw[c], X_ON_VECTOR[c])
-
         def dequantise(dst, piece):
             h, lo = divmod(piece * P, HALF)
             for t in range(PACK):
                 nc.tensor.matmul_mx(
                     out=dst[:, t * P : (t + 1) * P],
-                    lhsT=eye_w[t][:].bitcast(FP8X4), lhsT_scale=eye_s[t][:],
+                    lhsT=eye_w[t].bitcast(FP8X4), lhsT_scale=eye_s[t],
                     rhs=xq_w[h][:, lo : lo + P].bitcast(FP8X4), rhs_scale=xq_s[h][:, lo : lo + P],
                     start=True, stop=True,
                 )
@@ -126,10 +129,8 @@ def tile_list_tiert_xdl_silu_kernel(
                 op=mybir.AluOpType.subtract,
             )
 
-        def gather(h):
-            entries = offsets[:, h * (HALF // 16) : (h + 1) * (HALF // 16)]
-            nc.vector.tensor_copy(out=got_w[h][:], in_=tab_w[:].bitcast(U32).indirect(entries))
-            nc.vector.tensor_copy(out=got_s[h][:], in_=tab_s[:].indirect(entries))
+        def entries(h):
+            return offsets[:, h * (HALF // 16) : (h + 1) * (HALF // 16)]
 
         def product(acc, term, n, h, start, stop):
             rows = slice(n * P, (n + 1) * P)
@@ -160,7 +161,7 @@ def tile_list_tiert_xdl_silu_kernel(
             fill=1.0, base=-last, channel_multiplier=-PACK,
         )
         make_identity(nc, eye_f32[:])
-        nc.vector.quantize_mx(out=eye_w[last][:].bitcast(FP8X4), scales=eye_s[last][:], in_=diagonal[:, 0 : P * PACK])
+        nc.vector.quantize_mx(out=eye_w[last].bitcast(FP8X4), scales=eye_s[last], in_=diagonal[:, 0 : P * PACK])
 
         nc.vector.memset(table_warm[:], 0.0)
         nc.scalar.activation(out=table_warm[:], in_=table_warm[:], func=SILU)
@@ -170,34 +171,34 @@ def tile_list_tiert_xdl_silu_kernel(
         nc.vector.memset(tab_s[:].bitcast(I32), 0)
         nc.vector.memset(wt4_s[:].bitcast(I32), 0)
 
-        load_chunk(x_raw, x_planes, 0)
+        load_columns(x_loaded, x_planes, X_LOADS, 0)
         nc.sync.dma_start(out=b_rows[0:TILES, :], in_=b.rearrange("(c p) -> c p", p=P))
-        load_chunk(x_raw, x_planes, 1)
+        load_columns(x_loaded, x_planes, X_LOADS, 1)
         load_scales(wx_s, wx_scales)
         nc.sync.dma_start(out=wx_w[:].bitcast(I32), in_=wx_words[0].bitcast(I32))
         nc.sync.dma_start(out=tab_w[:], in_=tab_words[0].rearrange("p n t -> p (n t)").bitcast(I32))
         load_scales(tab_s, tab_scales)
         nc.sync.dma_start(offsets[:], offs)
-        load_chunk(wtd_raw, wtd_planes, 0)
+        load_columns(wtd_loaded, wtd_planes, WTD_LOADS, 0)
         nc.sync.dma_start(out=wt4_w[:].bitcast(I32), in_=wt4_words[0].bitcast(I32))
-        load_chunk(wtd_raw, wtd_planes, 1)
+        load_columns(wtd_loaded, wtd_planes, WTD_LOADS, 1)
         load_scales(wt4_s, wt4_scales)
-        load_chunk(wtd_raw, wtd_planes, 2)
-        load_chunk(x_raw, x_planes, 2)
-        load_chunk(x_raw, x_planes, 3)
-        load_chunk(wtd_raw, wtd_planes, 3)
+        load_columns(wtd_loaded, wtd_planes, WTD_LOADS, 2)
+        load_columns(x_loaded, x_planes, X_LOADS, 2)
+        load_columns(x_loaded, x_planes, X_LOADS, 3)
+        load_columns(wtd_loaded, wtd_planes, WTD_LOADS, 3)
 
-        for t in range(last):
+        for t in reversed(range(last)):
             nc.vector.tensor_copy(out=eye_bf[:, t, :], in_=diagonal[:, last - t : last - t + P * PACK])
-        for t in range(last):
-            nc.vector.quantize_mx(out=eye_w[t][:].bitcast(FP8X4), scales=eye_s[t][:], in_=eye_bf[:, t, :])
+        for t in reversed(range(last)):
+            nc.vector.quantize_mx(out=eye_w[t].bitcast(FP8X4), scales=eye_s[t], in_=eye_bf[:, t, :])
 
         idle = bank(3)
-        for i in range(WARM_PASSES):
+        for width in WARM_WIDTHS:
             nc.tensor.matmul_mx(
-                out=idle[:, (i % PACK) * P : (i % PACK + 1) * P],
-                lhsT=eye_w[last][:].bitcast(FP8X4), lhsT_scale=eye_s[last][:],
-                rhs=eye_w[last][:].bitcast(FP8X4), rhs_scale=eye_s[last][:],
+                out=idle[:, 0:width],
+                lhsT=eye_w[last].bitcast(FP8X4), lhsT_scale=eye_s[last],
+                rhs=eye_words[:, PACK * P - width :].bitcast(FP8X4), rhs_scale=eye_scales[:, PACK * P - width :],
                 start=True, stop=True,
             )
 
@@ -205,71 +206,164 @@ def tile_list_tiert_xdl_silu_kernel(
         nc.tensor.transpose(b_turned[:, 0:P], b_rows[:], eye_f32[:])
         nc.scalar.copy(out=b_cols[:], in_=b_turned[:, 0:TILES])
 
-        round_x(0, "staging")
+        x_bf[0] = keep.tile([P, CHUNK, PACK], BF16, name="staging", align_bytes=ALIGN)
+        round_chunk(x_bf[0], x_raw[0], X_ON_VECTOR[0])
         quantise_chunk(xq_w, xq_s, x_bf, 0)
-        round_x(1, "staging")
-        back = [bank(4 + piece) for piece in range(4)]
+        x_bf[1] = keep.tile([P, CHUNK, PACK], BF16, name="staging", align_bytes=ALIGN)
+        round_chunk(x_bf[1], x_raw[1], X_ON_VECTOR[1])
+        back[0] = bank(4)
         dequantise(back[0], 0)
+        back[1] = bank(5)
         dequantise(back[1], 1)
         quantise_chunk(xq_w, xq_s, x_bf, 1)
+        back[2] = bank(6)
         dequantise(back[2], 2)
+        back[3] = bank(7)
         dequantise(back[3], 3)
+        rest_bf[0] = keep.tile([P, CHUNK, PACK], BF16, name="rest_bf0", align_bytes=ALIGN)
         residual(back[0], 0)
         residual(back[1], 1)
-        sums = [bank(n) for n in range(4)]
-        for n in range(4):
-            product(sums[n], "xq", n, 0, True, False)
+        sums[0, 0] = bank(0)
+        product(sums[0, 0], "xq", 0, 0, True, False)
+        sums[1, 0] = bank(1)
+        product(sums[1, 0], "xq", 1, 0, True, False)
+        sums[2, 0] = bank(2)
+        product(sums[2, 0], "xq", 2, 0, True, False)
+        sums[3, 0] = bank(3)
+        product(sums[3, 0], "xq", 3, 0, True, False)
+        rest_bf[1] = keep.tile([P, CHUNK, PACK], BF16, name="rest_bf1", align_bytes=ALIGN)
         residual(back[2], 2)
         residual(back[3], 3)
         quantise_chunk(xr_w, xr_s, rest_bf, 0)
         quantise_chunk(xr_w, xr_s, rest_bf, 1)
-        sums += [bank(n) for n in range(4, TILES)]
-        for n in range(4, TILES):
-            product(sums[n], "xq", n, 0, True, False)
-        for n in range(TILES):
-            product(sums[n], "xr", n, 0, False, False)
-
-        got_w.append(shared.tile([P, HALF], U32, name="got_w0", align_bytes=ALIGN, offset=0))
-        got_s.append(shared.tile([P, HALF], U8, name="got_s0", align_bytes=ALIGN, offset=4 * HALF))
-        gather(0)
-        for c in range(N // CHUNK):
-            round_chunk(wtd_bf[c], wtd_raw[c], 0)
-            quantise_chunk(wtd_w, wtd_s, wtd_bf, c)
-        got_w.append(keep.tile([P, HALF], U32, name="wtd_raw0", align_bytes=ALIGN))
-        got_s.append(keep.tile([P, HALF], U8, name="wtd_raw1", align_bytes=ALIGN))
-        gather(1)
-        for n in range(EARLY_TILES):
-            product(sums[n], "wt4", n, 0, False, False)
-            product(sums[n], "wtd", n, 0, False, True)
-            finish(sums[n], n, 0, 0, HALF)
-        for n in range(EARLY_TILES, TILES):
-            product(sums[n], "wt4", n, 0, False, False)
-        for n in range(EARLY_TILES, TILES):
-            product(sums[n], "wtd", n, 0, False, True)
-            finish(sums[n], n, 0, 0, HALF)
-
-        round_x(2, "x_bf2")
+        sums[4, 0] = bank(4)
+        product(sums[4, 0], "xq", 4, 0, True, False)
+        sums[5, 0] = bank(5)
+        product(sums[5, 0], "xq", 5, 0, True, False)
+        sums[6, 0] = bank(6)
+        product(sums[6, 0], "xq", 6, 0, True, False)
+        sums[7, 0] = bank(7)
+        product(sums[7, 0], "xq", 7, 0, True, False)
+        product(sums[0, 0], "xr", 0, 0, False, False)
+        product(sums[1, 0], "xr", 1, 0, False, False)
+        product(sums[2, 0], "xr", 2, 0, False, False)
+        product(sums[3, 0], "xr", 3, 0, False, False)
+        product(sums[4, 0], "xr", 4, 0, False, False)
+        product(sums[5, 0], "xr", 5, 0, False, False)
+        product(sums[6, 0], "xr", 6, 0, False, False)
+        product(sums[7, 0], "xr", 7, 0, False, False)
+        got_w[0] = shared.tile([P, HALF], U32, name="got_w0", align_bytes=ALIGN, offset=0)
+        nc.vector.tensor_copy(out=got_w[0][:], in_=tab_w[:].bitcast(U32).indirect(entries(0)))
+        got_s[0] = shared.tile([P, HALF], U8, name="got_s0", align_bytes=ALIGN, offset=4 * HALF)
+        nc.vector.tensor_copy(out=got_s[0][:], in_=tab_s[:].indirect(entries(0)))
+        wtd_bf[0] = keep.tile([P, CHUNK, PACK], BF16, name="wtd_bf0", align_bytes=ALIGN)
+        round_chunk(wtd_bf[0], wtd_raw[0], WTD_ON_VECTOR[0])
+        quantise_chunk(wtd_w, wtd_s, wtd_bf, 0)
+        wtd_bf[1] = keep.tile([P, CHUNK, PACK], BF16, name="wtd_bf1", align_bytes=ALIGN)
+        round_chunk(wtd_bf[1], wtd_raw[1], WTD_ON_VECTOR[1])
+        quantise_chunk(wtd_w, wtd_s, wtd_bf, 1)
+        wtd_bf[2] = keep.tile([P, CHUNK, PACK], BF16, name="wtd_bf2", align_bytes=ALIGN)
+        round_chunk(wtd_bf[2], wtd_raw[2], WTD_ON_VECTOR[2])
+        quantise_chunk(wtd_w, wtd_s, wtd_bf, 2)
+        wtd_bf[3] = keep.tile([P, CHUNK, PACK], BF16, name="wtd_bf3", align_bytes=ALIGN)
+        round_chunk(wtd_bf[3], wtd_raw[3], WTD_ON_VECTOR[3])
+        quantise_chunk(wtd_w, wtd_s, wtd_bf, 3)
+        got_w[1] = keep.tile([P, HALF], U32, name="wtd_raw0", align_bytes=ALIGN)
+        nc.vector.tensor_copy(out=got_w[1][:], in_=tab_w[:].bitcast(U32).indirect(entries(1)))
+        got_s[1] = keep.tile([P, HALF], U8, name="wtd_raw1", align_bytes=ALIGN)
+        nc.vector.tensor_copy(out=got_s[1][:], in_=tab_s[:].indirect(entries(1)))
+        product(sums[0, 0], "wt4", 0, 0, False, False)
+        product(sums[0, 0], "wtd", 0, 0, False, True)
+        finish(sums[0, 0], 0, 0, 0, HALF)
+        product(sums[1, 0], "wt4", 1, 0, False, False)
+        product(sums[1, 0], "wtd", 1, 0, False, True)
+        finish(sums[1, 0], 1, 0, 0, HALF)
+        product(sums[2, 0], "wt4", 2, 0, False, False)
+        product(sums[3, 0], "wt4", 3, 0, False, False)
+        product(sums[4, 0], "wt4", 4, 0, False, False)
+        product(sums[5, 0], "wt4", 5, 0, False, False)
+        product(sums[6, 0], "wt4", 6, 0, False, False)
+        product(sums[7, 0], "wt4", 7, 0, False, False)
+        product(sums[2, 0], "wtd", 2, 0, False, True)
+        finish(sums[2, 0], 2, 0, 0, HALF)
+        product(sums[3, 0], "wtd", 3, 0, False, True)
+        finish(sums[3, 0], 3, 0, 0, HALF)
+        product(sums[4, 0], "wtd", 4, 0, False, True)
+        finish(sums[4, 0], 4, 0, 0, HALF)
+        product(sums[5, 0], "wtd", 5, 0, False, True)
+        finish(sums[5, 0], 5, 0, 0, HALF)
+        product(sums[6, 0], "wtd", 6, 0, False, True)
+        finish(sums[6, 0], 6, 0, 0, HALF)
+        product(sums[7, 0], "wtd", 7, 0, False, True)
+        finish(sums[7, 0], 7, 0, 0, HALF)
+        x_bf[2] = keep.tile([P, CHUNK, PACK], BF16, name="x_bf2", align_bytes=ALIGN)
+        round_chunk(x_bf[2], x_raw[2], X_ON_VECTOR[2])
         quantise_chunk(xq_w, xq_s, x_bf, 2)
-        back = [bank(i) for i in BACK_BANKS]
-        dequantise(back[0], 4)
-        dequantise(back[1], 5)
-        round_x(3, "x_bf3")
-        residual(back[0], 4)
+        back[4] = bank(1)
+        dequantise(back[4], 4)
+        back[5] = bank(2)
+        dequantise(back[5], 5)
+        x_bf[3] = keep.tile([P, CHUNK, PACK], BF16, name="x_bf3", align_bytes=ALIGN)
+        round_chunk(x_bf[3], x_raw[3], X_ON_VECTOR[3])
+        rest_bf[2] = keep.tile([P, CHUNK, PACK], BF16, name="rest_bf2", align_bytes=ALIGN)
+        residual(back[4], 4)
         quantise_chunk(xq_w, xq_s, x_bf, 3)
-        residual(back[1], 5)
-        back = [bank(i) for i in BACK_BANKS]
-        dequantise(back[0], 6)
-        dequantise(back[1], 7)
-        residual(back[0], 6)
-        residual(back[1], 7)
+        residual(back[5], 5)
+        back[6] = bank(1)
+        dequantise(back[6], 6)
+        back[7] = bank(2)
+        dequantise(back[7], 7)
+        rest_bf[3] = keep.tile([P, CHUNK, PACK], BF16, name="rest_bf3", align_bytes=ALIGN)
+        residual(back[6], 6)
+        residual(back[7], 7)
         quantise_chunk(xr_w, xr_s, rest_bf, 2)
         quantise_chunk(xr_w, xr_s, rest_bf, 3)
-        for n in range(TILES):
-            acc = bank(SECOND_BANKS[n])
-            product(acc, "wt4", n, 1, True, False)
-            product(acc, "wtd", n, 1, False, False)
-            product(acc, "xq", n, 1, False, False)
-            product(acc, "xr", n, 1, False, True)
-            width = HALF if n < TILES - 1 else HALF // 2
-            for lo in range(0, HALF, width):
-                finish(acc, n, 1, lo, width)
+        sums[0, 1] = bank(0)
+        product(sums[0, 1], "wt4", 0, 1, True, False)
+        product(sums[0, 1], "wtd", 0, 1, False, False)
+        product(sums[0, 1], "xq", 0, 1, False, False)
+        product(sums[0, 1], "xr", 0, 1, False, True)
+        finish(sums[0, 1], 0, 1, 0, HALF)
+        sums[1, 1] = bank(3)
+        product(sums[1, 1], "wt4", 1, 1, True, False)
+        product(sums[1, 1], "wtd", 1, 1, False, False)
+        product(sums[1, 1], "xq", 1, 1, False, False)
+        product(sums[1, 1], "xr", 1, 1, False, True)
+        finish(sums[1, 1], 1, 1, 0, HALF)
+        sums[2, 1] = bank(4)
+        product(sums[2, 1], "wt4", 2, 1, True, False)
+        product(sums[2, 1], "wtd", 2, 1, False, False)
+        product(sums[2, 1], "xq", 2, 1, False, False)
+        product(sums[2, 1], "xr", 2, 1, False, True)
+        finish(sums[2, 1], 2, 1, 0, HALF)
+        sums[3, 1] = bank(5)
+        product(sums[3, 1], "wt4", 3, 1, True, False)
+        product(sums[3, 1], "wtd", 3, 1, False, False)
+        product(sums[3, 1], "xq", 3, 1, False, False)
+        product(sums[3, 1], "xr", 3, 1, False, True)
+        finish(sums[3, 1], 3, 1, 0, HALF)
+        sums[4, 1] = bank(6)
+        product(sums[4, 1], "wt4", 4, 1, True, False)
+        product(sums[4, 1], "wtd", 4, 1, False, False)
+        product(sums[4, 1], "xq", 4, 1, False, False)
+        product(sums[4, 1], "xr", 4, 1, False, True)
+        finish(sums[4, 1], 4, 1, 0, HALF)
+        sums[5, 1] = bank(7)
+        product(sums[5, 1], "wt4", 5, 1, True, False)
+        product(sums[5, 1], "wtd", 5, 1, False, False)
+        product(sums[5, 1], "xq", 5, 1, False, False)
+        product(sums[5, 1], "xr", 5, 1, False, True)
+        finish(sums[5, 1], 5, 1, 0, HALF)
+        sums[6, 1] = bank(1)
+        product(sums[6, 1], "wt4", 6, 1, True, False)
+        product(sums[6, 1], "wtd", 6, 1, False, False)
+        product(sums[6, 1], "xq", 6, 1, False, False)
+        product(sums[6, 1], "xr", 6, 1, False, True)
+        finish(sums[6, 1], 6, 1, 0, HALF)
+        sums[7, 1] = bank(2)
+        product(sums[7, 1], "wt4", 7, 1, True, False)
+        product(sums[7, 1], "wtd", 7, 1, False, False)
+        product(sums[7, 1], "xq", 7, 1, False, False)
+        product(sums[7, 1], "xr", 7, 1, False, True)
+        finish(sums[7, 1], 7, 1, 0, HALF // 2)
+        finish(sums[7, 1], 7, 1, HALF // 2, HALF // 2)

@@ -23,9 +23,9 @@ CHUNK = 256
 TILES = N // P
 RUN = 2
 ALIGN = 64
-RESULT_BUFS = 6
+RESULT_BUFS = 17
 WARM_WIDTHS = (128, 128, 128, 128, 256, 256, 256, 256, 256)
-X_ON_VECTOR = (160, 96, 256, 256)
+X_ON_VECTOR = (160, 160, 128, 256)
 WTD_ON_VECTOR = (0, 0, 0, 0)
 X_LOADS = (256, 256, 256, 256,)
 WTD_LOADS = (256, 256, 256, 256,)
@@ -177,11 +177,11 @@ def tile_list_tiert_xdl_silu_kernel(
         load_scales(wx_s, wx_scales)
         nc.sync.dma_start(out=wx_w[:].bitcast(I32), in_=wx_words[0].bitcast(I32))
         nc.sync.dma_start(out=tab_w[:], in_=tab_words[0].rearrange("p n t -> p (n t)").bitcast(I32))
-        load_scales(tab_s, tab_scales)
         nc.sync.dma_start(offsets[:], offs)
         load_columns(wtd_loaded, wtd_planes, WTD_LOADS, 0)
-        nc.sync.dma_start(out=wt4_w[:].bitcast(I32), in_=wt4_words[0].bitcast(I32))
+        load_scales(tab_s, tab_scales)
         load_columns(wtd_loaded, wtd_planes, WTD_LOADS, 1)
+        nc.sync.dma_start(out=wt4_w[:].bitcast(I32), in_=wt4_words[0].bitcast(I32))
         load_scales(wt4_s, wt4_scales)
         load_columns(wtd_loaded, wtd_planes, WTD_LOADS, 2)
         load_columns(x_loaded, x_planes, X_LOADS, 2)
@@ -209,7 +209,7 @@ def tile_list_tiert_xdl_silu_kernel(
         x_bf[0] = keep.tile([P, CHUNK, PACK], BF16, name="staging", align_bytes=ALIGN)
         round_chunk(x_bf[0], x_raw[0], X_ON_VECTOR[0])
         quantise_chunk(xq_w, xq_s, x_bf, 0)
-        x_bf[1] = keep.tile([P, CHUNK, PACK], BF16, name="staging", align_bytes=ALIGN)
+        x_bf[1] = keep.tile([P, CHUNK, PACK], BF16, name="b_rows", align_bytes=ALIGN)
         round_chunk(x_bf[1], x_raw[1], X_ON_VECTOR[1])
         back[0] = bank(4)
         dequantise(back[0], 0)
@@ -256,111 +256,111 @@ def tile_list_tiert_xdl_silu_kernel(
         nc.vector.tensor_copy(out=got_w[0][:], in_=tab_w[:].bitcast(U32).indirect(entries(0)))
         got_s[0] = shared.tile([P, HALF], U8, name="got_s0", align_bytes=ALIGN, offset=4 * HALF)
         nc.vector.tensor_copy(out=got_s[0][:], in_=tab_s[:].indirect(entries(0)))
-        wtd_bf[0] = keep.tile([P, CHUNK, PACK], BF16, name="wtd_bf0", align_bytes=ALIGN)
+        wtd_bf[0] = keep.tile([P, CHUNK, PACK], BF16, name="rest_bf0", align_bytes=ALIGN)
         round_chunk(wtd_bf[0], wtd_raw[0], WTD_ON_VECTOR[0])
         quantise_chunk(wtd_w, wtd_s, wtd_bf, 0)
         wtd_bf[1] = keep.tile([P, CHUNK, PACK], BF16, name="wtd_bf1", align_bytes=ALIGN)
         round_chunk(wtd_bf[1], wtd_raw[1], WTD_ON_VECTOR[1])
         quantise_chunk(wtd_w, wtd_s, wtd_bf, 1)
+        got_w[1] = keep.tile([P, HALF], U32, name="wtd_raw1", align_bytes=ALIGN)
+        nc.vector.tensor_copy(out=got_w[1][:], in_=tab_w[:].bitcast(U32).indirect(entries(1)))
+        got_s[1] = keep.tile([P, HALF], U8, name="wtd_bf1", align_bytes=ALIGN)
+        nc.vector.tensor_copy(out=got_s[1][:], in_=tab_s[:].indirect(entries(1)))
         wtd_bf[2] = keep.tile([P, CHUNK, PACK], BF16, name="wtd_bf2", align_bytes=ALIGN)
         round_chunk(wtd_bf[2], wtd_raw[2], WTD_ON_VECTOR[2])
         quantise_chunk(wtd_w, wtd_s, wtd_bf, 2)
-        wtd_bf[3] = keep.tile([P, CHUNK, PACK], BF16, name="wtd_bf3", align_bytes=ALIGN)
-        round_chunk(wtd_bf[3], wtd_raw[3], WTD_ON_VECTOR[3])
-        quantise_chunk(wtd_w, wtd_s, wtd_bf, 3)
-        got_w[1] = keep.tile([P, HALF], U32, name="wtd_raw0", align_bytes=ALIGN)
-        nc.vector.tensor_copy(out=got_w[1][:], in_=tab_w[:].bitcast(U32).indirect(entries(1)))
-        got_s[1] = keep.tile([P, HALF], U8, name="wtd_raw1", align_bytes=ALIGN)
-        nc.vector.tensor_copy(out=got_s[1][:], in_=tab_s[:].indirect(entries(1)))
         product(sums[0, 0], "wt4", 0, 0, False, False)
-        product(sums[0, 0], "wtd", 0, 0, False, True)
-        finish(sums[0, 0], 0, 0, 0, HALF)
         product(sums[1, 0], "wt4", 1, 0, False, False)
-        product(sums[1, 0], "wtd", 1, 0, False, True)
-        finish(sums[1, 0], 1, 0, 0, HALF)
         product(sums[2, 0], "wt4", 2, 0, False, False)
+        product(sums[0, 0], "wtd", 0, 0, False, True)
+        product(sums[1, 0], "wtd", 1, 0, False, True)
         product(sums[3, 0], "wt4", 3, 0, False, False)
+        product(sums[2, 0], "wtd", 2, 0, False, True)
+        product(sums[3, 0], "wtd", 3, 0, False, True)
         product(sums[4, 0], "wt4", 4, 0, False, False)
         product(sums[5, 0], "wt4", 5, 0, False, False)
         product(sums[6, 0], "wt4", 6, 0, False, False)
         product(sums[7, 0], "wt4", 7, 0, False, False)
-        product(sums[2, 0], "wtd", 2, 0, False, True)
-        finish(sums[2, 0], 2, 0, 0, HALF)
-        product(sums[3, 0], "wtd", 3, 0, False, True)
-        finish(sums[3, 0], 3, 0, 0, HALF)
-        product(sums[4, 0], "wtd", 4, 0, False, True)
-        finish(sums[4, 0], 4, 0, 0, HALF)
-        product(sums[5, 0], "wtd", 5, 0, False, True)
-        finish(sums[5, 0], 5, 0, 0, HALF)
-        product(sums[6, 0], "wtd", 6, 0, False, True)
-        finish(sums[6, 0], 6, 0, 0, HALF)
-        product(sums[7, 0], "wtd", 7, 0, False, True)
-        finish(sums[7, 0], 7, 0, 0, HALF)
+        finish(sums[0, 0], 0, 0, 0, HALF)
+        finish(sums[1, 0], 1, 0, 0, HALF)
         x_bf[2] = keep.tile([P, CHUNK, PACK], BF16, name="x_bf2", align_bytes=ALIGN)
         round_chunk(x_bf[2], x_raw[2], X_ON_VECTOR[2])
-        quantise_chunk(xq_w, xq_s, x_bf, 2)
-        back[4] = bank(1)
-        dequantise(back[4], 4)
-        back[5] = bank(2)
-        dequantise(back[5], 5)
-        x_bf[3] = keep.tile([P, CHUNK, PACK], BF16, name="x_bf3", align_bytes=ALIGN)
-        round_chunk(x_bf[3], x_raw[3], X_ON_VECTOR[3])
-        rest_bf[2] = keep.tile([P, CHUNK, PACK], BF16, name="rest_bf2", align_bytes=ALIGN)
-        residual(back[4], 4)
-        quantise_chunk(xq_w, xq_s, x_bf, 3)
-        residual(back[5], 5)
-        back[6] = bank(1)
-        dequantise(back[6], 6)
-        back[7] = bank(2)
-        dequantise(back[7], 7)
-        rest_bf[3] = keep.tile([P, CHUNK, PACK], BF16, name="rest_bf3", align_bytes=ALIGN)
-        residual(back[6], 6)
-        residual(back[7], 7)
-        quantise_chunk(xr_w, xr_s, rest_bf, 2)
-        quantise_chunk(xr_w, xr_s, rest_bf, 3)
+        finish(sums[2, 0], 2, 0, 0, HALF)
+        finish(sums[3, 0], 3, 0, 0, HALF)
         sums[0, 1] = bank(0)
         product(sums[0, 1], "wt4", 0, 1, True, False)
         product(sums[0, 1], "wtd", 0, 1, False, False)
-        product(sums[0, 1], "xq", 0, 1, False, False)
-        product(sums[0, 1], "xr", 0, 1, False, True)
-        finish(sums[0, 1], 0, 1, 0, HALF)
-        sums[1, 1] = bank(3)
+        sums[1, 1] = bank(1)
         product(sums[1, 1], "wt4", 1, 1, True, False)
         product(sums[1, 1], "wtd", 1, 1, False, False)
-        product(sums[1, 1], "xq", 1, 1, False, False)
-        product(sums[1, 1], "xr", 1, 1, False, True)
-        finish(sums[1, 1], 1, 1, 0, HALF)
+        product(sums[4, 0], "wtd", 4, 0, False, True)
+        product(sums[5, 0], "wtd", 5, 0, False, True)
+        finish(sums[4, 0], 4, 0, 0, HALF)
+        finish(sums[5, 0], 5, 0, 0, HALF)
+        wtd_bf[3] = keep.tile([P, CHUNK, PACK], BF16, name="wtd_bf3", align_bytes=ALIGN)
+        round_chunk(wtd_bf[3], wtd_raw[3], WTD_ON_VECTOR[3])
+        quantise_chunk(xq_w, xq_s, x_bf, 2)
+        back[4] = bank(2)
+        dequantise(back[4], 4)
+        back[5] = bank(3)
+        dequantise(back[5], 5)
+        x_bf[3] = keep.tile([P, CHUNK, PACK], BF16, name="x_bf3", align_bytes=ALIGN)
+        round_chunk(x_bf[3], x_raw[3], X_ON_VECTOR[3])
+        quantise_chunk(xq_w, xq_s, x_bf, 3)
+        rest_bf[2] = keep.tile([P, CHUNK, PACK], BF16, name="rest_bf2", align_bytes=ALIGN)
+        residual(back[4], 4)
+        residual(back[5], 5)
         sums[2, 1] = bank(4)
         product(sums[2, 1], "wt4", 2, 1, True, False)
         product(sums[2, 1], "wtd", 2, 1, False, False)
+        back[6] = bank(5)
+        dequantise(back[6], 6)
+        product(sums[0, 1], "xq", 0, 1, False, False)
+        product(sums[1, 1], "xq", 1, 1, False, False)
         product(sums[2, 1], "xq", 2, 1, False, False)
-        product(sums[2, 1], "xr", 2, 1, False, True)
-        finish(sums[2, 1], 2, 1, 0, HALF)
-        sums[3, 1] = bank(5)
+        back[7] = bank(2)
+        dequantise(back[7], 7)
+        quantise_chunk(wtd_w, wtd_s, wtd_bf, 3)
+        rest_bf[3] = keep.tile([P, CHUNK, PACK], BF16, name="rest_bf3", align_bytes=ALIGN)
+        residual(back[6], 6)
+        quantise_chunk(xr_w, xr_s, rest_bf, 2)
+        residual(back[7], 7)
+        quantise_chunk(xr_w, xr_s, rest_bf, 3)
+        sums[3, 1] = bank(3)
         product(sums[3, 1], "wt4", 3, 1, True, False)
         product(sums[3, 1], "wtd", 3, 1, False, False)
         product(sums[3, 1], "xq", 3, 1, False, False)
+        product(sums[6, 0], "wtd", 6, 0, False, True)
+        product(sums[7, 0], "wtd", 7, 0, False, True)
+        finish(sums[6, 0], 6, 0, 0, HALF)
+        finish(sums[7, 0], 7, 0, 0, HALF)
+        product(sums[0, 1], "xr", 0, 1, False, True)
+        finish(sums[0, 1], 0, 1, 0, HALF)
+        product(sums[1, 1], "xr", 1, 1, False, True)
+        finish(sums[1, 1], 1, 1, 0, HALF)
+        product(sums[2, 1], "xr", 2, 1, False, True)
+        finish(sums[2, 1], 2, 1, 0, HALF)
         product(sums[3, 1], "xr", 3, 1, False, True)
         finish(sums[3, 1], 3, 1, 0, HALF)
-        sums[4, 1] = bank(6)
+        sums[4, 1] = bank(5)
         product(sums[4, 1], "wt4", 4, 1, True, False)
         product(sums[4, 1], "wtd", 4, 1, False, False)
         product(sums[4, 1], "xq", 4, 1, False, False)
         product(sums[4, 1], "xr", 4, 1, False, True)
         finish(sums[4, 1], 4, 1, 0, HALF)
-        sums[5, 1] = bank(7)
+        sums[5, 1] = bank(2)
         product(sums[5, 1], "wt4", 5, 1, True, False)
         product(sums[5, 1], "wtd", 5, 1, False, False)
         product(sums[5, 1], "xq", 5, 1, False, False)
         product(sums[5, 1], "xr", 5, 1, False, True)
         finish(sums[5, 1], 5, 1, 0, HALF)
-        sums[6, 1] = bank(1)
+        sums[6, 1] = bank(6)
         product(sums[6, 1], "wt4", 6, 1, True, False)
         product(sums[6, 1], "wtd", 6, 1, False, False)
         product(sums[6, 1], "xq", 6, 1, False, False)
         product(sums[6, 1], "xr", 6, 1, False, True)
         finish(sums[6, 1], 6, 1, 0, HALF)
-        sums[7, 1] = bank(2)
+        sums[7, 1] = bank(7)
         product(sums[7, 1], "wt4", 7, 1, True, False)
         product(sums[7, 1], "wtd", 7, 1, False, False)
         product(sums[7, 1], "xq", 7, 1, False, False)

@@ -21,17 +21,14 @@ PACK = 4
 HALF = 512
 CHUNK = 256
 TILES = N // P
+PIECES = HALF // P
 RUN = 2
 ALIGN = 64
-RESULT_BUFS = 17
-WARM_WIDTHS = (128, 128, 128, 128, 256, 256, 256, 256, 256)
-X_ON_VECTOR = (160, 160, 128, 256)
-WTD_ON_VECTOR = (0, 0, 0, 0)
-X_LOADS = (256, 256, 256, 256,)
-WTD_LOADS = (256, 256, 256, 256,)
-EARLY_TILES = 2
-BACK_BANKS = (1, 2)
-SECOND_BANKS = (0, 3, 4, 5, 6, 7, 1, 2)
+RESULT_BUFS = 2 * TILES + 1
+VECTOR_SHARE = 160
+LEAD = 3
+WARM_NARROW, WARM_WIDE = 4, 5
+WARM_BANK = PIECES - 1
 
 
 def packed_by_runs(ap):
@@ -55,35 +52,31 @@ def tile_list_tiert_xdl_silu_kernel(
         def bank(i):
             return psum.tile([P, HALF], F32, name="bank%d" % i)
 
+        def tile(name, shape, dtype):
+            return keep.tile(shape, dtype, name=name, align_bytes=ALIGN)
+
         def tiles(name, count, shape, dtype):
-            return [keep.tile(shape, dtype, name="%s%d" % (name, i), align_bytes=ALIGN) for i in range(count)]
+            return [tile("%s%d" % (name, i), shape, dtype) for i in range(count)]
 
         offsets = keep.tile([P, J // 16], U16, name="offsets")
-        tab_w = keep.tile([P, T], I32, name="tab_w", align_bytes=ALIGN)
-        tab_s = keep.tile([P, T], U8, name="tab_s", align_bytes=ALIGN)
-        wt4_w = keep.tile([P, 2 * N], U8, name="wt4_w", align_bytes=ALIGN)
-        wt4_s = keep.tile([P, N], U8, name="wt4_s", align_bytes=ALIGN)
-        wx_w = keep.tile([P, 2 * N], U8, name="wx_w", align_bytes=ALIGN)
-        wx_s = keep.tile([P, N], U8, name="wx_s", align_bytes=ALIGN)
-        x_loaded = [keep.tile([P, PACK, w], F32, name="x_raw%d" % i, align_bytes=ALIGN) for i, w in enumerate(X_LOADS) if i != 1]
-        x_loaded.insert(1, shared.tile([P, PACK, X_LOADS[1]], F32, name="x_raw1", align_bytes=ALIGN, offset=0))
-        wtd_loaded = [keep.tile([P, PACK, w], F32, name="wtd_raw%d" % i, align_bytes=ALIGN) for i, w in enumerate(WTD_LOADS)]
-        x_raw = [t[:, :, lo : lo + CHUNK] for t in x_loaded for lo in range(0, t.shape[2], CHUNK)]
-        wtd_raw = [t[:, :, lo : lo + CHUNK] for t in wtd_loaded for lo in range(0, t.shape[2], CHUNK)]
+        tab_w, tab_s = tile("tab_w", [P, T], I32), tile("tab_s", [P, T], U8)
+        wt4_w, wt4_s = tile("wt4_w", [P, 2 * N], U8), tile("wt4_s", [P, N], U8)
+        wx_w, wx_s = tile("wx_w", [P, 2 * N], U8), tile("wx_s", [P, N], U8)
+        x_raw = [tile("x_raw%d" % c, [P, PACK, CHUNK], F32) for c in (0, 2, 3)]
+        x_raw.insert(1, shared.tile([P, PACK, CHUNK], F32, name="x_raw1", align_bytes=ALIGN, offset=0))
+        wtd_raw = tiles("wtd_raw", N // CHUNK, [P, PACK, CHUNK], F32)
         xq_w, xq_s = tiles("xq_w", 2, [P, HALF], U32), tiles("xq_s", 2, [P, HALF], U8)
         xr_w, xr_s = tiles("xr_w", 2, [P, HALF], U32), tiles("xr_s", 2, [P, HALF], U8)
         wtd_w, wtd_s = tiles("wtd_w", N // CHUNK, [P, CHUNK], U32), tiles("wtd_s", N // CHUNK, [P, CHUNK], U8)
-        eye_words = keep.tile([P, PACK * P], U32, name="eye_words", align_bytes=ALIGN)
-        eye_scales = keep.tile([P, PACK * P], U8, name="eye_scales", align_bytes=ALIGN)
-        eye_w = [eye_words[:, t * P : (t + 1) * P] for t in range(PACK)]
-        eye_s = [eye_scales[:, t * P : (t + 1) * P] for t in range(PACK)]
+        eye_w, eye_s = tile("eye_w", [P, PACK * P], U32), tile("eye_s", [P, PACK * P], U8)
         eye_f32 = keep.tile([P, P], F32, name="eye_f32")
-        eye_bf = keep.tile([P, PACK - 1, P * PACK], BF16, name="staging", align_bytes=ALIGN)
-        diagonal = keep.tile([P, P * PACK + PACK], BF16, name="diagonal", align_bytes=ALIGN)
-        b_rows = keep.tile([P, P], F32, name="b_rows", align_bytes=ALIGN)
+        eye_bf = tile("eye_bf", [P, PACK - 1, P * PACK], BF16)
+        diagonal = tile("diagonal", [P, P * PACK + PACK], BF16)
+        b_rows = tile("b_rows", [P, P], F32)
         b_cols = keep.tile([P, TILES], F32, name="b_cols")
         table_warm = keep.tile([P, 8], F32, name="table_warm")
         x_bf, wtd_bf, rest_bf, got_w, got_s, back, sums = {}, {}, {}, {}, {}, {}, {}
+        free_banks = []
 
         x_planes = x.rearrange("(p t) j -> p t j", t=PACK)
         wtd_planes = wtd.rearrange("(p t) n -> p t n", t=PACK)
@@ -92,15 +85,21 @@ def tile_list_tiert_xdl_silu_kernel(
             for r in range(4):
                 nc.sync.dma_start(out=plane[r:P:32, :].bitcast(I32), in_=rows[0, r:16:4, :].bitcast(I32))
 
-        def load_columns(loaded, planes, widths, i):
-            lo = sum(widths[:i])
-            nc.sync.dma_start(out=loaded[i][:], in_=planes[:, :, lo : lo + widths[i]])
+        def load_chunk(raw, planes, c):
+            nc.sync.dma_start(out=raw[c][:], in_=planes[:, :, c * CHUNK : (c + 1) * CHUNK])
 
-        def round_chunk(dst, src, on_vector):
-            if on_vector > 0:
-                nc.vector.tensor_copy(out=packed_by_runs(dst[:, 0:on_vector, :]), in_=planes_by_runs(src[:, :, 0:on_vector]))
+        def round_columns(copy, dst, src, lo, hi):
+            copy(out=packed_by_runs(dst[:, lo:hi, :]), in_=planes_by_runs(src[:, :, lo:hi]))
+
+        def round_x(c, buffer, on_vector):
+            x_bf[c] = tile(buffer, [P, CHUNK, PACK], BF16)
+            round_columns(nc.vector.tensor_copy, x_bf[c], x_raw[c], 0, on_vector)
             if on_vector < CHUNK:
-                nc.scalar.copy(out=packed_by_runs(dst[:, on_vector:CHUNK, :]), in_=planes_by_runs(src[:, :, on_vector:CHUNK]))
+                round_columns(nc.scalar.copy, x_bf[c], x_raw[c], on_vector, CHUNK)
+
+        def round_wtd(c, buffer):
+            wtd_bf[c] = tile(buffer, [P, CHUNK, PACK], BF16)
+            round_columns(nc.scalar.copy, wtd_bf[c], wtd_raw[c], 0, CHUNK)
 
         def quantise_chunk(words, scales, src, c):
             i, lo = divmod(c * CHUNK, words[0].shape[1])
@@ -110,29 +109,38 @@ def tile_list_tiert_xdl_silu_kernel(
                 in_=src[c][:].rearrange("p c t -> p (c t)"),
             )
 
-        def dequantise(dst, piece):
+        def dequantise(piece, bank_index):
             h, lo = divmod(piece * P, HALF)
+            back[piece] = (bank(bank_index), bank_index)
             for t in range(PACK):
+                columns = slice(t * P, (t + 1) * P)
                 nc.tensor.matmul_mx(
-                    out=dst[:, t * P : (t + 1) * P],
-                    lhsT=eye_w[t].bitcast(FP8X4), lhsT_scale=eye_s[t],
+                    out=back[piece][0][:, columns],
+                    lhsT=eye_w[:, columns].bitcast(FP8X4), lhsT_scale=eye_s[:, columns],
                     rhs=xq_w[h][:, lo : lo + P].bitcast(FP8X4), rhs_scale=xq_s[h][:, lo : lo + P],
                     start=True, stop=True,
                 )
 
-        def residual(back, piece):
+        def residual(piece):
             c, lo = divmod(piece * P, CHUNK)
+            if lo == 0:
+                rest_bf[c] = tile("rest_bf%d" % c, [P, CHUNK, PACK], BF16)
+            values, bank_index = back[piece]
             nc.vector.tensor_tensor(
                 out=packed_by_runs(rest_bf[c][:, lo : lo + P, :]),
                 in0=planes_by_runs(x_raw[c][:, :, lo : lo + P]),
-                in1=back[:].rearrange("p (t c i) -> p c t i", t=PACK, i=RUN),
+                in1=values[:].rearrange("p (t c i) -> p c t i", t=PACK, i=RUN),
                 op=mybir.AluOpType.subtract,
             )
+            free_banks.append(bank_index)
 
-        def entries(h):
-            return offsets[:, h * (HALF // 16) : (h + 1) * (HALF // 16)]
+        def gather(dst, table, h):
+            entries = offsets[:, h * (HALF // 16) : (h + 1) * (HALF // 16)]
+            nc.vector.tensor_copy(out=dst[:], in_=table.indirect(entries))
 
-        def product(acc, term, n, h, start, stop):
+        def product(term, n, h, opens_bank=None, closes=False):
+            if opens_bank is not None:
+                sums[n, h] = (bank(opens_bank), opens_bank)
             rows = slice(n * P, (n + 1) * P)
             fp4_bytes = slice(2 * n * P, 2 * (n + 1) * P)
             c, lo = divmod(n * P, CHUNK)
@@ -145,14 +153,31 @@ def tile_list_tiert_xdl_silu_kernel(
             else:
                 w, w_s, a, a_s = wx_w[:, fp4_bytes].bitcast(FP4X4), wx_s[:, rows], xr_w[h], xr_s[h]
             nc.tensor.matmul_mx(
-                out=acc[:], lhsT=w, lhsT_scale=w_s, rhs=a[:].bitcast(FP8X4), rhs_scale=a_s[:], start=start, stop=stop
+                out=sums[n, h][0][:], lhsT=w, lhsT_scale=w_s, rhs=a[:].bitcast(FP8X4), rhs_scale=a_s[:],
+                start=opens_bank is not None, stop=closes,
             )
 
-        def finish(acc, n, h, lo, width):
-            res = results.tile([P, width], F32, name="res")
-            nc.scalar.activation(out=res[:], in_=acc[:, lo : lo + width], func=SILU, bias=b_cols[:, n : n + 1])
-            j0 = h * HALF + lo
-            nc.sync.dma_start(out=out[n * P : (n + 1) * P, j0 : j0 + width], in_=res[:])
+        def table_products(n):
+            product("wt4", n, 1, opens_bank=free_banks.pop(0))
+            product("wtd", n, 1)
+
+        def finish(n, h, parts=1):
+            acc, bank_index = sums[n, h]
+            width = HALF // parts
+            for lo in range(0, HALF, width):
+                res = results.tile([P, width], F32, name="res")
+                nc.scalar.activation(out=res[:], in_=acc[:, lo : lo + width], func=SILU, bias=b_cols[:, n : n + 1])
+                j0 = h * HALF + lo
+                nc.sync.dma_start(out=out[n * P : (n + 1) * P, j0 : j0 + width], in_=res[:])
+            free_banks.append(bank_index)
+
+        def close_pair(c):
+            for n in (2 * c, 2 * c + 1):
+                product("wtd", n, 0, closes=True)
+
+        def finish_pair(c):
+            for n in (2 * c, 2 * c + 1):
+                finish(n, 0)
 
         last = PACK - 1
         nc.gpsimd.memset(diagonal[:].bitcast(I32), 0)
@@ -161,209 +186,127 @@ def tile_list_tiert_xdl_silu_kernel(
             fill=1.0, base=-last, channel_multiplier=-PACK,
         )
         make_identity(nc, eye_f32[:])
-        nc.vector.quantize_mx(out=eye_w[last].bitcast(FP8X4), scales=eye_s[last], in_=diagonal[:, 0 : P * PACK])
+        last_eye = slice(last * P, PACK * P)
+        nc.vector.quantize_mx(out=eye_w[:, last_eye].bitcast(FP8X4), scales=eye_s[:, last_eye], in_=diagonal[:, 0 : P * PACK])
 
         nc.vector.memset(table_warm[:], 0.0)
         nc.scalar.activation(out=table_warm[:], in_=table_warm[:], func=SILU)
 
         nc.vector.memset(b_rows[:], 0.0)
-        nc.vector.memset(wx_s[:].bitcast(I32), 0)
-        nc.vector.memset(tab_s[:].bitcast(I32), 0)
-        nc.vector.memset(wt4_s[:].bitcast(I32), 0)
+        for plane in (wx_s, tab_s, wt4_s):
+            nc.vector.memset(plane[:].bitcast(I32), 0)
 
-        load_columns(x_loaded, x_planes, X_LOADS, 0)
+        load_chunk(x_raw, x_planes, 0)
         nc.sync.dma_start(out=b_rows[0:TILES, :], in_=b.rearrange("(c p) -> c p", p=P))
-        load_columns(x_loaded, x_planes, X_LOADS, 1)
+        load_chunk(x_raw, x_planes, 1)
         load_scales(wx_s, wx_scales)
         nc.sync.dma_start(out=wx_w[:].bitcast(I32), in_=wx_words[0].bitcast(I32))
         nc.sync.dma_start(out=tab_w[:], in_=tab_words[0].rearrange("p n t -> p (n t)").bitcast(I32))
         nc.sync.dma_start(offsets[:], offs)
-        load_columns(wtd_loaded, wtd_planes, WTD_LOADS, 0)
+        load_chunk(wtd_raw, wtd_planes, 0)
         load_scales(tab_s, tab_scales)
-        load_columns(wtd_loaded, wtd_planes, WTD_LOADS, 1)
+        load_chunk(wtd_raw, wtd_planes, 1)
         nc.sync.dma_start(out=wt4_w[:].bitcast(I32), in_=wt4_words[0].bitcast(I32))
         load_scales(wt4_s, wt4_scales)
-        load_columns(wtd_loaded, wtd_planes, WTD_LOADS, 2)
-        load_columns(x_loaded, x_planes, X_LOADS, 2)
-        load_columns(x_loaded, x_planes, X_LOADS, 3)
-        load_columns(wtd_loaded, wtd_planes, WTD_LOADS, 3)
+        load_chunk(wtd_raw, wtd_planes, 2)
+        load_chunk(x_raw, x_planes, 2)
+        load_chunk(x_raw, x_planes, 3)
+        load_chunk(wtd_raw, wtd_planes, 3)
 
         for t in reversed(range(last)):
             nc.vector.tensor_copy(out=eye_bf[:, t, :], in_=diagonal[:, last - t : last - t + P * PACK])
         for t in reversed(range(last)):
-            nc.vector.quantize_mx(out=eye_w[t].bitcast(FP8X4), scales=eye_s[t], in_=eye_bf[:, t, :])
+            columns = slice(t * P, (t + 1) * P)
+            nc.vector.quantize_mx(out=eye_w[:, columns].bitcast(FP8X4), scales=eye_s[:, columns], in_=eye_bf[:, t, :])
 
-        idle = bank(3)
-        for width in WARM_WIDTHS:
+        idle = bank(WARM_BANK)
+        for width in [P] * WARM_NARROW + [2 * P] * WARM_WIDE:
             nc.tensor.matmul_mx(
                 out=idle[:, 0:width],
-                lhsT=eye_w[last].bitcast(FP8X4), lhsT_scale=eye_s[last],
-                rhs=eye_words[:, PACK * P - width :].bitcast(FP8X4), rhs_scale=eye_scales[:, PACK * P - width :],
+                lhsT=eye_w[:, last_eye].bitcast(FP8X4), lhsT_scale=eye_s[:, last_eye],
+                rhs=eye_w[:, PACK * P - width :].bitcast(FP8X4), rhs_scale=eye_s[:, PACK * P - width :],
                 start=True, stop=True,
             )
 
-        b_turned = bank(3)
+        b_turned = bank(WARM_BANK)
         nc.tensor.transpose(b_turned[:, 0:P], b_rows[:], eye_f32[:])
         nc.scalar.copy(out=b_cols[:], in_=b_turned[:, 0:TILES])
 
-        x_bf[0] = keep.tile([P, CHUNK, PACK], BF16, name="staging", align_bytes=ALIGN)
-        round_chunk(x_bf[0], x_raw[0], X_ON_VECTOR[0])
+        round_x(0, "eye_bf", VECTOR_SHARE)
         quantise_chunk(xq_w, xq_s, x_bf, 0)
-        x_bf[1] = keep.tile([P, CHUNK, PACK], BF16, name="b_rows", align_bytes=ALIGN)
-        round_chunk(x_bf[1], x_raw[1], X_ON_VECTOR[1])
-        back[0] = bank(4)
-        dequantise(back[0], 0)
-        back[1] = bank(5)
-        dequantise(back[1], 1)
+        round_x(1, "b_rows", VECTOR_SHARE)
+        for piece in (0, 1):
+            dequantise(piece, PIECES + piece)
         quantise_chunk(xq_w, xq_s, x_bf, 1)
-        back[2] = bank(6)
-        dequantise(back[2], 2)
-        back[3] = bank(7)
-        dequantise(back[3], 3)
-        rest_bf[0] = keep.tile([P, CHUNK, PACK], BF16, name="rest_bf0", align_bytes=ALIGN)
-        residual(back[0], 0)
-        residual(back[1], 1)
-        sums[0, 0] = bank(0)
-        product(sums[0, 0], "xq", 0, 0, True, False)
-        sums[1, 0] = bank(1)
-        product(sums[1, 0], "xq", 1, 0, True, False)
-        sums[2, 0] = bank(2)
-        product(sums[2, 0], "xq", 2, 0, True, False)
-        sums[3, 0] = bank(3)
-        product(sums[3, 0], "xq", 3, 0, True, False)
-        rest_bf[1] = keep.tile([P, CHUNK, PACK], BF16, name="rest_bf1", align_bytes=ALIGN)
-        residual(back[2], 2)
-        residual(back[3], 3)
-        quantise_chunk(xr_w, xr_s, rest_bf, 0)
-        quantise_chunk(xr_w, xr_s, rest_bf, 1)
-        sums[4, 0] = bank(4)
-        product(sums[4, 0], "xq", 4, 0, True, False)
-        sums[5, 0] = bank(5)
-        product(sums[5, 0], "xq", 5, 0, True, False)
-        sums[6, 0] = bank(6)
-        product(sums[6, 0], "xq", 6, 0, True, False)
-        sums[7, 0] = bank(7)
-        product(sums[7, 0], "xq", 7, 0, True, False)
-        product(sums[0, 0], "xr", 0, 0, False, False)
-        product(sums[1, 0], "xr", 1, 0, False, False)
-        product(sums[2, 0], "xr", 2, 0, False, False)
-        product(sums[3, 0], "xr", 3, 0, False, False)
-        product(sums[4, 0], "xr", 4, 0, False, False)
-        product(sums[5, 0], "xr", 5, 0, False, False)
-        product(sums[6, 0], "xr", 6, 0, False, False)
-        product(sums[7, 0], "xr", 7, 0, False, False)
+        for piece in (2, 3):
+            dequantise(piece, PIECES + piece)
+        for n in range(PIECES):
+            product("xq", n, 0, opens_bank=n)
+        for piece in range(PIECES):
+            residual(piece)
+        for c in (0, 1):
+            quantise_chunk(xr_w, xr_s, rest_bf, c)
+        for n in range(PIECES, TILES):
+            product("xq", n, 0, opens_bank=free_banks.pop(0))
+        for n in range(TILES):
+            product("xr", n, 0)
+
         got_w[0] = shared.tile([P, HALF], U32, name="got_w0", align_bytes=ALIGN, offset=0)
-        nc.vector.tensor_copy(out=got_w[0][:], in_=tab_w[:].bitcast(U32).indirect(entries(0)))
+        gather(got_w[0], tab_w[:].bitcast(U32), 0)
         got_s[0] = shared.tile([P, HALF], U8, name="got_s0", align_bytes=ALIGN, offset=4 * HALF)
-        nc.vector.tensor_copy(out=got_s[0][:], in_=tab_s[:].indirect(entries(0)))
-        wtd_bf[0] = keep.tile([P, CHUNK, PACK], BF16, name="rest_bf0", align_bytes=ALIGN)
-        round_chunk(wtd_bf[0], wtd_raw[0], WTD_ON_VECTOR[0])
+        gather(got_s[0], tab_s[:], 0)
+        round_wtd(0, "rest_bf0")
         quantise_chunk(wtd_w, wtd_s, wtd_bf, 0)
-        wtd_bf[1] = keep.tile([P, CHUNK, PACK], BF16, name="wtd_bf1", align_bytes=ALIGN)
-        round_chunk(wtd_bf[1], wtd_raw[1], WTD_ON_VECTOR[1])
+        got_w[1] = tile("wtd_raw0", [P, HALF], U32)
+        gather(got_w[1], tab_w[:].bitcast(U32), 1)
+        round_wtd(1, "wtd_bf1")
         quantise_chunk(wtd_w, wtd_s, wtd_bf, 1)
-        got_w[1] = keep.tile([P, HALF], U32, name="wtd_raw1", align_bytes=ALIGN)
-        nc.vector.tensor_copy(out=got_w[1][:], in_=tab_w[:].bitcast(U32).indirect(entries(1)))
-        got_s[1] = keep.tile([P, HALF], U8, name="wtd_bf1", align_bytes=ALIGN)
-        nc.vector.tensor_copy(out=got_s[1][:], in_=tab_s[:].indirect(entries(1)))
-        wtd_bf[2] = keep.tile([P, CHUNK, PACK], BF16, name="wtd_bf2", align_bytes=ALIGN)
-        round_chunk(wtd_bf[2], wtd_raw[2], WTD_ON_VECTOR[2])
+        got_s[1] = tile("wtd_raw1", [P, HALF], U8)
+        gather(got_s[1], tab_s[:], 1)
+        round_wtd(2, "wtd_bf2")
         quantise_chunk(wtd_w, wtd_s, wtd_bf, 2)
-        product(sums[0, 0], "wt4", 0, 0, False, False)
-        product(sums[1, 0], "wt4", 1, 0, False, False)
-        product(sums[2, 0], "wt4", 2, 0, False, False)
-        product(sums[0, 0], "wtd", 0, 0, False, True)
-        product(sums[1, 0], "wtd", 1, 0, False, True)
-        product(sums[3, 0], "wt4", 3, 0, False, False)
-        product(sums[2, 0], "wtd", 2, 0, False, True)
-        product(sums[3, 0], "wtd", 3, 0, False, True)
-        product(sums[4, 0], "wt4", 4, 0, False, False)
-        product(sums[5, 0], "wt4", 5, 0, False, False)
-        product(sums[6, 0], "wt4", 6, 0, False, False)
-        product(sums[7, 0], "wt4", 7, 0, False, False)
-        finish(sums[0, 0], 0, 0, 0, HALF)
-        finish(sums[1, 0], 1, 0, 0, HALF)
-        x_bf[2] = keep.tile([P, CHUNK, PACK], BF16, name="x_bf2", align_bytes=ALIGN)
-        round_chunk(x_bf[2], x_raw[2], X_ON_VECTOR[2])
-        finish(sums[2, 0], 2, 0, 0, HALF)
-        finish(sums[3, 0], 3, 0, 0, HALF)
-        sums[0, 1] = bank(0)
-        product(sums[0, 1], "wt4", 0, 1, True, False)
-        product(sums[0, 1], "wtd", 0, 1, False, False)
-        sums[1, 1] = bank(1)
-        product(sums[1, 1], "wt4", 1, 1, True, False)
-        product(sums[1, 1], "wtd", 1, 1, False, False)
-        product(sums[4, 0], "wtd", 4, 0, False, True)
-        product(sums[5, 0], "wtd", 5, 0, False, True)
-        finish(sums[4, 0], 4, 0, 0, HALF)
-        finish(sums[5, 0], 5, 0, 0, HALF)
-        wtd_bf[3] = keep.tile([P, CHUNK, PACK], BF16, name="wtd_bf3", align_bytes=ALIGN)
-        round_chunk(wtd_bf[3], wtd_raw[3], WTD_ON_VECTOR[3])
+
+        for c in (0, 1):
+            for n in range(c * LEAD, (c + 1) * LEAD):
+                product("wt4", n, 0)
+            close_pair(c)
+        for n in range(2 * LEAD, TILES):
+            product("wt4", n, 0)
+        for c in (0, 1):
+            finish_pair(c)
+
+        for n in (0, 1):
+            table_products(n)
+        close_pair(2)
+        round_wtd(3, "wtd_bf3")
+        finish_pair(2)
+        round_x(2, "x_bf2", CHUNK)
         quantise_chunk(xq_w, xq_s, x_bf, 2)
-        back[4] = bank(2)
-        dequantise(back[4], 4)
-        back[5] = bank(3)
-        dequantise(back[5], 5)
-        x_bf[3] = keep.tile([P, CHUNK, PACK], BF16, name="x_bf3", align_bytes=ALIGN)
-        round_chunk(x_bf[3], x_raw[3], X_ON_VECTOR[3])
+        for piece in (PIECES, PIECES + 1):
+            dequantise(piece, free_banks.pop(0))
+        round_x(3, "x_bf3", CHUNK)
         quantise_chunk(xq_w, xq_s, x_bf, 3)
-        rest_bf[2] = keep.tile([P, CHUNK, PACK], BF16, name="rest_bf2", align_bytes=ALIGN)
-        residual(back[4], 4)
-        residual(back[5], 5)
-        sums[2, 1] = bank(4)
-        product(sums[2, 1], "wt4", 2, 1, True, False)
-        product(sums[2, 1], "wtd", 2, 1, False, False)
-        back[6] = bank(5)
-        dequantise(back[6], 6)
-        product(sums[0, 1], "xq", 0, 1, False, False)
-        product(sums[1, 1], "xq", 1, 1, False, False)
-        product(sums[2, 1], "xq", 2, 1, False, False)
-        back[7] = bank(2)
-        dequantise(back[7], 7)
+        for piece in (PIECES, PIECES + 1):
+            residual(piece)
+        table_products(2)
+        dequantise(PIECES + 2, free_banks.pop(0))
+        for n in (0, 1, 2):
+            product("xq", n, 1)
+        dequantise(PIECES + 3, free_banks.pop(0))
         quantise_chunk(wtd_w, wtd_s, wtd_bf, 3)
-        rest_bf[3] = keep.tile([P, CHUNK, PACK], BF16, name="rest_bf3", align_bytes=ALIGN)
-        residual(back[6], 6)
+        residual(PIECES + 2)
         quantise_chunk(xr_w, xr_s, rest_bf, 2)
-        residual(back[7], 7)
+        residual(PIECES + 3)
         quantise_chunk(xr_w, xr_s, rest_bf, 3)
-        sums[3, 1] = bank(3)
-        product(sums[3, 1], "wt4", 3, 1, True, False)
-        product(sums[3, 1], "wtd", 3, 1, False, False)
-        product(sums[3, 1], "xq", 3, 1, False, False)
-        product(sums[6, 0], "wtd", 6, 0, False, True)
-        product(sums[7, 0], "wtd", 7, 0, False, True)
-        finish(sums[6, 0], 6, 0, 0, HALF)
-        finish(sums[7, 0], 7, 0, 0, HALF)
-        product(sums[0, 1], "xr", 0, 1, False, True)
-        finish(sums[0, 1], 0, 1, 0, HALF)
-        product(sums[1, 1], "xr", 1, 1, False, True)
-        finish(sums[1, 1], 1, 1, 0, HALF)
-        product(sums[2, 1], "xr", 2, 1, False, True)
-        finish(sums[2, 1], 2, 1, 0, HALF)
-        product(sums[3, 1], "xr", 3, 1, False, True)
-        finish(sums[3, 1], 3, 1, 0, HALF)
-        sums[4, 1] = bank(5)
-        product(sums[4, 1], "wt4", 4, 1, True, False)
-        product(sums[4, 1], "wtd", 4, 1, False, False)
-        product(sums[4, 1], "xq", 4, 1, False, False)
-        product(sums[4, 1], "xr", 4, 1, False, True)
-        finish(sums[4, 1], 4, 1, 0, HALF)
-        sums[5, 1] = bank(2)
-        product(sums[5, 1], "wt4", 5, 1, True, False)
-        product(sums[5, 1], "wtd", 5, 1, False, False)
-        product(sums[5, 1], "xq", 5, 1, False, False)
-        product(sums[5, 1], "xr", 5, 1, False, True)
-        finish(sums[5, 1], 5, 1, 0, HALF)
-        sums[6, 1] = bank(6)
-        product(sums[6, 1], "wt4", 6, 1, True, False)
-        product(sums[6, 1], "wtd", 6, 1, False, False)
-        product(sums[6, 1], "xq", 6, 1, False, False)
-        product(sums[6, 1], "xr", 6, 1, False, True)
-        finish(sums[6, 1], 6, 1, 0, HALF)
-        sums[7, 1] = bank(7)
-        product(sums[7, 1], "wt4", 7, 1, True, False)
-        product(sums[7, 1], "wtd", 7, 1, False, False)
-        product(sums[7, 1], "xq", 7, 1, False, False)
-        product(sums[7, 1], "xr", 7, 1, False, True)
-        finish(sums[7, 1], 7, 1, 0, HALF // 2)
-        finish(sums[7, 1], 7, 1, HALF // 2, HALF // 2)
+        table_products(3)
+        product("xq", 3, 1)
+        close_pair(3)
+        finish_pair(3)
+
+        opened = PIECES
+        for n in range(TILES):
+            if n >= opened:
+                table_products(n)
+                product("xq", n, 1)
+            product("xr", n, 1, closes=True)
+            finish(n, 1, parts=2 if n == TILES - 1 else 1)

@@ -23,7 +23,7 @@ CHUNK = 256
 TILES = N // P
 PIECES = HALF // P
 RUN = 2
-ALIGN = 64
+ALIGN = 256
 RESULT_BUFS = 2 * TILES + 1
 VECTOR_SHARE = 160
 LEAD = 3

@@ -24,10 +24,10 @@ TILES = N // P
 PIECES = HALF // P
 RUN = 2
 ALIGN = 256
-RESULT_BUFS = 2 * TILES + 1
+RESULT_BUFS = 2 * TILES + 3
 VECTOR_SHARE = 160
 LEAD = 3
-WARM_NARROW, WARM_WIDE = 4, 5
+WARM_NARROW, WARM_WIDE = 4, 3
 WARM_BANK = PIECES - 1
 
 
@@ -46,6 +46,8 @@ def tile_list_tiert_xdl_silu_kernel(
     with ExitStack() as ctx:
         keep = ctx.enter_context(tc.tile_pool(name="keep", bufs=1))
         shared = ctx.enter_context(tc.tile_pool(name="shared", bufs=1))
+        early = ctx.enter_context(tc.tile_pool(name="early", bufs=1))
+        later = ctx.enter_context(tc.tile_pool(name="later", bufs=1))
         results = ctx.enter_context(tc.tile_pool(name="results", bufs=RESULT_BUFS))
         psum = ctx.enter_context(tc.psum_pool(name="psum", bufs=1))
 
@@ -62,15 +64,20 @@ def tile_list_tiert_xdl_silu_kernel(
         tab_w, tab_s = tile("tab_w", [P, T], I32), tile("tab_s", [P, T], U8)
         wt4_w, wt4_s = tile("wt4_w", [P, 2 * N], U8), tile("wt4_s", [P, N], U8)
         wx_w, wx_s = tile("wx_w", [P, 2 * N], U8), tile("wx_s", [P, N], U8)
-        x_raw = [tile("x_raw%d" % c, [P, PACK, CHUNK], F32) for c in (0, 2, 3)]
-        x_raw.insert(1, shared.tile([P, PACK, CHUNK], F32, name="x_raw1", align_bytes=ALIGN, offset=0))
-        wtd_raw = tiles("wtd_raw", N // CHUNK, [P, PACK, CHUNK], F32)
+        x_first = tiles("x_first", PIECES - 1, [P, PACK, P], F32)
+        x_first.append(shared.tile([P, PACK, P], F32, name="x_first3", align_bytes=ALIGN, offset=2 * HALF))
+        x_raw = {c: tile("x_raw%d" % c, [P, PACK, CHUNK], F32) for c in (2, 3)}
+        wtd_raw = {c: tile("wtd_raw%d" % c, [P, PACK, CHUNK], F32) for c in (0, 3)}
+        for c in (1, 2):
+            wtd_raw[c] = later.tile(
+                [P, PACK, CHUNK], F32, name="wtd_raw%d" % c, align_bytes=ALIGN, offset=(c - 1) * 10 * HALF
+            )
         xq_w, xq_s = tiles("xq_w", 2, [P, HALF], U32), tiles("xq_s", 2, [P, HALF], U8)
         xr_w, xr_s = tiles("xr_w", 2, [P, HALF], U32), tiles("xr_s", 2, [P, HALF], U8)
         wtd_w, wtd_s = tiles("wtd_w", N // CHUNK, [P, CHUNK], U32), tiles("wtd_s", N // CHUNK, [P, CHUNK], U8)
         eye_w, eye_s = tile("eye_w", [P, PACK * P], U32), tile("eye_s", [P, PACK * P], U8)
         eye_f32 = keep.tile([P, P], F32, name="eye_f32")
-        eye_bf = tile("eye_bf", [P, PACK - 1, P * PACK], BF16)
+        eye_bf = early.tile([P, PACK - 1, P * PACK], BF16, name="eye_bf", align_bytes=ALIGN, offset=0)
         diagonal = tile("diagonal", [P, P * PACK + PACK], BF16)
         b_rows = tile("b_rows", [P, P], F32)
         b_cols = keep.tile([P, TILES], F32, name="b_cols")
@@ -109,6 +116,15 @@ def tile_list_tiert_xdl_silu_kernel(
                 in_=src[c][:].rearrange("p c t -> p (c t)"),
             )
 
+        def quantise_piece(words, scales, src, piece):
+            columns = slice(piece * P, (piece + 1) * P)
+            nc.vector.quantize_mx(
+                out=words[:, columns].bitcast(FP8X4), scales=scales[:, columns], in_=src.rearrange("p c t -> p (c t)")
+            )
+
+        def load_piece(piece):
+            nc.sync.dma_start(out=x_first[piece][:], in_=x_planes[:, :, piece * P : (piece + 1) * P])
+
         def dequantise(piece, bank_index):
             h, lo = divmod(piece * P, HALF)
             back[piece] = (bank(bank_index), bank_index)
@@ -128,7 +144,7 @@ def tile_list_tiert_xdl_silu_kernel(
             values, bank_index = back[piece]
             nc.vector.tensor_tensor(
                 out=packed_by_runs(rest_bf[c][:, lo : lo + P, :]),
-                in0=planes_by_runs(x_raw[c][:, :, lo : lo + P]),
+                in0=planes_by_runs(x_first[piece][:] if piece < PIECES else x_raw[c][:, :, lo : lo + P]),
                 in1=values[:].rearrange("p (t c i) -> p c t i", t=PACK, i=RUN),
                 op=mybir.AluOpType.subtract,
             )
@@ -138,7 +154,7 @@ def tile_list_tiert_xdl_silu_kernel(
             entries = offsets[:, h * (HALF // 16) : (h + 1) * (HALF // 16)]
             nc.vector.tensor_copy(out=dst[:], in_=table.indirect(entries))
 
-        def product(term, n, h, opens_bank=None, closes=False):
+        def product(term, n, h, opens_bank=None, closes=False, lo_j=0, width=HALF):
             if opens_bank is not None:
                 sums[n, h] = (bank(opens_bank), opens_bank)
             rows = slice(n * P, (n + 1) * P)
@@ -153,7 +169,8 @@ def tile_list_tiert_xdl_silu_kernel(
             else:
                 w, w_s, a, a_s = wx_w[:, fp4_bytes].bitcast(FP4X4), wx_s[:, rows], xr_w[h], xr_s[h]
             nc.tensor.matmul_mx(
-                out=sums[n, h][0][:], lhsT=w, lhsT_scale=w_s, rhs=a[:].bitcast(FP8X4), rhs_scale=a_s[:],
+                out=sums[n, h][0][:, 0:width], lhsT=w, lhsT_scale=w_s,
+                rhs=a[:, lo_j : lo_j + width].bitcast(FP8X4), rhs_scale=a_s[:, lo_j : lo_j + width],
                 start=opens_bank is not None, stop=closes,
             )
 
@@ -161,13 +178,15 @@ def tile_list_tiert_xdl_silu_kernel(
             product("wt4", n, 1, opens_bank=free_banks.pop(0))
             product("wtd", n, 1)
 
-        def finish(n, h, parts=1):
+        def finish(n, h, lo_j=0, width=HALF):
             acc, bank_index = sums[n, h]
-            width = HALF // parts
-            for lo in range(0, HALF, width):
-                res = results.tile([P, width], F32, name="res")
+            for lo in (0,):
+                if h == 0 and n < 4:
+                    res = later.tile([P, width], F32, name="res%d" % n, align_bytes=ALIGN, offset=n * 5 * HALF)
+                else:
+                    res = results.tile([P, width], F32, name="res")
                 nc.scalar.activation(out=res[:], in_=acc[:, lo : lo + width], func=SILU, bias=b_cols[:, n : n + 1])
-                j0 = h * HALF + lo
+                j0 = h * HALF + lo_j
                 nc.sync.dma_start(out=out[n * P : (n + 1) * P, j0 : j0 + width], in_=res[:])
             free_banks.append(bank_index)
 
@@ -196,18 +215,19 @@ def tile_list_tiert_xdl_silu_kernel(
         for plane in (wx_s, tab_s, wt4_s):
             nc.vector.memset(plane[:].bitcast(I32), 0)
 
-        load_chunk(x_raw, x_planes, 0)
+        load_piece(0)
         nc.sync.dma_start(out=b_rows[0:TILES, :], in_=b.rearrange("(c p) -> c p", p=P))
-        load_chunk(x_raw, x_planes, 1)
+        for piece in range(1, PIECES):
+            load_piece(piece)
         load_scales(wx_s, wx_scales)
         nc.sync.dma_start(out=wx_w[:].bitcast(I32), in_=wx_words[0].bitcast(I32))
         nc.sync.dma_start(out=tab_w[:], in_=tab_words[0].rearrange("p n t -> p (n t)").bitcast(I32))
         nc.sync.dma_start(offsets[:], offs)
-        load_chunk(wtd_raw, wtd_planes, 0)
         load_scales(tab_s, tab_scales)
-        load_chunk(wtd_raw, wtd_planes, 1)
         nc.sync.dma_start(out=wt4_w[:].bitcast(I32), in_=wt4_words[0].bitcast(I32))
+        load_chunk(wtd_raw, wtd_planes, 0)
         load_scales(wt4_s, wt4_scales)
+        load_chunk(wtd_raw, wtd_planes, 1)
         load_chunk(wtd_raw, wtd_planes, 2)
         load_chunk(x_raw, x_planes, 2)
         load_chunk(x_raw, x_planes, 3)
@@ -228,24 +248,30 @@ def tile_list_tiert_xdl_silu_kernel(
                 start=True, stop=True,
             )
 
-        b_turned = bank(WARM_BANK)
-        nc.tensor.transpose(b_turned[:, 0:P], b_rows[:], eye_f32[:])
+        for piece in range(PIECES):
+            if piece == 0:
+                rounded = tile("diagonal", [P, P, PACK], BF16)
+                round_columns(nc.scalar.copy, rounded, x_first[piece], 0, P)
+            else:
+                rounded = early.tile(
+                    [P, P, PACK], BF16, name="rounded%d" % piece, align_bytes=ALIGN, offset=(piece - 1) * 2 * P * PACK
+                )
+                round_columns(nc.scalar.copy, rounded, x_first[piece], 0, P)
+            quantise_piece(xq_w[0], xq_s[0], rounded[:], piece)
+            dequantise(piece, PIECES + piece)
+            if piece == 1:
+                residual(0)
+                b_turned = bank(PIECES)
+                nc.tensor.transpose(b_turned[:, 0:P], b_rows[:], eye_f32[:])
+        for piece in (1, 2):
+            residual(piece)
         nc.scalar.copy(out=b_cols[:], in_=b_turned[:, 0:TILES])
-
-        round_x(0, "eye_bf", VECTOR_SHARE)
-        quantise_chunk(xq_w, xq_s, x_bf, 0)
-        round_x(1, "b_rows", VECTOR_SHARE)
-        for piece in (0, 1):
-            dequantise(piece, PIECES + piece)
-        quantise_chunk(xq_w, xq_s, x_bf, 1)
-        for piece in (2, 3):
-            dequantise(piece, PIECES + piece)
         for n in range(PIECES):
             product("xq", n, 0, opens_bank=n)
-        for piece in range(PIECES):
-            residual(piece)
-        for c in (0, 1):
-            quantise_chunk(xr_w, xr_s, rest_bf, c)
+        quantise_chunk(xr_w, xr_s, rest_bf, 0)
+        residual(PIECES - 1)
+        for piece in (2, 3):
+            quantise_piece(xr_w[0], xr_s[0], rest_bf[1][:, (piece - 2) * P : (piece - 1) * P, :], piece)
         for n in range(PIECES, TILES):
             product("xq", n, 0, opens_bank=free_banks.pop(0))
         for n in range(TILES):
@@ -261,52 +287,58 @@ def tile_list_tiert_xdl_silu_kernel(
         gather(got_w[1], tab_w[:].bitcast(U32), 1)
         round_wtd(1, "wtd_bf1")
         quantise_chunk(wtd_w, wtd_s, wtd_bf, 1)
-        got_s[1] = tile("wtd_raw1", [P, HALF], U8)
+        got_s[1] = later.tile([P, HALF], U8, name="got_s1", align_bytes=ALIGN, offset=4 * HALF)
         gather(got_s[1], tab_s[:], 1)
-        round_wtd(2, "wtd_bf2")
-        quantise_chunk(wtd_w, wtd_s, wtd_bf, 2)
 
-        for c in (0, 1):
-            for n in range(c * LEAD, (c + 1) * LEAD):
-                product("wt4", n, 0)
-            close_pair(c)
-        for n in range(2 * LEAD, TILES):
+        for n in (0, 1):
             product("wt4", n, 0)
-        for c in (0, 1):
-            finish_pair(c)
+        close_pair(0)
+        for n in range(2, TILES):
+            product("wt4", n, 0)
+            if n == 4:
+                close_pair(1)
+        finish_pair(0)
+        round_wtd(2, "wtd_bf2")
+        finish_pair(1)
+        round_x(2, "x_bf2", CHUNK)
+        quantise_chunk(wtd_w, wtd_s, wtd_bf, 2)
+        quantise_chunk(xq_w, xq_s, x_bf, 2)
 
         for n in (0, 1):
             table_products(n)
         close_pair(2)
         round_wtd(3, "wtd_bf3")
         finish_pair(2)
-        round_x(2, "x_bf2", CHUNK)
-        quantise_chunk(xq_w, xq_s, x_bf, 2)
         for piece in (PIECES, PIECES + 1):
             dequantise(piece, free_banks.pop(0))
         round_x(3, "x_bf3", CHUNK)
         quantise_chunk(xq_w, xq_s, x_bf, 3)
-        for piece in (PIECES, PIECES + 1):
-            residual(piece)
-        table_products(2)
-        dequantise(PIECES + 2, free_banks.pop(0))
-        for n in (0, 1, 2):
-            product("xq", n, 1)
-        dequantise(PIECES + 3, free_banks.pop(0))
+        residual(PIECES)
         quantise_chunk(wtd_w, wtd_s, wtd_bf, 3)
-        residual(PIECES + 2)
-        quantise_chunk(xr_w, xr_s, rest_bf, 2)
-        residual(PIECES + 3)
-        quantise_chunk(xr_w, xr_s, rest_bf, 3)
-        table_products(3)
-        product("xq", 3, 1)
+        residual(PIECES + 1)
+        for n in (0, 1):
+            product("xq", n, 1)
         close_pair(3)
         finish_pair(3)
+        for piece in (PIECES + 2, PIECES + 3):
+            dequantise(piece, free_banks.pop(0))
+        quantise_chunk(xr_w, xr_s, rest_bf, 2)
+        for n in (2, 3, 4):
+            table_products(n)
+            product("xq", n, 1)
+        for piece in (PIECES + 2, PIECES + 3):
+            residual(piece)
+        quantise_chunk(xr_w, xr_s, rest_bf, 3)
 
-        opened = PIECES
-        for n in range(TILES):
+        opened = PIECES + 1
+        for n in range(TILES - 1):
             if n >= opened:
                 table_products(n)
                 product("xq", n, 1)
             product("xr", n, 1, closes=True)
-            finish(n, 1, parts=2 if n == TILES - 1 else 1)
+            finish(n, 1)
+        for lo_j in range(0, HALF, P):
+            for term in ("wt4", "wtd", "xq", "xr"):
+                opens = free_banks.pop(0) if term == "wt4" else None
+                product(term, TILES - 1, 1, opens_bank=opens, closes=term == "xr", lo_j=lo_j, width=P)
+            finish(TILES - 1, 1, lo_j, P)

@@ -307,28 +307,30 @@ def tile_list_tiert_xdl_silu_kernel(
         for n in (0, 1):
             table_products(n)
         close_pair(2)
-        round_wtd(3, "wtd_bf3")
         finish_pair(2)
+        round_wtd(3, "wtd_bf3")
         for piece in (PIECES, PIECES + 1):
             dequantise(piece, free_banks.pop(0))
         round_x(3, "x_bf3", CHUNK)
         quantise_chunk(xq_w, xq_s, x_bf, 3)
-        residual(PIECES)
-        quantise_chunk(wtd_w, wtd_s, wtd_bf, 3)
-        residual(PIECES + 1)
+        for piece in (PIECES, PIECES + 1):
+            residual(piece)
         for n in (0, 1):
             product("xq", n, 1)
-        close_pair(3)
-        finish_pair(3)
         for piece in (PIECES + 2, PIECES + 3):
             dequantise(piece, free_banks.pop(0))
+        residual(PIECES + 2)
+        quantise_chunk(wtd_w, wtd_s, wtd_bf, 3)
         quantise_chunk(xr_w, xr_s, rest_bf, 2)
-        for n in (2, 3, 4):
+        for n in (2, 3):
             table_products(n)
             product("xq", n, 1)
-        for piece in (PIECES + 2, PIECES + 3):
-            residual(piece)
+        close_pair(3)
+        table_products(4)
+        product("xq", 4, 1)
+        residual(PIECES + 3)
         quantise_chunk(xr_w, xr_s, rest_bf, 3)
+        finish_pair(3)
 
         opened = PIECES + 1
         for n in range(TILES - 1):

@@ -27,7 +27,7 @@ ALIGN = 256
 RESULT_BUFS = 2 * TILES + 3
 VECTOR_SHARE = 160
 LEAD = 3
-WARM_NARROW, WARM_WIDE = 4, 3
+WARM_NARROW, WARM_WIDE = 4, 2
 WARM_BANK = PIECES - 1
 
 
@@ -67,11 +67,8 @@ def tile_list_tiert_xdl_silu_kernel(
         x_first = tiles("x_first", PIECES - 1, [P, PACK, P], F32)
         x_first.append(shared.tile([P, PACK, P], F32, name="x_first3", align_bytes=ALIGN, offset=2 * HALF))
         x_raw = {c: tile("x_raw%d" % c, [P, PACK, CHUNK], F32) for c in (2, 3)}
-        wtd_raw = {c: tile("wtd_raw%d" % c, [P, PACK, CHUNK], F32) for c in (0, 3)}
-        for c in (1, 2):
-            wtd_raw[c] = later.tile(
-                [P, PACK, CHUNK], F32, name="wtd_raw%d" % c, align_bytes=ALIGN, offset=(c - 1) * 10 * HALF
-            )
+        wtd_raw = {c: tile("wtd_raw%d" % c, [P, PACK, CHUNK], F32) for c in (0, 1, 3)}
+        wtd_raw[2] = later.tile([P, 2 * PACK, CHUNK], F32, name="wtd_raw2", align_bytes=ALIGN, offset=0)[:, 0:PACK, :]
         xq_w, xq_s = tiles("xq_w", 2, [P, HALF], U32), tiles("xq_s", 2, [P, HALF], U8)
         xr_w, xr_s = tiles("xr_w", 2, [P, HALF], U32), tiles("xr_s", 2, [P, HALF], U8)
         wtd_w, wtd_s = tiles("wtd_w", N // CHUNK, [P, CHUNK], U32), tiles("wtd_s", N // CHUNK, [P, CHUNK], U8)
@@ -182,7 +179,7 @@ def tile_list_tiert_xdl_silu_kernel(
             acc, bank_index = sums[n, h]
             for lo in (0,):
                 if h == 0 and n < 4:
-                    res = later.tile([P, width], F32, name="res%d" % n, align_bytes=ALIGN, offset=n * 5 * HALF)
+                    res = later.tile([P, width], F32, name="res%d" % n, align_bytes=ALIGN, offset=n * 4 * HALF)
                 else:
                     res = results.tile([P, width], F32, name="res")
                 nc.scalar.activation(out=res[:], in_=acc[:, lo : lo + width], func=SILU, bias=b_cols[:, n : n + 1])
@@ -221,13 +218,13 @@ def tile_list_tiert_xdl_silu_kernel(
             load_piece(piece)
         load_scales(wx_s, wx_scales)
         nc.sync.dma_start(out=wx_w[:].bitcast(I32), in_=wx_words[0].bitcast(I32))
-        nc.sync.dma_start(out=tab_w[:], in_=tab_words[0].rearrange("p n t -> p (n t)").bitcast(I32))
+        load_chunk(wtd_raw, wtd_planes, 0)
         nc.sync.dma_start(offsets[:], offs)
         load_scales(tab_s, tab_scales)
-        nc.sync.dma_start(out=wt4_w[:].bitcast(I32), in_=wt4_words[0].bitcast(I32))
-        load_chunk(wtd_raw, wtd_planes, 0)
+        nc.sync.dma_start(out=tab_w[:], in_=tab_words[0].rearrange("p n t -> p (n t)").bitcast(I32))
         load_scales(wt4_s, wt4_scales)
         load_chunk(wtd_raw, wtd_planes, 1)
+        nc.sync.dma_start(out=wt4_w[:].bitcast(I32), in_=wt4_words[0].bitcast(I32))
         load_chunk(wtd_raw, wtd_planes, 2)
         load_chunk(x_raw, x_planes, 2)
         load_chunk(x_raw, x_planes, 3)
@@ -248,10 +245,12 @@ def tile_list_tiert_xdl_silu_kernel(
                 start=True, stop=True,
             )
 
+        b_turned = bank(WARM_BANK)
+        nc.tensor.transpose(b_turned[:, 0:P], b_rows[:], eye_f32[:])
         for piece in range(PIECES):
-            if piece == 0:
+            if piece % 2 == 0:
                 rounded = tile("diagonal", [P, P, PACK], BF16)
-                round_columns(nc.scalar.copy, rounded, x_first[piece], 0, P)
+                round_columns(nc.vector.tensor_copy, rounded, x_first[piece], 0, P)
             else:
                 rounded = early.tile(
                     [P, P, PACK], BF16, name="rounded%d" % piece, align_bytes=ALIGN, offset=(piece - 1) * 2 * P * PACK
@@ -259,10 +258,8 @@ def tile_list_tiert_xdl_silu_kernel(
                 round_columns(nc.scalar.copy, rounded, x_first[piece], 0, P)
             quantise_piece(xq_w[0], xq_s[0], rounded[:], piece)
             dequantise(piece, PIECES + piece)
-            if piece == 1:
+            if piece == 2:
                 residual(0)
-                b_turned = bank(PIECES)
-                nc.tensor.transpose(b_turned[:, 0:P], b_rows[:], eye_f32[:])
         for piece in (1, 2):
             residual(piece)
         nc.scalar.copy(out=b_cols[:], in_=b_turned[:, 0:TILES])
@@ -277,18 +274,20 @@ def tile_list_tiert_xdl_silu_kernel(
         for n in range(TILES):
             product("xr", n, 0)
 
-        got_w[0] = shared.tile([P, HALF], U32, name="got_w0", align_bytes=ALIGN, offset=0)
-        gather(got_w[0], tab_w[:].bitcast(U32), 0)
         got_s[0] = shared.tile([P, HALF], U8, name="got_s0", align_bytes=ALIGN, offset=4 * HALF)
         gather(got_s[0], tab_s[:], 0)
+        got_w[0] = shared.tile([P, HALF], U32, name="got_w0", align_bytes=ALIGN, offset=0)
+        gather(got_w[0], tab_w[:].bitcast(U32), 0)
         round_wtd(0, "rest_bf0")
         quantise_chunk(wtd_w, wtd_s, wtd_bf, 0)
-        got_w[1] = tile("wtd_raw0", [P, HALF], U32)
-        gather(got_w[1], tab_w[:].bitcast(U32), 1)
+        got_s[1] = tile("wtd_raw0", [P, HALF], U8)
+        gather(got_s[1], tab_s[:], 1)
         round_wtd(1, "wtd_bf1")
         quantise_chunk(wtd_w, wtd_s, wtd_bf, 1)
-        got_s[1] = later.tile([P, HALF], U8, name="got_s1", align_bytes=ALIGN, offset=4 * HALF)
-        gather(got_s[1], tab_s[:], 1)
+        got_w[1] = tile("wtd_raw1", [P, HALF], U32)
+        gather(got_w[1], tab_w[:].bitcast(U32), 1)
+        round_wtd(2, "wtd_bf2")
+        quantise_chunk(wtd_w, wtd_s, wtd_bf, 2)
 
         for n in (0, 1):
             product("wt4", n, 0)
@@ -298,10 +297,8 @@ def tile_list_tiert_xdl_silu_kernel(
             if n == 4:
                 close_pair(1)
         finish_pair(0)
-        round_wtd(2, "wtd_bf2")
         finish_pair(1)
         round_x(2, "x_bf2", CHUNK)
-        quantise_chunk(wtd_w, wtd_s, wtd_bf, 2)
         quantise_chunk(xq_w, xq_s, x_bf, 2)
 
         for n in (0, 1):

@@ -25,10 +25,13 @@ PIECES = HALF // P
 RUN = 2
 ALIGN = 256
 RESULT_BUFS = 2 * TILES + 3
-VECTOR_SHARE = 160
-LEAD = 3
+HELD_RESULTS = 4
+SECOND_PAIR_AFTER = 5
+OPENED_EARLY = 5
 WARM_NARROW, WARM_WIDE = 4, 2
 WARM_BANK = PIECES - 1
+RESULT_BYTES = 4 * HALF
+PIECE_BYTES = 2 * PACK * P
 
 
 def packed_by_runs(ap):
@@ -65,7 +68,7 @@ def tile_list_tiert_xdl_silu_kernel(
         wt4_w, wt4_s = tile("wt4_w", [P, 2 * N], U8), tile("wt4_s", [P, N], U8)
         wx_w, wx_s = tile("wx_w", [P, 2 * N], U8), tile("wx_s", [P, N], U8)
         x_first = tiles("x_first", PIECES - 1, [P, PACK, P], F32)
-        x_first.append(shared.tile([P, PACK, P], F32, name="x_first3", align_bytes=ALIGN, offset=2 * HALF))
+        x_first.append(shared.tile([P, PACK, P], F32, name="x_first3", align_bytes=ALIGN, offset=RESULT_BYTES // 2))
         x_raw = {c: tile("x_raw%d" % c, [P, PACK, CHUNK], F32) for c in (2, 3)}
         wtd_raw = {c: tile("wtd_raw%d" % c, [P, PACK, CHUNK], F32) for c in (0, 1, 3)}
         wtd_raw[2] = later.tile([P, 2 * PACK, CHUNK], F32, name="wtd_raw2", align_bytes=ALIGN, offset=0)[:, 0:PACK, :]
@@ -92,18 +95,16 @@ def tile_list_tiert_xdl_silu_kernel(
         def load_chunk(raw, planes, c):
             nc.sync.dma_start(out=raw[c][:], in_=planes[:, :, c * CHUNK : (c + 1) * CHUNK])
 
-        def round_columns(copy, dst, src, lo, hi):
-            copy(out=packed_by_runs(dst[:, lo:hi, :]), in_=planes_by_runs(src[:, :, lo:hi]))
+        def round_planes(copy, dst, src):
+            copy(out=packed_by_runs(dst[:]), in_=planes_by_runs(src[:]))
 
-        def round_x(c, buffer, on_vector):
-            x_bf[c] = tile(buffer, [P, CHUNK, PACK], BF16)
-            round_columns(nc.vector.tensor_copy, x_bf[c], x_raw[c], 0, on_vector)
-            if on_vector < CHUNK:
-                round_columns(nc.scalar.copy, x_bf[c], x_raw[c], on_vector, CHUNK)
+        def round_x(c):
+            x_bf[c] = tile("x_bf%d" % c, [P, CHUNK, PACK], BF16)
+            round_planes(nc.vector.tensor_copy, x_bf[c], x_raw[c])
 
         def round_wtd(c, buffer):
             wtd_bf[c] = tile(buffer, [P, CHUNK, PACK], BF16)
-            round_columns(nc.scalar.copy, wtd_bf[c], wtd_raw[c], 0, CHUNK)
+            round_planes(nc.scalar.copy, wtd_bf[c], wtd_raw[c])
 
         def quantise_chunk(words, scales, src, c):
             i, lo = divmod(c * CHUNK, words[0].shape[1])
@@ -151,7 +152,7 @@ def tile_list_tiert_xdl_silu_kernel(
             entries = offsets[:, h * (HALF // 16) : (h + 1) * (HALF // 16)]
             nc.vector.tensor_copy(out=dst[:], in_=table.indirect(entries))
 
-        def product(term, n, h, opens_bank=None, closes=False, lo_j=0, width=HALF):
+        def product(term, n, h, opens_bank=None, closes=False, first=0, width=HALF):
             if opens_bank is not None:
                 sums[n, h] = (bank(opens_bank), opens_bank)
             rows = slice(n * P, (n + 1) * P)
@@ -167,7 +168,7 @@ def tile_list_tiert_xdl_silu_kernel(
                 w, w_s, a, a_s = wx_w[:, fp4_bytes].bitcast(FP4X4), wx_s[:, rows], xr_w[h], xr_s[h]
             nc.tensor.matmul_mx(
                 out=sums[n, h][0][:, 0:width], lhsT=w, lhsT_scale=w_s,
-                rhs=a[:, lo_j : lo_j + width].bitcast(FP8X4), rhs_scale=a_s[:, lo_j : lo_j + width],
+                rhs=a[:, first : first + width].bitcast(FP8X4), rhs_scale=a_s[:, first : first + width],
                 start=opens_bank is not None, stop=closes,
             )
 
@@ -175,16 +176,15 @@ def tile_list_tiert_xdl_silu_kernel(
             product("wt4", n, 1, opens_bank=free_banks.pop(0))
             product("wtd", n, 1)
 
-        def finish(n, h, lo_j=0, width=HALF):
+        def finish(n, h, first=0, width=HALF):
             acc, bank_index = sums[n, h]
-            for lo in (0,):
-                if h == 0 and n < 4:
-                    res = later.tile([P, width], F32, name="res%d" % n, align_bytes=ALIGN, offset=n * 4 * HALF)
-                else:
-                    res = results.tile([P, width], F32, name="res")
-                nc.scalar.activation(out=res[:], in_=acc[:, lo : lo + width], func=SILU, bias=b_cols[:, n : n + 1])
-                j0 = h * HALF + lo_j
-                nc.sync.dma_start(out=out[n * P : (n + 1) * P, j0 : j0 + width], in_=res[:])
+            if h == 0 and n < HELD_RESULTS:
+                res = later.tile([P, width], F32, name="res%d" % n, align_bytes=ALIGN, offset=n * RESULT_BYTES)
+            else:
+                res = results.tile([P, width], F32, name="res")
+            nc.scalar.activation(out=res[:], in_=acc[:, 0:width], func=SILU, bias=b_cols[:, n : n + 1])
+            j0 = h * HALF + first
+            nc.sync.dma_start(out=out[n * P : (n + 1) * P, j0 : j0 + width], in_=res[:])
             free_banks.append(bank_index)
 
         def close_pair(c):
@@ -223,8 +223,8 @@ def tile_list_tiert_xdl_silu_kernel(
         load_scales(tab_s, tab_scales)
         nc.sync.dma_start(out=tab_w[:], in_=tab_words[0].rearrange("p n t -> p (n t)").bitcast(I32))
         load_scales(wt4_s, wt4_scales)
-        load_chunk(wtd_raw, wtd_planes, 1)
         nc.sync.dma_start(out=wt4_w[:].bitcast(I32), in_=wt4_words[0].bitcast(I32))
+        load_chunk(wtd_raw, wtd_planes, 1)
         load_chunk(wtd_raw, wtd_planes, 2)
         load_chunk(x_raw, x_planes, 2)
         load_chunk(x_raw, x_planes, 3)
@@ -247,18 +247,19 @@ def tile_list_tiert_xdl_silu_kernel(
 
         b_turned = bank(WARM_BANK)
         nc.tensor.transpose(b_turned[:, 0:P], b_rows[:], eye_f32[:])
+
         for piece in range(PIECES):
             if piece % 2 == 0:
                 rounded = tile("diagonal", [P, P, PACK], BF16)
-                round_columns(nc.vector.tensor_copy, rounded, x_first[piece], 0, P)
+                round_planes(nc.vector.tensor_copy, rounded, x_first[piece])
             else:
                 rounded = early.tile(
-                    [P, P, PACK], BF16, name="rounded%d" % piece, align_bytes=ALIGN, offset=(piece - 1) * 2 * P * PACK
+                    [P, P, PACK], BF16, name="rounded%d" % piece, align_bytes=ALIGN, offset=(piece - 1) * PIECE_BYTES
                 )
-                round_columns(nc.scalar.copy, rounded, x_first[piece], 0, P)
+                round_planes(nc.scalar.copy, rounded, x_first[piece])
             quantise_piece(xq_w[0], xq_s[0], rounded[:], piece)
             dequantise(piece, PIECES + piece)
-            if piece == 2:
+            if piece == PIECES - 2:
                 residual(0)
         for piece in (1, 2):
             residual(piece)
@@ -274,7 +275,7 @@ def tile_list_tiert_xdl_silu_kernel(
         for n in range(TILES):
             product("xr", n, 0)
 
-        got_s[0] = shared.tile([P, HALF], U8, name="got_s0", align_bytes=ALIGN, offset=4 * HALF)
+        got_s[0] = shared.tile([P, HALF], U8, name="got_s0", align_bytes=ALIGN, offset=RESULT_BYTES)
         gather(got_s[0], tab_s[:], 0)
         got_w[0] = shared.tile([P, HALF], U32, name="got_w0", align_bytes=ALIGN, offset=0)
         gather(got_w[0], tab_w[:].bitcast(U32), 0)
@@ -294,13 +295,13 @@ def tile_list_tiert_xdl_silu_kernel(
         close_pair(0)
         for n in range(2, TILES):
             product("wt4", n, 0)
-            if n == 4:
+            if n == SECOND_PAIR_AFTER:
                 close_pair(1)
         finish_pair(0)
         finish_pair(1)
-        round_x(2, "x_bf2", CHUNK)
-        quantise_chunk(xq_w, xq_s, x_bf, 2)
 
+        round_x(2)
+        quantise_chunk(xq_w, xq_s, x_bf, 2)
         for n in (0, 1):
             table_products(n)
         close_pair(2)
@@ -308,7 +309,7 @@ def tile_list_tiert_xdl_silu_kernel(
         round_wtd(3, "wtd_bf3")
         for piece in (PIECES, PIECES + 1):
             dequantise(piece, free_banks.pop(0))
-        round_x(3, "x_bf3", CHUNK)
+        round_x(3)
         quantise_chunk(xq_w, xq_s, x_bf, 3)
         for piece in (PIECES, PIECES + 1):
             residual(piece)
@@ -323,21 +324,21 @@ def tile_list_tiert_xdl_silu_kernel(
             table_products(n)
             product("xq", n, 1)
         close_pair(3)
-        table_products(4)
-        product("xq", 4, 1)
+        table_products(OPENED_EARLY - 1)
+        product("xq", OPENED_EARLY - 1, 1)
         residual(PIECES + 3)
         quantise_chunk(xr_w, xr_s, rest_bf, 3)
         finish_pair(3)
 
-        opened = PIECES + 1
         for n in range(TILES - 1):
-            if n >= opened:
+            if n >= OPENED_EARLY:
                 table_products(n)
                 product("xq", n, 1)
             product("xr", n, 1, closes=True)
             finish(n, 1)
-        for lo_j in range(0, HALF, P):
-            for term in ("wt4", "wtd", "xq", "xr"):
-                opens = free_banks.pop(0) if term == "wt4" else None
-                product(term, TILES - 1, 1, opens_bank=opens, closes=term == "xr", lo_j=lo_j, width=P)
-            finish(TILES - 1, 1, lo_j, P)
+
+        for first in range(0, HALF, P):
+            product("wt4", TILES - 1, 1, opens_bank=free_banks.pop(0), first=first, width=P)
+            for term in ("wtd", "xq", "xr"):
+                product(term, TILES - 1, 1, closes=term == "xr", first=first, width=P)
+            finish(TILES - 1, 1, first, P)

@@ -51,6 +51,7 @@ def tile_list_tiert_xdl_silu_kernel(
         shared = ctx.enter_context(tc.tile_pool(name="shared", bufs=1))
         early = ctx.enter_context(tc.tile_pool(name="early", bufs=1))
         later = ctx.enter_context(tc.tile_pool(name="later", bufs=1))
+        middle = ctx.enter_context(tc.tile_pool(name="middle", bufs=1))
         results = ctx.enter_context(tc.tile_pool(name="results", bufs=RESULT_BUFS))
         psum = ctx.enter_context(tc.psum_pool(name="psum", bufs=1))
 
@@ -65,13 +66,14 @@ def tile_list_tiert_xdl_silu_kernel(
 
         offsets = keep.tile([P, J // 16], U16, name="offsets")
         tab_w, tab_s = tile("tab_w", [P, T], I32), tile("tab_s", [P, T], U8)
-        wt4_w, wt4_s = tile("wt4_w", [P, 2 * N], U8), tile("wt4_s", [P, N], U8)
+        wt4_w, wt4_s = tiles("wt4_w", 2, [P, N], U8), tile("wt4_s", [P, N], U8)
         wx_w, wx_s = tile("wx_w", [P, 2 * N], U8), tile("wx_s", [P, N], U8)
         x_first = tiles("x_first", PIECES - 1, [P, PACK, P], F32)
         x_first.append(shared.tile([P, PACK, P], F32, name="x_first3", align_bytes=ALIGN, offset=RESULT_BYTES // 2))
         x_raw = {c: tile("x_raw%d" % c, [P, PACK, CHUNK], F32) for c in (2, 3)}
-        wtd_raw = {c: tile("wtd_raw%d" % c, [P, PACK, CHUNK], F32) for c in (0, 1, 3)}
-        wtd_raw[2] = later.tile([P, 2 * PACK, CHUNK], F32, name="wtd_raw2", align_bytes=ALIGN, offset=0)[:, 0:PACK, :]
+        wtd_raw = {c: tile("wtd_raw%d" % c, [P, PACK, CHUNK], F32) for c in (0, 3)}
+        wtd_raw[1] = middle.tile([P, PACK + 2, CHUNK], F32, name="wtd_raw1", align_bytes=ALIGN, offset=0)[:, 0:PACK, :]
+        wtd_raw[2] = later.tile([P, PACK, CHUNK], F32, name="wtd_raw2", align_bytes=ALIGN, offset=0)
         xq_w, xq_s = tiles("xq_w", 2, [P, HALF], U32), tiles("xq_s", 2, [P, HALF], U8)
         xr_w, xr_s = tiles("xr_w", 2, [P, HALF], U32), tiles("xr_s", 2, [P, HALF], U8)
         wtd_w, wtd_s = tiles("wtd_w", N // CHUNK, [P, CHUNK], U32), tiles("wtd_s", N // CHUNK, [P, CHUNK], U8)
@@ -81,6 +83,7 @@ def tile_list_tiert_xdl_silu_kernel(
         diagonal = tile("diagonal", [P, P * PACK + PACK], BF16)
         b_rows = tile("b_rows", [P, P], F32)
         b_cols = keep.tile([P, TILES], F32, name="b_cols")
+        b_own = {0: tile("wtd_bf2", [P, 8], F32), 5: tile("wtd_bf3", [P, 8], F32)}
         table_warm = keep.tile([P, 8], F32, name="table_warm")
         x_bf, wtd_bf, rest_bf, got_w, got_s, back, sums = {}, {}, {}, {}, {}, {}, {}
         free_banks = []
@@ -159,7 +162,8 @@ def tile_list_tiert_xdl_silu_kernel(
             fp4_bytes = slice(2 * n * P, 2 * (n + 1) * P)
             c, lo = divmod(n * P, CHUNK)
             if term == "wt4":
-                w, w_s, a, a_s = wt4_w[:, fp4_bytes].bitcast(FP4X4), wt4_s[:, rows], got_w[h], got_s[h]
+                part, at = divmod(2 * n * P, N)
+                w, w_s, a, a_s = wt4_w[part][:, at : at + 2 * P].bitcast(FP4X4), wt4_s[:, rows], got_w[h], got_s[h]
             elif term == "wtd":
                 w, w_s, a, a_s = wtd_w[c][:, lo : lo + P].bitcast(FP8X4), wtd_s[c][:, lo : lo + P], got_w[h], got_s[h]
             elif term == "xq":
@@ -179,10 +183,11 @@ def tile_list_tiert_xdl_silu_kernel(
         def finish(n, h, first=0, width=HALF):
             acc, bank_index = sums[n, h]
             if h == 0 and n < HELD_RESULTS:
-                res = later.tile([P, width], F32, name="res%d" % n, align_bytes=ALIGN, offset=n * RESULT_BYTES)
+                pool = middle if n < 2 else later
+                res = pool.tile([P, width], F32, name="res%d" % n, align_bytes=ALIGN, offset=n % 2 * RESULT_BYTES)
             else:
                 res = results.tile([P, width], F32, name="res")
-            nc.scalar.activation(out=res[:], in_=acc[:, 0:width], func=SILU, bias=b_cols[:, n : n + 1])
+            nc.scalar.activation(out=res[:], in_=acc[:, 0:width], func=SILU, bias=b_own[n][:, 0:1] if h == 0 and n in b_own else b_cols[:, n : n + 1])
             j0 = h * HALF + first
             nc.sync.dma_start(out=out[n * P : (n + 1) * P, j0 : j0 + width], in_=res[:])
             free_banks.append(bank_index)
@@ -197,9 +202,10 @@ def tile_list_tiert_xdl_silu_kernel(
 
         last = PACK - 1
         nc.gpsimd.memset(diagonal[:].bitcast(I32), 0)
+        pairs = diagonal[:].bitcast(F32)
         nc.gpsimd.affine_select(
-            out=diagonal[:], in_=diagonal[:], pattern=[[1, P * PACK + PACK]], compare_op=mybir.AluOpType.not_equal,
-            fill=1.0, base=-last, channel_multiplier=-PACK,
+            out=pairs, in_=pairs, pattern=[[1, (P * PACK + PACK) // 2]], compare_op=mybir.AluOpType.not_equal,
+            fill=1.0, base=-1, channel_multiplier=-2,
         )
         make_identity(nc, eye_f32[:])
         last_eye = slice(last * P, PACK * P)
@@ -222,9 +228,10 @@ def tile_list_tiert_xdl_silu_kernel(
         nc.sync.dma_start(offsets[:], offs)
         load_scales(tab_s, tab_scales)
         nc.sync.dma_start(out=tab_w[:], in_=tab_words[0].rearrange("p n t -> p (n t)").bitcast(I32))
-        load_scales(wt4_s, wt4_scales)
-        nc.sync.dma_start(out=wt4_w[:].bitcast(I32), in_=wt4_words[0].bitcast(I32))
         load_chunk(wtd_raw, wtd_planes, 1)
+        load_scales(wt4_s, wt4_scales)
+        nc.sync.dma_start(out=wt4_w[0][:].bitcast(I32), in_=wt4_words[0][:, 0:N].bitcast(I32))
+        nc.sync.dma_start(out=wt4_w[1][:].bitcast(I32), in_=wt4_words[0][:, N : 2 * N].bitcast(I32))
         load_chunk(wtd_raw, wtd_planes, 2)
         load_chunk(x_raw, x_planes, 2)
         load_chunk(x_raw, x_planes, 3)
@@ -261,15 +268,15 @@ def tile_list_tiert_xdl_silu_kernel(
             dequantise(piece, PIECES + piece)
             if piece == PIECES - 2:
                 residual(0)
-        for piece in (1, 2):
+        for piece in (1, 2, 3):
             residual(piece)
         nc.scalar.copy(out=b_cols[:], in_=b_turned[:, 0:TILES])
+        for n in b_own:
+            nc.scalar.copy(out=b_own[n][:, 0:1], in_=b_turned[:, n : n + 1])
         for n in range(PIECES):
             product("xq", n, 0, opens_bank=n)
-        quantise_chunk(xr_w, xr_s, rest_bf, 0)
-        residual(PIECES - 1)
-        for piece in (2, 3):
-            quantise_piece(xr_w[0], xr_s[0], rest_bf[1][:, (piece - 2) * P : (piece - 1) * P, :], piece)
+        for c in (0, 1):
+            quantise_chunk(xr_w, xr_s, rest_bf, c)
         for n in range(PIECES, TILES):
             product("xq", n, 0, opens_bank=free_banks.pop(0))
         for n in range(TILES):
@@ -285,10 +292,8 @@ def tile_list_tiert_xdl_silu_kernel(
         gather(got_s[1], tab_s[:], 1)
         round_wtd(1, "wtd_bf1")
         quantise_chunk(wtd_w, wtd_s, wtd_bf, 1)
-        got_w[1] = tile("wtd_raw1", [P, HALF], U32)
+        got_w[1] = middle.tile([P, HALF], U32, name="got_w1", align_bytes=ALIGN, offset=2 * RESULT_BYTES)
         gather(got_w[1], tab_w[:].bitcast(U32), 1)
-        round_wtd(2, "wtd_bf2")
-        quantise_chunk(wtd_w, wtd_s, wtd_bf, 2)
 
         for n in (0, 1):
             product("wt4", n, 0)
@@ -298,9 +303,11 @@ def tile_list_tiert_xdl_silu_kernel(
             if n == SECOND_PAIR_AFTER:
                 close_pair(1)
         finish_pair(0)
+        round_wtd(2, "wtd_bf2")
         finish_pair(1)
 
         round_x(2)
+        quantise_chunk(wtd_w, wtd_s, wtd_bf, 2)
         quantise_chunk(xq_w, xq_s, x_bf, 2)
         for n in (0, 1):
             table_products(n)

@@ -1,7 +1,6 @@
 from contextlib import ExitStack
 
 import concourse.mybir as mybir
-from concourse.masks import make_identity
 
 K, L, N, T, J = 512, 512, 1024, 2048, 1024
 FLOPS = 4 * 2 * K * N * J + 2 * L * L * J
@@ -50,6 +49,7 @@ def tile_list_tiert_xdl_silu_kernel(
         keep = ctx.enter_context(tc.tile_pool(name="keep", bufs=1))
         shared = ctx.enter_context(tc.tile_pool(name="shared", bufs=1))
         early = ctx.enter_context(tc.tile_pool(name="early", bufs=1))
+        first_pool = ctx.enter_context(tc.tile_pool(name="first", bufs=1))
         later = ctx.enter_context(tc.tile_pool(name="later", bufs=1))
         middle = ctx.enter_context(tc.tile_pool(name="middle", bufs=1))
         results = ctx.enter_context(tc.tile_pool(name="results", bufs=RESULT_BUFS))
@@ -66,7 +66,7 @@ def tile_list_tiert_xdl_silu_kernel(
 
         offsets = keep.tile([P, J // 16], U16, name="offsets")
         tab_w, tab_s = tile("tab_w", [P, T], I32), tile("tab_s", [P, T], U8)
-        wt4_w, wt4_s = tiles("wt4_w", 2, [P, N], U8), tile("wt4_s", [P, N], U8)
+        wt4_w = tiles("wt4_w", 2, [P, N], U8)
         wx_w, wx_s = tile("wx_w", [P, 2 * N], U8), tile("wx_s", [P, N], U8)
         x_first = tiles("x_first", PIECES - 1, [P, PACK, P], F32)
         x_first.append(shared.tile([P, PACK, P], F32, name="x_first3", align_bytes=ALIGN, offset=RESULT_BYTES // 2))
@@ -80,7 +80,8 @@ def tile_list_tiert_xdl_silu_kernel(
         eye_w, eye_s = tile("eye_w", [P, PACK * P], U32), tile("eye_s", [P, PACK * P], U8)
         eye_f32 = keep.tile([P, P], F32, name="eye_f32")
         eye_bf = early.tile([P, PACK - 1, P * PACK], BF16, name="eye_bf", align_bytes=ALIGN, offset=0)
-        diagonal = tile("diagonal", [P, P * PACK + PACK], BF16)
+        diagonal = first_pool.tile([P, P * PACK + PACK], BF16, name="diagonal", align_bytes=ALIGN, offset=0)
+        wt4_s = first_pool.tile([P, N], U8, name="wt4_s", align_bytes=ALIGN, offset=PIECE_BYTES)
         b_rows = tile("b_rows", [P, P], F32)
         b_cols = keep.tile([P, TILES], F32, name="b_cols")
         b_own = {0: tile("wtd_bf2", [P, 8], F32), 5: tile("wtd_bf3", [P, 8], F32)}
@@ -201,21 +202,21 @@ def tile_list_tiert_xdl_silu_kernel(
                 finish(n, 0)
 
         last = PACK - 1
-        nc.gpsimd.memset(diagonal[:].bitcast(I32), 0)
+        nc.vector.memset(b_rows[:], 0.0)
+        nc.vector.memset(diagonal[:].bitcast(I32), 0)
         pairs = diagonal[:].bitcast(F32)
         nc.gpsimd.affine_select(
             out=pairs, in_=pairs, pattern=[[1, (P * PACK + PACK) // 2]], compare_op=mybir.AluOpType.not_equal,
             fill=1.0, base=-1, channel_multiplier=-2,
         )
-        make_identity(nc, eye_f32[:])
+        nc.scalar.copy(out=eye_f32[:], in_=diagonal[:, last : P * PACK : PACK])
         last_eye = slice(last * P, PACK * P)
         nc.vector.quantize_mx(out=eye_w[:, last_eye].bitcast(FP8X4), scales=eye_s[:, last_eye], in_=diagonal[:, 0 : P * PACK])
 
         nc.vector.memset(table_warm[:], 0.0)
         nc.scalar.activation(out=table_warm[:], in_=table_warm[:], func=SILU)
 
-        nc.vector.memset(b_rows[:], 0.0)
-        for plane in (wx_s, tab_s, wt4_s):
+        for plane in (wx_s, tab_s):
             nc.vector.memset(plane[:].bitcast(I32), 0)
 
         load_piece(0)
@@ -229,19 +230,24 @@ def tile_list_tiert_xdl_silu_kernel(
         load_scales(tab_s, tab_scales)
         nc.sync.dma_start(out=tab_w[:], in_=tab_words[0].rearrange("p n t -> p (n t)").bitcast(I32))
         load_chunk(wtd_raw, wtd_planes, 1)
-        load_scales(wt4_s, wt4_scales)
-        nc.sync.dma_start(out=wt4_w[0][:].bitcast(I32), in_=wt4_words[0][:, 0:N].bitcast(I32))
-        nc.sync.dma_start(out=wt4_w[1][:].bitcast(I32), in_=wt4_words[0][:, N : 2 * N].bitcast(I32))
-        load_chunk(wtd_raw, wtd_planes, 2)
-        load_chunk(x_raw, x_planes, 2)
-        load_chunk(x_raw, x_planes, 3)
-        load_chunk(wtd_raw, wtd_planes, 3)
+
+        def late_loads():
+            load_scales(wt4_s, wt4_scales)
+            nc.sync.dma_start(out=wt4_w[0][:].bitcast(I32), in_=wt4_words[0][:, 0:N].bitcast(I32))
+            nc.sync.dma_start(out=wt4_w[1][:].bitcast(I32), in_=wt4_words[0][:, N : 2 * N].bitcast(I32))
+            load_chunk(wtd_raw, wtd_planes, 2)
+            load_chunk(x_raw, x_planes, 2)
+            load_chunk(x_raw, x_planes, 3)
+            load_chunk(wtd_raw, wtd_planes, 3)
 
         for t in reversed(range(last)):
             nc.vector.tensor_copy(out=eye_bf[:, t, :], in_=diagonal[:, last - t : last - t + P * PACK])
-        for t in reversed(range(last)):
-            columns = slice(t * P, (t + 1) * P)
-            nc.vector.quantize_mx(out=eye_w[:, columns].bitcast(FP8X4), scales=eye_s[:, columns], in_=eye_bf[:, t, :])
+        for lo, hi in ((last - 1, last), (0, last - 1)):
+            columns = slice(lo * P, hi * P)
+            nc.vector.quantize_mx(
+                out=eye_w[:, columns].bitcast(FP8X4), scales=eye_s[:, columns],
+                in_=eye_bf[:, lo:hi, :].rearrange("p t c -> p (t c)"),
+            )
 
         idle = bank(WARM_BANK)
         for width in [P] * WARM_NARROW + [2 * P] * WARM_WIDE:
@@ -257,8 +263,11 @@ def tile_list_tiert_xdl_silu_kernel(
 
         for piece in range(PIECES):
             if piece % 2 == 0:
-                rounded = tile("diagonal", [P, P, PACK], BF16)
+                rounded = first_pool.tile([P, P, PACK], BF16, name="rounded%d" % piece, align_bytes=ALIGN, offset=0)
                 round_planes(nc.vector.tensor_copy, rounded, x_first[piece])
+                if piece == 0:
+                    nc.vector.memset(wt4_s[:].bitcast(I32), 0)
+                    late_loads()
             else:
                 rounded = early.tile(
                     [P, P, PACK], BF16, name="rounded%d" % piece, align_bytes=ALIGN, offset=(piece - 1) * PIECE_BYTES

@@ -27,7 +27,7 @@ RESULT_BUFS = 2 * TILES + 3
 HELD_RESULTS = 4
 SECOND_PAIR_AFTER = 5
 OPENED_EARLY = 5
-WARM_NARROW, WARM_WIDE = 4, 2
+WARM_NARROW, WARM_WIDE = 10, 0
 WARM_BANK = PIECES - 1
 RESULT_BYTES = 4 * HALF
 PIECE_BYTES = 2 * PACK * P
@@ -81,7 +81,7 @@ def tile_list_tiert_xdl_silu_kernel(
         eye_f32 = keep.tile([P, P], F32, name="eye_f32")
         eye_bf = early.tile([P, PACK - 1, P * PACK], BF16, name="eye_bf", align_bytes=ALIGN, offset=0)
         diagonal = first_pool.tile([P, P * PACK + PACK], BF16, name="diagonal", align_bytes=ALIGN, offset=0)
-        wt4_s = first_pool.tile([P, N], U8, name="wt4_s", align_bytes=ALIGN, offset=PIECE_BYTES)
+        wt4_s = tile("wt4_s", [P, N], U8)
         b_rows = tile("b_rows", [P, P], F32)
         b_cols = keep.tile([P, TILES], F32, name="b_cols")
         b_own = {0: tile("wtd_bf2", [P, 8], F32), 5: tile("wtd_bf3", [P, 8], F32)}
@@ -202,21 +202,20 @@ def tile_list_tiert_xdl_silu_kernel(
                 finish(n, 0)
 
         last = PACK - 1
-        nc.vector.memset(b_rows[:], 0.0)
-        nc.vector.memset(diagonal[:].bitcast(I32), 0)
+        nc.gpsimd.memset(b_rows[:], 0.0)
+        nc.gpsimd.memset(diagonal[:].bitcast(I32), 0)
         pairs = diagonal[:].bitcast(F32)
         nc.gpsimd.affine_select(
             out=pairs, in_=pairs, pattern=[[1, (P * PACK + PACK) // 2]], compare_op=mybir.AluOpType.not_equal,
             fill=1.0, base=-1, channel_multiplier=-2,
         )
-        nc.scalar.copy(out=eye_f32[:], in_=diagonal[:, last : P * PACK : PACK])
         last_eye = slice(last * P, PACK * P)
         nc.vector.quantize_mx(out=eye_w[:, last_eye].bitcast(FP8X4), scales=eye_s[:, last_eye], in_=diagonal[:, 0 : P * PACK])
 
         nc.vector.memset(table_warm[:], 0.0)
         nc.scalar.activation(out=table_warm[:], in_=table_warm[:], func=SILU)
 
-        for plane in (wx_s, tab_s):
+        for plane in (wx_s, tab_s, wt4_s):
             nc.vector.memset(plane[:].bitcast(I32), 0)
 
         load_piece(0)
@@ -230,19 +229,22 @@ def tile_list_tiert_xdl_silu_kernel(
         load_scales(tab_s, tab_scales)
         nc.sync.dma_start(out=tab_w[:], in_=tab_words[0].rearrange("p n t -> p (n t)").bitcast(I32))
         load_chunk(wtd_raw, wtd_planes, 1)
+        load_scales(wt4_s, wt4_scales)
+        nc.sync.dma_start(out=wt4_w[0][:].bitcast(I32), in_=wt4_words[0][:, 0:N].bitcast(I32))
+        nc.sync.dma_start(out=wt4_w[1][:].bitcast(I32), in_=wt4_words[0][:, N : 2 * N].bitcast(I32))
+        load_chunk(wtd_raw, wtd_planes, 2)
+        load_chunk(x_raw, x_planes, 2)
+        load_chunk(x_raw, x_planes, 3)
+        load_chunk(wtd_raw, wtd_planes, 3)
 
-        def late_loads():
-            load_scales(wt4_s, wt4_scales)
-            nc.sync.dma_start(out=wt4_w[0][:].bitcast(I32), in_=wt4_words[0][:, 0:N].bitcast(I32))
-            nc.sync.dma_start(out=wt4_w[1][:].bitcast(I32), in_=wt4_words[0][:, N : 2 * N].bitcast(I32))
-            load_chunk(wtd_raw, wtd_planes, 2)
-            load_chunk(x_raw, x_planes, 2)
-            load_chunk(x_raw, x_planes, 3)
-            load_chunk(wtd_raw, wtd_planes, 3)
-
-        for t in reversed(range(last)):
+        for t in (2, 1):
             nc.vector.tensor_copy(out=eye_bf[:, t, :], in_=diagonal[:, last - t : last - t + P * PACK])
-        for lo, hi in ((last - 1, last), (0, last - 1)):
+        eye_row = eye_bf[:].rearrange("p t c -> p (t c)")
+        nc.scalar.copy(out=eye_bf[:, 0, :], in_=eye_row[:, P * PACK + 1 : 2 * P * PACK + 1])
+        nc.scalar.copy(out=eye_f32[:], in_=eye_bf[:, 2, 2 : P * PACK : PACK])
+        rounded = {0: first_pool.tile([P, P, PACK], BF16, name="rounded0", align_bytes=ALIGN, offset=0)}
+        round_planes(nc.vector.tensor_copy, rounded[0], x_first[0])
+        for lo, hi in ((1, last), (0, 1)):
             columns = slice(lo * P, hi * P)
             nc.vector.quantize_mx(
                 out=eye_w[:, columns].bitcast(FP8X4), scales=eye_s[:, columns],
@@ -262,20 +264,18 @@ def tile_list_tiert_xdl_silu_kernel(
         nc.tensor.transpose(b_turned[:, 0:P], b_rows[:], eye_f32[:])
 
         for piece in range(PIECES):
-            if piece % 2 == 0:
-                rounded = first_pool.tile([P, P, PACK], BF16, name="rounded%d" % piece, align_bytes=ALIGN, offset=0)
-                round_planes(nc.vector.tensor_copy, rounded, x_first[piece])
-                if piece == 0:
-                    nc.vector.memset(wt4_s[:].bitcast(I32), 0)
-                    late_loads()
-            else:
-                rounded = early.tile(
-                    [P, P, PACK], BF16, name="rounded%d" % piece, align_bytes=ALIGN, offset=(piece - 1) * PIECE_BYTES
-                )
-                round_planes(nc.scalar.copy, rounded, x_first[piece])
-            quantise_piece(xq_w[0], xq_s[0], rounded[:], piece)
+            if piece == 1:
+                rounded[1] = first_pool.tile([P, P, PACK], BF16, name="rounded1", align_bytes=ALIGN, offset=PIECE_BYTES)
+                round_planes(nc.scalar.copy, rounded[1], x_first[1])
+            elif piece == 2:
+                rounded[2] = first_pool.tile([P, P, PACK], BF16, name="rounded2", align_bytes=ALIGN, offset=0)
+                round_planes(nc.vector.tensor_copy, rounded[2], x_first[2])
+            elif piece == 3:
+                rounded[3] = early.tile([P, P, PACK], BF16, name="rounded3", align_bytes=ALIGN, offset=0)
+                round_planes(nc.scalar.copy, rounded[3], x_first[3])
+            quantise_piece(xq_w[0], xq_s[0], rounded[piece][:], piece)
             dequantise(piece, PIECES + piece)
-            if piece == PIECES - 2:
+            if piece == 1:
                 residual(0)
         for piece in (1, 2, 3):
             residual(piece)

@@ -25,9 +25,10 @@ RUN = 2
 ALIGN = 256
 RESULT_BUFS = 2 * TILES + 3
 HELD_RESULTS = 4
+SPLIT_CHUNK = 1
 SECOND_PAIR_AFTER = 5
 OPENED_EARLY = 5
-WARM_NARROW, WARM_WIDE = 10, 0
+WARM_PASSES = 10
 WARM_BANK = PIECES - 1
 RESULT_BYTES = 4 * HALF
 PIECE_BYTES = 2 * PACK * P
@@ -48,10 +49,10 @@ def tile_list_tiert_xdl_silu_kernel(
     with ExitStack() as ctx:
         keep = ctx.enter_context(tc.tile_pool(name="keep", bufs=1))
         shared = ctx.enter_context(tc.tile_pool(name="shared", bufs=1))
-        early = ctx.enter_context(tc.tile_pool(name="early", bufs=1))
-        first_pool = ctx.enter_context(tc.tile_pool(name="first", bufs=1))
-        later = ctx.enter_context(tc.tile_pool(name="later", bufs=1))
-        middle = ctx.enter_context(tc.tile_pool(name="middle", bufs=1))
+        on_eyes = ctx.enter_context(tc.tile_pool(name="on_eyes", bufs=1))
+        on_diagonal = ctx.enter_context(tc.tile_pool(name="on_diagonal", bufs=1))
+        on_chunk2 = ctx.enter_context(tc.tile_pool(name="on_chunk2", bufs=1))
+        on_chunk1 = ctx.enter_context(tc.tile_pool(name="on_chunk1", bufs=1))
         results = ctx.enter_context(tc.tile_pool(name="results", bufs=RESULT_BUFS))
         psum = ctx.enter_context(tc.psum_pool(name="psum", bufs=1))
 
@@ -61,32 +62,37 @@ def tile_list_tiert_xdl_silu_kernel(
         def tile(name, shape, dtype):
             return keep.tile(shape, dtype, name=name, align_bytes=ALIGN)
 
+        def placed(pool, name, shape, dtype, offset):
+            return pool.tile(shape, dtype, name=name, align_bytes=ALIGN, offset=offset)
+
         def tiles(name, count, shape, dtype):
             return [tile("%s%d" % (name, i), shape, dtype) for i in range(count)]
 
         offsets = keep.tile([P, J // 16], U16, name="offsets")
         tab_w, tab_s = tile("tab_w", [P, T], I32), tile("tab_s", [P, T], U8)
-        wt4_w = tiles("wt4_w", 2, [P, N], U8)
+        wt4_w, wt4_s = tiles("wt4_w", 2, [P, N], U8), tile("wt4_s", [P, N], U8)
         wx_w, wx_s = tile("wx_w", [P, 2 * N], U8), tile("wx_s", [P, N], U8)
         x_first = tiles("x_first", PIECES - 1, [P, PACK, P], F32)
-        x_first.append(shared.tile([P, PACK, P], F32, name="x_first3", align_bytes=ALIGN, offset=RESULT_BYTES // 2))
+        x_first.append(placed(shared, "x_first3", [P, PACK, P], F32, RESULT_BYTES // 2))
         x_raw = {c: tile("x_raw%d" % c, [P, PACK, CHUNK], F32) for c in (2, 3)}
         wtd_raw = {c: tile("wtd_raw%d" % c, [P, PACK, CHUNK], F32) for c in (0, 3)}
-        wtd_raw[1] = middle.tile([P, PACK + 2, CHUNK], F32, name="wtd_raw1", align_bytes=ALIGN, offset=0)[:, 0:PACK, :]
-        wtd_raw[2] = later.tile([P, PACK, CHUNK], F32, name="wtd_raw2", align_bytes=ALIGN, offset=0)
+        wtd_part = [
+            placed(on_chunk1, "wtd_part0", [P, PACK, P], F32, 0),
+            placed(on_chunk1, "wtd_part1", [P, 2 * PACK, P], F32, RESULT_BYTES)[:, 0:PACK, :],
+        ]
+        wtd_raw[2] = placed(on_chunk2, "wtd_raw2", [P, PACK, CHUNK], F32, 0)
         xq_w, xq_s = tiles("xq_w", 2, [P, HALF], U32), tiles("xq_s", 2, [P, HALF], U8)
         xr_w, xr_s = tiles("xr_w", 2, [P, HALF], U32), tiles("xr_s", 2, [P, HALF], U8)
         wtd_w, wtd_s = tiles("wtd_w", N // CHUNK, [P, CHUNK], U32), tiles("wtd_s", N // CHUNK, [P, CHUNK], U8)
         eye_w, eye_s = tile("eye_w", [P, PACK * P], U32), tile("eye_s", [P, PACK * P], U8)
         eye_f32 = keep.tile([P, P], F32, name="eye_f32")
-        eye_bf = early.tile([P, PACK - 1, P * PACK], BF16, name="eye_bf", align_bytes=ALIGN, offset=0)
-        diagonal = first_pool.tile([P, P * PACK + PACK], BF16, name="diagonal", align_bytes=ALIGN, offset=0)
-        wt4_s = tile("wt4_s", [P, N], U8)
+        eye_bf = placed(on_eyes, "eye_bf", [P, PACK - 1, P * PACK], BF16, 0)
+        diagonal = placed(on_diagonal, "diagonal", [P, P * PACK + PACK], BF16, 0)
         b_rows = tile("b_rows", [P, P], F32)
         b_cols = keep.tile([P, TILES], F32, name="b_cols")
-        b_own = {0: tile("wtd_bf2", [P, 8], F32), 5: tile("wtd_bf3", [P, 8], F32)}
+        b_first = tile("wtd_bf2", [P, TILES], F32)
         table_warm = keep.tile([P, 8], F32, name="table_warm")
-        x_bf, wtd_bf, rest_bf, got_w, got_s, back, sums = {}, {}, {}, {}, {}, {}, {}
+        rounded, x_bf, wtd_bf, rest_bf, got_w, got_s, back, sums = {}, {}, {}, {}, {}, {}, {}, {}
         free_banks = []
 
         x_planes = x.rearrange("(p t) j -> p t j", t=PACK)
@@ -100,7 +106,11 @@ def tile_list_tiert_xdl_silu_kernel(
             nc.sync.dma_start(out=raw[c][:], in_=planes[:, :, c * CHUNK : (c + 1) * CHUNK])
 
         def round_planes(copy, dst, src):
-            copy(out=packed_by_runs(dst[:]), in_=planes_by_runs(src[:]))
+            copy(out=packed_by_runs(dst[:, :, :]), in_=planes_by_runs(src[:, :, :]))
+
+        def round_piece(piece, copy, pool, offset):
+            rounded[piece] = placed(pool, "rounded%d" % piece, [P, P, PACK], BF16, offset)
+            round_planes(copy, rounded[piece], x_first[piece])
 
         def round_x(c):
             x_bf[c] = tile("x_bf%d" % c, [P, CHUNK, PACK], BF16)
@@ -118,10 +128,11 @@ def tile_list_tiert_xdl_silu_kernel(
                 in_=src[c][:].rearrange("p c t -> p (c t)"),
             )
 
-        def quantise_piece(words, scales, src, piece):
+        def quantise_piece(piece):
             columns = slice(piece * P, (piece + 1) * P)
             nc.vector.quantize_mx(
-                out=words[:, columns].bitcast(FP8X4), scales=scales[:, columns], in_=src.rearrange("p c t -> p (c t)")
+                out=xq_w[0][:, columns].bitcast(FP8X4), scales=xq_s[0][:, columns],
+                in_=rounded[piece][:].rearrange("p c t -> p (c t)"),
             )
 
         def load_piece(piece):
@@ -142,7 +153,7 @@ def tile_list_tiert_xdl_silu_kernel(
         def residual(piece):
             c, lo = divmod(piece * P, CHUNK)
             if lo == 0:
-                rest_bf[c] = tile("rest_bf%d" % c, [P, CHUNK, PACK], BF16)
+                rest_bf[c] = tile("x_bf3" if piece == PIECES else "rest_bf%d" % c, [P, CHUNK, PACK], BF16)
             values, bank_index = back[piece]
             nc.vector.tensor_tensor(
                 out=packed_by_runs(rest_bf[c][:, lo : lo + P, :]),
@@ -184,11 +195,11 @@ def tile_list_tiert_xdl_silu_kernel(
         def finish(n, h, first=0, width=HALF):
             acc, bank_index = sums[n, h]
             if h == 0 and n < HELD_RESULTS:
-                pool = middle if n < 2 else later
-                res = pool.tile([P, width], F32, name="res%d" % n, align_bytes=ALIGN, offset=n % 2 * RESULT_BYTES)
+                res = placed((on_chunk1, on_chunk2)[n // 2], "res%d" % n, [P, width], F32, n % 2 * RESULT_BYTES)
             else:
                 res = results.tile([P, width], F32, name="res")
-            nc.scalar.activation(out=res[:], in_=acc[:, 0:width], func=SILU, bias=b_own[n][:, 0:1] if h == 0 and n in b_own else b_cols[:, n : n + 1])
+            bias = b_first[:, 0:1] if (n, h) == (0, 0) else b_cols[:, n : n + 1]
+            nc.scalar.activation(out=res[:], in_=acc[:, 0:width], func=SILU, bias=bias)
             j0 = h * HALF + first
             nc.sync.dma_start(out=out[n * P : (n + 1) * P, j0 : j0 + width], in_=res[:])
             free_banks.append(bank_index)
@@ -201,8 +212,9 @@ def tile_list_tiert_xdl_silu_kernel(
             for n in (2 * c, 2 * c + 1):
                 finish(n, 0)
 
-        last = PACK - 1
         nc.gpsimd.memset(b_rows[:], 0.0)
+
+        last = PACK - 1
         nc.gpsimd.memset(diagonal[:].bitcast(I32), 0)
         pairs = diagonal[:].bitcast(F32)
         nc.gpsimd.affine_select(
@@ -210,7 +222,9 @@ def tile_list_tiert_xdl_silu_kernel(
             fill=1.0, base=-1, channel_multiplier=-2,
         )
         last_eye = slice(last * P, PACK * P)
-        nc.vector.quantize_mx(out=eye_w[:, last_eye].bitcast(FP8X4), scales=eye_s[:, last_eye], in_=diagonal[:, 0 : P * PACK])
+        nc.vector.quantize_mx(
+            out=eye_w[:, last_eye].bitcast(FP8X4), scales=eye_s[:, last_eye], in_=diagonal[:, 0 : P * PACK]
+        )
 
         nc.vector.memset(table_warm[:], 0.0)
         nc.scalar.activation(out=table_warm[:], in_=table_warm[:], func=SILU)
@@ -228,10 +242,13 @@ def tile_list_tiert_xdl_silu_kernel(
         nc.sync.dma_start(offsets[:], offs)
         load_scales(tab_s, tab_scales)
         nc.sync.dma_start(out=tab_w[:], in_=tab_words[0].rearrange("p n t -> p (n t)").bitcast(I32))
-        load_chunk(wtd_raw, wtd_planes, 1)
-        load_scales(wt4_s, wt4_scales)
-        nc.sync.dma_start(out=wt4_w[0][:].bitcast(I32), in_=wt4_words[0][:, 0:N].bitcast(I32))
-        nc.sync.dma_start(out=wt4_w[1][:].bitcast(I32), in_=wt4_words[0][:, N : 2 * N].bitcast(I32))
+        for part in range(2):
+            lo = SPLIT_CHUNK * CHUNK + part * P
+            nc.sync.dma_start(out=wtd_part[part][:], in_=wtd_planes[:, :, lo : lo + P])
+            if part == 0:
+                load_scales(wt4_s, wt4_scales)
+            words = wt4_words[0][:, part * N : (part + 1) * N]
+            nc.sync.dma_start(out=wt4_w[part][:].bitcast(I32), in_=words.bitcast(I32))
         load_chunk(wtd_raw, wtd_planes, 2)
         load_chunk(x_raw, x_planes, 2)
         load_chunk(x_raw, x_planes, 3)
@@ -242,8 +259,7 @@ def tile_list_tiert_xdl_silu_kernel(
         eye_row = eye_bf[:].rearrange("p t c -> p (t c)")
         nc.scalar.copy(out=eye_bf[:, 0, :], in_=eye_row[:, P * PACK + 1 : 2 * P * PACK + 1])
         nc.scalar.copy(out=eye_f32[:], in_=eye_bf[:, 2, 2 : P * PACK : PACK])
-        rounded = {0: first_pool.tile([P, P, PACK], BF16, name="rounded0", align_bytes=ALIGN, offset=0)}
-        round_planes(nc.vector.tensor_copy, rounded[0], x_first[0])
+        round_piece(0, nc.vector.tensor_copy, on_diagonal, 0)
         for lo, hi in ((1, last), (0, 1)):
             columns = slice(lo * P, hi * P)
             nc.vector.quantize_mx(
@@ -252,36 +268,33 @@ def tile_list_tiert_xdl_silu_kernel(
             )
 
         idle = bank(WARM_BANK)
-        for width in [P] * WARM_NARROW + [2 * P] * WARM_WIDE:
+        for warm_pass in range(WARM_PASSES):
             nc.tensor.matmul_mx(
-                out=idle[:, 0:width],
+                out=idle[:, 0:P],
                 lhsT=eye_w[:, last_eye].bitcast(FP8X4), lhsT_scale=eye_s[:, last_eye],
-                rhs=eye_w[:, PACK * P - width :].bitcast(FP8X4), rhs_scale=eye_s[:, PACK * P - width :],
+                rhs=eye_w[:, last_eye].bitcast(FP8X4), rhs_scale=eye_s[:, last_eye],
                 start=True, stop=True,
             )
 
         b_turned = bank(WARM_BANK)
         nc.tensor.transpose(b_turned[:, 0:P], b_rows[:], eye_f32[:])
 
+        later_pieces = {
+            1: (nc.scalar.copy, on_diagonal, PIECE_BYTES),
+            2: (nc.vector.tensor_copy, on_diagonal, 0),
+            3: (nc.scalar.copy, on_eyes, 0),
+        }
         for piece in range(PIECES):
-            if piece == 1:
-                rounded[1] = first_pool.tile([P, P, PACK], BF16, name="rounded1", align_bytes=ALIGN, offset=PIECE_BYTES)
-                round_planes(nc.scalar.copy, rounded[1], x_first[1])
-            elif piece == 2:
-                rounded[2] = first_pool.tile([P, P, PACK], BF16, name="rounded2", align_bytes=ALIGN, offset=0)
-                round_planes(nc.vector.tensor_copy, rounded[2], x_first[2])
-            elif piece == 3:
-                rounded[3] = early.tile([P, P, PACK], BF16, name="rounded3", align_bytes=ALIGN, offset=0)
-                round_planes(nc.scalar.copy, rounded[3], x_first[3])
-            quantise_piece(xq_w[0], xq_s[0], rounded[piece][:], piece)
+            if piece in later_pieces:
+                round_piece(piece, *later_pieces[piece])
+            quantise_piece(piece)
             dequantise(piece, PIECES + piece)
             if piece == 1:
                 residual(0)
-        for piece in (1, 2, 3):
+        for piece in range(1, PIECES):
             residual(piece)
         nc.scalar.copy(out=b_cols[:], in_=b_turned[:, 0:TILES])
-        for n in b_own:
-            nc.scalar.copy(out=b_own[n][:, 0:1], in_=b_turned[:, n : n + 1])
+        nc.scalar.copy(out=b_first[:, 0:1], in_=b_turned[:, 0:1])
         for n in range(PIECES):
             product("xq", n, 0, opens_bank=n)
         for c in (0, 1):
@@ -291,17 +304,19 @@ def tile_list_tiert_xdl_silu_kernel(
         for n in range(TILES):
             product("xr", n, 0)
 
-        got_s[0] = shared.tile([P, HALF], U8, name="got_s0", align_bytes=ALIGN, offset=RESULT_BYTES)
+        got_s[0] = placed(shared, "got_s0", [P, HALF], U8, RESULT_BYTES)
         gather(got_s[0], tab_s[:], 0)
-        got_w[0] = shared.tile([P, HALF], U32, name="got_w0", align_bytes=ALIGN, offset=0)
+        got_w[0] = placed(shared, "got_w0", [P, HALF], U32, 0)
         gather(got_w[0], tab_w[:].bitcast(U32), 0)
         round_wtd(0, "rest_bf0")
         quantise_chunk(wtd_w, wtd_s, wtd_bf, 0)
         got_s[1] = tile("wtd_raw0", [P, HALF], U8)
         gather(got_s[1], tab_s[:], 1)
-        round_wtd(1, "wtd_bf1")
-        quantise_chunk(wtd_w, wtd_s, wtd_bf, 1)
-        got_w[1] = middle.tile([P, HALF], U32, name="got_w1", align_bytes=ALIGN, offset=2 * RESULT_BYTES)
+        wtd_bf[SPLIT_CHUNK] = tile("wtd_bf1", [P, CHUNK, PACK], BF16)
+        for part in range(2):
+            round_planes(nc.scalar.copy, wtd_bf[SPLIT_CHUNK][:, part * P : (part + 1) * P, :], wtd_part[part])
+        quantise_chunk(wtd_w, wtd_s, wtd_bf, SPLIT_CHUNK)
+        got_w[1] = placed(on_chunk1, "got_w1", [P, HALF], U32, 2 * RESULT_BYTES)
         gather(got_w[1], tab_w[:].bitcast(U32), 1)
 
         for n in (0, 1):
@@ -335,15 +350,15 @@ def tile_list_tiert_xdl_silu_kernel(
             dequantise(piece, free_banks.pop(0))
         residual(PIECES + 2)
         quantise_chunk(wtd_w, wtd_s, wtd_bf, 3)
-        quantise_chunk(xr_w, xr_s, rest_bf, 2)
+        residual(PIECES + 3)
+        for c in (2, 3):
+            quantise_chunk(xr_w, xr_s, rest_bf, c)
         for n in (2, 3):
             table_products(n)
             product("xq", n, 1)
         close_pair(3)
         table_products(OPENED_EARLY - 1)
         product("xq", OPENED_EARLY - 1, 1)
-        residual(PIECES + 3)
-        quantise_chunk(xr_w, xr_s, rest_bf, 3)
         finish_pair(3)
 
         for n in range(TILES - 1):

@@ -23,11 +23,8 @@ TILES = N // P
 PIECES = HALF // P
 RUN = 2
 ALIGN = 256
-RESULT_BUFS = 2 * TILES + 3
-HELD_RESULTS = 4
-SPLIT_CHUNK = 1
-SECOND_PAIR_AFTER = 5
-OPENED_EARLY = 5
+RESULT_BUFS = 20
+SPLIT_TILES = 4
 WARM_PASSES = 10
 WARM_BANK = PIECES - 1
 RESULT_BYTES = 4 * HALF
@@ -51,8 +48,10 @@ def tile_list_tiert_xdl_silu_kernel(
         shared = ctx.enter_context(tc.tile_pool(name="shared", bufs=1))
         on_eyes = ctx.enter_context(tc.tile_pool(name="on_eyes", bufs=1))
         on_diagonal = ctx.enter_context(tc.tile_pool(name="on_diagonal", bufs=1))
-        on_chunk2 = ctx.enter_context(tc.tile_pool(name="on_chunk2", bufs=1))
+        on_part1 = ctx.enter_context(tc.tile_pool(name="on_part1", bufs=1))
         on_chunk1 = ctx.enter_context(tc.tile_pool(name="on_chunk1", bufs=1))
+        on_chunk3 = ctx.enter_context(tc.tile_pool(name="on_chunk3", bufs=1))
+        on_last = ctx.enter_context(tc.tile_pool(name="on_last", bufs=1))
         results = ctx.enter_context(tc.tile_pool(name="results", bufs=RESULT_BUFS))
         psum = ctx.enter_context(tc.psum_pool(name="psum", bufs=1))
 
@@ -73,14 +72,12 @@ def tile_list_tiert_xdl_silu_kernel(
         wt4_w, wt4_s = tiles("wt4_w", 2, [P, N], U8), tile("wt4_s", [P, N], U8)
         wx_w, wx_s = tile("wx_w", [P, 2 * N], U8), tile("wx_s", [P, N], U8)
         x_first = tiles("x_first", PIECES - 1, [P, PACK, P], F32)
-        x_first.append(placed(shared, "x_first3", [P, PACK, P], F32, RESULT_BYTES // 2))
+        x_first.append(placed(shared, "x_first3", [P, PACK, P], F32, RESULT_BYTES))
         x_raw = {c: tile("x_raw%d" % c, [P, PACK, CHUNK], F32) for c in (2, 3)}
-        wtd_raw = {c: tile("wtd_raw%d" % c, [P, PACK, CHUNK], F32) for c in (0, 3)}
-        wtd_part = [
-            placed(on_chunk1, "wtd_part0", [P, PACK, P], F32, 0),
-            placed(on_chunk1, "wtd_part1", [P, 2 * PACK, P], F32, RESULT_BYTES)[:, 0:PACK, :],
-        ]
-        wtd_raw[2] = placed(on_chunk2, "wtd_raw2", [P, PACK, CHUNK], F32, 0)
+        wtd_part = [placed(shared, "wtd_part0", [P, PACK, P], F32, 0), placed(on_part1, "wtd_part1", [P, PACK, P], F32, 0)]
+        wtd_raw = {2: tile("wtd_raw2", [P, PACK, CHUNK], F32)}
+        wtd_raw[3] = placed(on_chunk3, "wtd_raw3", [P, PACK, CHUNK], F32, RESULT_BYTES // 2)
+        wtd_raw[1] = placed(on_chunk1, "wtd_raw1", [P, PACK, CHUNK], F32, 0)
         xq_w, xq_s = tiles("xq_w", 2, [P, HALF], U32), tiles("xq_s", 2, [P, HALF], U8)
         xr_w, xr_s = tiles("xr_w", 2, [P, HALF], U32), tiles("xr_s", 2, [P, HALF], U8)
         wtd_w, wtd_s = tiles("wtd_w", N // CHUNK, [P, CHUNK], U32), tiles("wtd_s", N // CHUNK, [P, CHUNK], U8)
@@ -90,7 +87,6 @@ def tile_list_tiert_xdl_silu_kernel(
         diagonal = placed(on_diagonal, "diagonal", [P, P * PACK + PACK], BF16, 0)
         b_rows = tile("b_rows", [P, P], F32)
         b_cols = keep.tile([P, TILES], F32, name="b_cols")
-        b_first = tile("wtd_bf2", [P, TILES], F32)
         table_warm = keep.tile([P, 8], F32, name="table_warm")
         rounded, x_bf, wtd_bf, rest_bf, got_w, got_s, back, sums = {}, {}, {}, {}, {}, {}, {}, {}
         free_banks = []
@@ -105,38 +101,35 @@ def tile_list_tiert_xdl_silu_kernel(
         def load_chunk(raw, planes, c):
             nc.sync.dma_start(out=raw[c][:], in_=planes[:, :, c * CHUNK : (c + 1) * CHUNK])
 
+        def load_part(part):
+            nc.sync.dma_start(out=wtd_part[part][:], in_=wtd_planes[:, :, part * P : (part + 1) * P])
+
+        def load_wt4(part):
+            words = wt4_words[0][:, part * N : (part + 1) * N]
+            nc.sync.dma_start(out=wt4_w[part][:].bitcast(I32), in_=words.bitcast(I32))
+
         def round_planes(copy, dst, src):
             copy(out=packed_by_runs(dst[:, :, :]), in_=planes_by_runs(src[:, :, :]))
 
+        def raw_piece(piece):
+            c, lo = divmod(piece * P, CHUNK)
+            return x_first[piece][:] if piece < PIECES else x_raw[c][:, :, lo : lo + P]
+
         def round_piece(piece, copy, pool, offset):
             rounded[piece] = placed(pool, "rounded%d" % piece, [P, P, PACK], BF16, offset)
-            round_planes(copy, rounded[piece], x_first[piece])
+            round_planes(copy, rounded[piece], raw_piece(piece))
 
-        def round_x(c):
-            x_bf[c] = tile("x_bf%d" % c, [P, CHUNK, PACK], BF16)
-            round_planes(nc.vector.tensor_copy, x_bf[c], x_raw[c])
+        def round_chunk(copy, dst, raw, name, c):
+            dst[c] = tile("%s%d" % (name, c), [P, CHUNK, PACK], BF16)
+            round_planes(copy, dst[c], raw[c])
 
-        def round_wtd(c, buffer):
-            wtd_bf[c] = tile(buffer, [P, CHUNK, PACK], BF16)
-            round_planes(nc.scalar.copy, wtd_bf[c], wtd_raw[c])
-
-        def quantise_chunk(words, scales, src, c):
-            i, lo = divmod(c * CHUNK, words[0].shape[1])
+        def quantise(words, scales, first, src):
+            i, lo = divmod(first, words[0].shape[1])
+            columns = slice(lo, lo + src.shape[1])
             nc.vector.quantize_mx(
-                out=words[i][:, lo : lo + CHUNK].bitcast(FP8X4),
-                scales=scales[i][:, lo : lo + CHUNK],
-                in_=src[c][:].rearrange("p c t -> p (c t)"),
+                out=words[i][:, columns].bitcast(FP8X4), scales=scales[i][:, columns],
+                in_=src[:].rearrange("p c t -> p (c t)"),
             )
-
-        def quantise_piece(piece):
-            columns = slice(piece * P, (piece + 1) * P)
-            nc.vector.quantize_mx(
-                out=xq_w[0][:, columns].bitcast(FP8X4), scales=xq_s[0][:, columns],
-                in_=rounded[piece][:].rearrange("p c t -> p (c t)"),
-            )
-
-        def load_piece(piece):
-            nc.sync.dma_start(out=x_first[piece][:], in_=x_planes[:, :, piece * P : (piece + 1) * P])
 
         def dequantise(piece, bank_index):
             h, lo = divmod(piece * P, HALF)
@@ -152,68 +145,71 @@ def tile_list_tiert_xdl_silu_kernel(
 
         def residual(piece):
             c, lo = divmod(piece * P, CHUNK)
-            if lo == 0:
-                rest_bf[c] = tile("x_bf3" if piece == PIECES else "rest_bf%d" % c, [P, CHUNK, PACK], BF16)
+            if c not in rest_bf:
+                rest_bf[c] = tile("rest_bf%d" % c, [P, CHUNK, PACK], BF16)
             values, bank_index = back[piece]
             nc.vector.tensor_tensor(
                 out=packed_by_runs(rest_bf[c][:, lo : lo + P, :]),
-                in0=planes_by_runs(x_first[piece][:] if piece < PIECES else x_raw[c][:, :, lo : lo + P]),
+                in0=planes_by_runs(raw_piece(piece)),
                 in1=values[:].rearrange("p (t c i) -> p c t i", t=PACK, i=RUN),
                 op=mybir.AluOpType.subtract,
             )
             free_banks.append(bank_index)
 
-        def gather(dst, table, h):
-            entries = offsets[:, h * (HALF // 16) : (h + 1) * (HALF // 16)]
-            nc.vector.tensor_copy(out=dst[:], in_=table.indirect(entries))
+        def gather(dst, table, j0):
+            entries = offsets[:, j0 // 16 : (j0 + dst.shape[1]) // 16]
+            nc.vector.tensor_copy(out=dst, in_=table.indirect(entries))
 
-        def product(term, n, h, opens_bank=None, closes=False, first=0, width=HALF):
+        def products(terms, block, opens_bank=None, closes=False, part=None):
+            n0, count, j0, width = block
             if opens_bank is not None:
-                sums[n, h] = (bank(opens_bank), opens_bank)
-            rows = slice(n * P, (n + 1) * P)
-            fp4_bytes = slice(2 * n * P, 2 * (n + 1) * P)
-            c, lo = divmod(n * P, CHUNK)
-            if term == "wt4":
-                part, at = divmod(2 * n * P, N)
-                w, w_s, a, a_s = wt4_w[part][:, at : at + 2 * P].bitcast(FP4X4), wt4_s[:, rows], got_w[h], got_s[h]
-            elif term == "wtd":
-                w, w_s, a, a_s = wtd_w[c][:, lo : lo + P].bitcast(FP8X4), wtd_s[c][:, lo : lo + P], got_w[h], got_s[h]
-            elif term == "xq":
-                w, w_s, a, a_s = wx_w[:, fp4_bytes].bitcast(FP4X4), wx_s[:, rows], xq_w[h], xq_s[h]
-            else:
-                w, w_s, a, a_s = wx_w[:, fp4_bytes].bitcast(FP4X4), wx_s[:, rows], xr_w[h], xr_s[h]
-            nc.tensor.matmul_mx(
-                out=sums[n, h][0][:, 0:width], lhsT=w, lhsT_scale=w_s,
-                rhs=a[:, first : first + width].bitcast(FP8X4), rhs_scale=a_s[:, first : first + width],
-                start=opens_bank is not None, stop=closes,
-            )
+                sums[block] = (bank(opens_bank), opens_bank)
+            skip, span = part if part else (0, width)
+            h, x_first_token = divmod(j0 + skip, HALF)
+            run = max(r for r in got_w if r <= j0 + skip) if terms[0] in table_terms else 0
+            scale_first = x_first_token
+            passes = [(term, n) for term in terms for n in range(n0, n0 + count)]
+            for i, (term, n) in enumerate(passes):
+                rows = slice(n * P, (n + 1) * P)
+                fp4_bytes = slice(2 * n * P, 2 * (n + 1) * P)
+                c, lo = divmod(n * P, CHUNK)
+                if term == "wt4":
+                    half, at = divmod(2 * n * P, N)
+                    w, w_s, a, a_s = wt4_w[half][:, at : at + 2 * P].bitcast(FP4X4), wt4_s[:, rows], got_w[run], got_s[h * HALF]
+                elif term == "wtd":
+                    w, w_s, a, a_s = wtd_w[c][:, lo : lo + P].bitcast(FP8X4), wtd_s[c][:, lo : lo + P], got_w[run], got_s[h * HALF]
+                elif term == "xq":
+                    w, w_s, a, a_s = wx_w[:, fp4_bytes].bitcast(FP4X4), wx_s[:, rows], xq_w[h], xq_s[h]
+                else:
+                    w, w_s, a, a_s = wx_w[:, fp4_bytes].bitcast(FP4X4), wx_s[:, rows], xr_w[h], xr_s[h]
+                at = (n - n0) * width + skip
+                first = j0 + skip - run if term in table_terms else x_first_token
+                nc.tensor.matmul_mx(
+                    out=sums[block][0][:, at : at + span], lhsT=w, lhsT_scale=w_s,
+                    rhs=a[:, first : first + span].bitcast(FP8X4), rhs_scale=a_s[:, scale_first : scale_first + span],
+                    start=opens_bank is not None and i == 0, stop=closes and i == len(passes) - 1,
+                )
 
-        def table_products(n):
-            product("wt4", n, 1, opens_bank=free_banks.pop(0))
-            product("wtd", n, 1)
-
-        def finish(n, h, first=0, width=HALF):
-            acc, bank_index = sums[n, h]
-            if h == 0 and n < HELD_RESULTS:
-                res = placed((on_chunk1, on_chunk2)[n // 2], "res%d" % n, [P, width], F32, n % 2 * RESULT_BYTES)
-            else:
-                res = results.tile([P, width], F32, name="res")
-            bias = b_first[:, 0:1] if (n, h) == (0, 0) else b_cols[:, n : n + 1]
-            nc.scalar.activation(out=res[:], in_=acc[:, 0:width], func=SILU, bias=bias)
-            j0 = h * HALF + first
-            nc.sync.dma_start(out=out[n * P : (n + 1) * P, j0 : j0 + width], in_=res[:])
+        def finish(block, res=None, bias=b_cols):
+            n0, count, j0, width = block
+            acc, bank_index = sums[block]
+            if res is None:
+                res = results.tile([P, count, width], F32, name="res")
+            for i in range(count):
+                nc.scalar.activation(
+                    out=res[:, i, :], in_=acc[:, i * width : (i + 1) * width], func=SILU,
+                    bias=bias[:, n0 + i : n0 + i + 1],
+                )
+            rows = out[n0 * P : (n0 + count) * P, j0 : j0 + width]
+            nc.sync.dma_start(out=rows.rearrange("(i p) j -> p i j", p=P), in_=res[:])
             free_banks.append(bank_index)
 
-        def close_pair(c):
-            for n in (2 * c, 2 * c + 1):
-                product("wtd", n, 0, closes=True)
-
-        def finish_pair(c):
-            for n in (2 * c, 2 * c + 1):
-                finish(n, 0)
+        wide = [(n, 1, 0, HALF) for n in range(TILES)]
+        third = [(2 * m, 2, HALF, CHUNK) for m in range(TILES // 2)]
+        fourth = HALF + CHUNK
+        table_terms, x_terms = ("wt4", "wtd"), ("xq", "xr")
 
         nc.gpsimd.memset(b_rows[:], 0.0)
-
         last = PACK - 1
         nc.gpsimd.memset(diagonal[:].bitcast(I32), 0)
         pairs = diagonal[:].bitcast(F32)
@@ -232,25 +228,23 @@ def tile_list_tiert_xdl_silu_kernel(
         for plane in (wx_s, tab_s, wt4_s):
             nc.vector.memset(plane[:].bitcast(I32), 0)
 
-        load_piece(0)
+        nc.sync.dma_start(out=x_first[0][:], in_=x_planes[:, :, 0:P])
         nc.sync.dma_start(out=b_rows[0:TILES, :], in_=b.rearrange("(c p) -> c p", p=P))
         for piece in range(1, PIECES):
-            load_piece(piece)
+            nc.sync.dma_start(out=x_first[piece][:], in_=x_planes[:, :, piece * P : (piece + 1) * P])
         load_scales(wx_s, wx_scales)
         nc.sync.dma_start(out=wx_w[:].bitcast(I32), in_=wx_words[0].bitcast(I32))
-        load_chunk(wtd_raw, wtd_planes, 0)
+        load_part(0)
         nc.sync.dma_start(offsets[:], offs)
         load_scales(tab_s, tab_scales)
         nc.sync.dma_start(out=tab_w[:], in_=tab_words[0].rearrange("p n t -> p (n t)").bitcast(I32))
-        for part in range(2):
-            lo = SPLIT_CHUNK * CHUNK + part * P
-            nc.sync.dma_start(out=wtd_part[part][:], in_=wtd_planes[:, :, lo : lo + P])
-            if part == 0:
-                load_scales(wt4_s, wt4_scales)
-            words = wt4_words[0][:, part * N : (part + 1) * N]
-            nc.sync.dma_start(out=wt4_w[part][:].bitcast(I32), in_=words.bitcast(I32))
-        load_chunk(wtd_raw, wtd_planes, 2)
+        load_scales(wt4_s, wt4_scales)
+        load_wt4(0)
+        load_part(1)
+        load_chunk(wtd_raw, wtd_planes, 1)
+        load_wt4(1)
         load_chunk(x_raw, x_planes, 2)
+        load_chunk(wtd_raw, wtd_planes, 2)
         load_chunk(x_raw, x_planes, 3)
         load_chunk(wtd_raw, wtd_planes, 3)
 
@@ -287,89 +281,102 @@ def tile_list_tiert_xdl_silu_kernel(
         for piece in range(PIECES):
             if piece in later_pieces:
                 round_piece(piece, *later_pieces[piece])
-            quantise_piece(piece)
+            quantise(xq_w, xq_s, piece * P, rounded[piece])
             dequantise(piece, PIECES + piece)
             if piece == 1:
                 residual(0)
         for piece in range(1, PIECES):
             residual(piece)
         nc.scalar.copy(out=b_cols[:], in_=b_turned[:, 0:TILES])
-        nc.scalar.copy(out=b_first[:, 0:1], in_=b_turned[:, 0:1])
         for n in range(PIECES):
-            product("xq", n, 0, opens_bank=n)
+            products(("xq",), wide[n], opens_bank=n)
         for c in (0, 1):
-            quantise_chunk(xr_w, xr_s, rest_bf, c)
+            quantise(xr_w, xr_s, c * CHUNK, rest_bf[c])
         for n in range(PIECES, TILES):
-            product("xq", n, 0, opens_bank=free_banks.pop(0))
+            products(("xq",), wide[n], opens_bank=free_banks.pop(0))
         for n in range(TILES):
-            product("xr", n, 0)
+            products(("xr",), wide[n])
 
-        got_s[0] = placed(shared, "got_s0", [P, HALF], U8, RESULT_BYTES)
-        gather(got_s[0], tab_s[:], 0)
-        got_w[0] = placed(shared, "got_w0", [P, HALF], U32, 0)
-        gather(got_w[0], tab_w[:].bitcast(U32), 0)
-        round_wtd(0, "rest_bf0")
-        quantise_chunk(wtd_w, wtd_s, wtd_bf, 0)
-        got_s[1] = tile("wtd_raw0", [P, HALF], U8)
-        gather(got_s[1], tab_s[:], 1)
-        wtd_bf[SPLIT_CHUNK] = tile("wtd_bf1", [P, CHUNK, PACK], BF16)
-        for part in range(2):
-            round_planes(nc.scalar.copy, wtd_bf[SPLIT_CHUNK][:, part * P : (part + 1) * P, :], wtd_part[part])
-        quantise_chunk(wtd_w, wtd_s, wtd_bf, SPLIT_CHUNK)
-        got_w[1] = placed(on_chunk1, "got_w1", [P, HALF], U32, 2 * RESULT_BYTES)
-        gather(got_w[1], tab_w[:].bitcast(U32), 1)
+        part_bf = [tile("rest_bf0", [P, P, PACK], BF16), tile("part_bf1", [P, P, PACK], BF16)]
+        round_planes(nc.scalar.copy, part_bf[0], wtd_part[0])
+        got_s[0] = placed(shared, "got_s0", [P, HALF], U8, 3 * RESULT_BYTES // 2)
+        gather(got_s[0][:], tab_s[:], 0)
+        quantise(wtd_w, wtd_s, 0, part_bf[0])
+        got_w[0] = placed(shared, "got_w0", [P, HALF], U32, RESULT_BYTES // 2)
+        table_words = tab_w[:].bitcast(U32)
+        for first in (0, CHUNK):
+            gather(got_w[0][:, first : first + CHUNK], table_words, first)
+        got_s[HALF] = placed(shared, "got_s1", [P, HALF], U8, 0)
+        gather(got_s[HALF][:], tab_s[:], HALF)
+        round_planes(nc.scalar.copy, part_bf[1], wtd_part[1])
+        quantise(wtd_w, wtd_s, P, part_bf[1])
+        got_w[HALF] = placed(on_part1, "got_w2", [P, CHUNK], U32, 0)
+        gather(got_w[HALF][:], table_words, HALF)
 
+        for first in (0, CHUNK):
+            for n in range(SPLIT_TILES):
+                products(("wt4",), wide[n], part=(first, CHUNK))
+        products(("wtd",), wide[0], closes=True)
+        for n in range(SPLIT_TILES, TILES):
+            products(("wt4",), wide[n])
+        products(("wtd",), wide[1], closes=True)
+        round_chunk(nc.scalar.copy, wtd_bf, wtd_raw, "wtd_bf", 1)
         for n in (0, 1):
-            product("wt4", n, 0)
-        close_pair(0)
-        for n in range(2, TILES):
-            product("wt4", n, 0)
-            if n == SECOND_PAIR_AFTER:
-                close_pair(1)
-        finish_pair(0)
-        round_wtd(2, "wtd_bf2")
-        finish_pair(1)
+            finish(wide[n], placed(on_chunk1, "res%d" % n, [P, 1, HALF], F32, n * RESULT_BYTES))
+        quantise(wtd_w, wtd_s, CHUNK, wtd_bf[1])
+        round_chunk(nc.vector.tensor_copy, x_bf, x_raw, "x_bf", 2)
+        quantise(xq_w, xq_s, 2 * CHUNK, x_bf[2])
+        round_chunk(nc.vector.tensor_copy, wtd_bf, wtd_raw, "wtd_bf", 2)
+        quantise(wtd_w, wtd_s, 2 * CHUNK, wtd_bf[2])
 
-        round_x(2)
-        quantise_chunk(wtd_w, wtd_s, wtd_bf, 2)
-        quantise_chunk(xq_w, xq_s, x_bf, 2)
-        for n in (0, 1):
-            table_products(n)
-        close_pair(2)
-        finish_pair(2)
-        round_wtd(3, "wtd_bf3")
-        for piece in (PIECES, PIECES + 1):
-            dequantise(piece, free_banks.pop(0))
-        round_x(3)
-        quantise_chunk(xq_w, xq_s, x_bf, 3)
-        for piece in (PIECES, PIECES + 1):
-            residual(piece)
-        for n in (0, 1):
-            product("xq", n, 1)
-        for piece in (PIECES + 2, PIECES + 3):
-            dequantise(piece, free_banks.pop(0))
-        residual(PIECES + 2)
-        quantise_chunk(wtd_w, wtd_s, wtd_bf, 3)
-        residual(PIECES + 3)
-        for c in (2, 3):
-            quantise_chunk(xr_w, xr_s, rest_bf, c)
         for n in (2, 3):
-            table_products(n)
-            product("xq", n, 1)
-        close_pair(3)
-        table_products(OPENED_EARLY - 1)
-        product("xq", OPENED_EARLY - 1, 1)
-        finish_pair(3)
-
-        for n in range(TILES - 1):
-            if n >= OPENED_EARLY:
-                table_products(n)
-                product("xq", n, 1)
-            product("xr", n, 1, closes=True)
-            finish(n, 1)
-
-        for first in range(0, HALF, P):
-            product("wt4", TILES - 1, 1, opens_bank=free_banks.pop(0), first=first, width=P)
-            for term in ("wtd", "xq", "xr"):
-                product(term, TILES - 1, 1, closes=term == "xr", first=first, width=P)
-            finish(TILES - 1, 1, first, P)
+            products(("wtd",), wide[n], closes=True)
+            finish(wide[n])
+        for m in (0, 1):
+            products(table_terms, third[m], opens_bank=free_banks.pop(0))
+        for m in (0, 1):
+            dequantise(4 + m, free_banks.pop(0))
+            products(("xq",), third[m])
+        for n in (4, 5):
+            products(("wtd",), wide[n], closes=True)
+        for piece in (6, 7):
+            rounded[piece] = tile("rounded%d" % piece, [P, P, PACK], BF16)
+            round_planes(nc.scalar.copy, rounded[piece], raw_piece(piece))
+        rest_bf[2] = tile("wtd_bf2", [P, CHUNK, PACK], BF16)
+        for piece in (4, 5):
+            residual(piece)
+        quantise(xq_w, xq_s, 6 * P, rounded[6])
+        quantise(xr_w, xr_s, 2 * CHUNK, rest_bf[2])
+        quantise(xq_w, xq_s, 7 * P, rounded[7])
+        wtd_bf[3] = placed(on_last, "wtd_bf3", [P, CHUNK, PACK], BF16, 0)
+        round_planes(nc.scalar.copy, wtd_bf[3], wtd_raw[3])
+        finish(wide[4], placed(on_chunk3, "res4", [P, 1, HALF], F32, 0))
+        finish(wide[5], placed(on_chunk3, "res5", [P, 1, HALF], F32, 2 * RESULT_BYTES + ALIGN))
+        b_late = placed(on_chunk3, "b_late", [P, TILES], F32, 2 * RESULT_BYTES)
+        quantise(wtd_w, wtd_s, 3 * CHUNK, wtd_bf[3])
+        nc.vector.tensor_copy(out=b_late[:], in_=b_cols[:])
+        products(table_terms + ("xq",), third[2], opens_bank=free_banks.pop(0))
+        dequantise(6, free_banks.pop(0))
+        for m in range(3):
+            products(("xr",), third[m], closes=True)
+            finish(third[m], bias=b_late)
+        dequantise(7, free_banks.pop(0))
+        rest_bf[3] = placed(on_chunk3, "rest_bf3", [P, CHUNK, PACK], BF16, RESULT_BYTES)
+        residual(6)
+        got_w[fourth] = placed(on_last, "got_w3", [P, CHUNK], U32, 0)
+        gather(got_w[fourth][:], table_words, fourth)
+        residual(7)
+        quantise(xr_w, xr_s, 3 * CHUNK, rest_bf[3])
+        for n in (6, 7):
+            products(("wtd",), wide[n], closes=True)
+            finish(wide[n])
+        products(table_terms + x_terms, third[3], opens_bank=free_banks.pop(0), closes=True)
+        finish(third[3])
+        for n0 in (0, 2):
+            pair = (n0, 2, fourth, CHUNK)
+            products(table_terms + x_terms, pair, opens_bank=free_banks.pop(0), closes=True)
+            finish(pair)
+        blocks = [(n, 1, fourth, CHUNK) for n in (4, 5, 6)] + [(7, 1, fourth, P), (7, 1, fourth + P, P)]
+        for block in blocks:
+            products(table_terms + x_terms, block, opens_bank=free_banks.pop(0), closes=True)
+            finish(block)

@@ -48,7 +48,6 @@ def tile_list_tiert_xdl_silu_kernel(
         shared = ctx.enter_context(tc.tile_pool(name="shared", bufs=1))
         on_eyes = ctx.enter_context(tc.tile_pool(name="on_eyes", bufs=1))
         on_diagonal = ctx.enter_context(tc.tile_pool(name="on_diagonal", bufs=1))
-        on_part1 = ctx.enter_context(tc.tile_pool(name="on_part1", bufs=1))
         on_chunk1 = ctx.enter_context(tc.tile_pool(name="on_chunk1", bufs=1))
         on_chunk3 = ctx.enter_context(tc.tile_pool(name="on_chunk3", bufs=1))
         on_last = ctx.enter_context(tc.tile_pool(name="on_last", bufs=1))
@@ -72,11 +71,11 @@ def tile_list_tiert_xdl_silu_kernel(
         wt4_w, wt4_s = tiles("wt4_w", 2, [P, N], U8), tile("wt4_s", [P, N], U8)
         wx_w, wx_s = tile("wx_w", [P, 2 * N], U8), tile("wx_s", [P, N], U8)
         x_first = tiles("x_first", PIECES - 1, [P, PACK, P], F32)
-        x_first.append(placed(shared, "x_first3", [P, PACK, P], F32, RESULT_BYTES))
+        x_first.append(placed(shared, "x_first3", [P, PACK, P], F32, 2 * RESULT_BYTES))
         x_raw = {c: tile("x_raw%d" % c, [P, PACK, CHUNK], F32) for c in (2, 3)}
-        wtd_part = [placed(shared, "wtd_part0", [P, PACK, P], F32, 0), placed(on_part1, "wtd_part1", [P, PACK, P], F32, 0)]
         wtd_raw = {2: tile("wtd_raw2", [P, PACK, CHUNK], F32)}
         wtd_raw[3] = placed(on_chunk3, "wtd_raw3", [P, PACK, CHUNK], F32, RESULT_BYTES // 2)
+        wtd_raw[0] = placed(shared, "wtd_raw0", [P, PACK, CHUNK], F32, 0)
         wtd_raw[1] = placed(on_chunk1, "wtd_raw1", [P, PACK, CHUNK], F32, 0)
         xq_w, xq_s = tiles("xq_w", 2, [P, HALF], U32), tiles("xq_s", 2, [P, HALF], U8)
         xr_w, xr_s = tiles("xr_w", 2, [P, HALF], U32), tiles("xr_s", 2, [P, HALF], U8)
@@ -100,9 +99,6 @@ def tile_list_tiert_xdl_silu_kernel(
 
         def load_chunk(raw, planes, c):
             nc.sync.dma_start(out=raw[c][:], in_=planes[:, :, c * CHUNK : (c + 1) * CHUNK])
-
-        def load_part(part):
-            nc.sync.dma_start(out=wtd_part[part][:], in_=wtd_planes[:, :, part * P : (part + 1) * P])
 
         def load_wt4(part):
             words = wt4_words[0][:, part * N : (part + 1) * N]
@@ -234,13 +230,12 @@ def tile_list_tiert_xdl_silu_kernel(
             nc.sync.dma_start(out=x_first[piece][:], in_=x_planes[:, :, piece * P : (piece + 1) * P])
         load_scales(wx_s, wx_scales)
         nc.sync.dma_start(out=wx_w[:].bitcast(I32), in_=wx_words[0].bitcast(I32))
-        load_part(0)
+        load_chunk(wtd_raw, wtd_planes, 0)
         nc.sync.dma_start(offsets[:], offs)
         load_scales(tab_s, tab_scales)
         nc.sync.dma_start(out=tab_w[:], in_=tab_words[0].rearrange("p n t -> p (n t)").bitcast(I32))
         load_scales(wt4_s, wt4_scales)
         load_wt4(0)
-        load_part(1)
         load_chunk(wtd_raw, wtd_planes, 1)
         load_wt4(1)
         load_chunk(x_raw, x_planes, 2)
@@ -294,32 +289,33 @@ def tile_list_tiert_xdl_silu_kernel(
             quantise(xr_w, xr_s, c * CHUNK, rest_bf[c])
         for n in range(PIECES, TILES):
             products(("xq",), wide[n], opens_bank=free_banks.pop(0))
-        for n in range(TILES):
+        for first in (0, CHUNK):
+            for n in range(SPLIT_TILES):
+                products(("xr",), wide[n], part=(first, CHUNK))
+        for n in range(SPLIT_TILES, TILES):
             products(("xr",), wide[n])
 
-        part_bf = [tile("rest_bf0", [P, P, PACK], BF16), tile("part_bf1", [P, P, PACK], BF16)]
-        round_planes(nc.scalar.copy, part_bf[0], wtd_part[0])
-        got_s[0] = placed(shared, "got_s0", [P, HALF], U8, 3 * RESULT_BYTES // 2)
+        wtd_bf[0] = tile("rest_bf0", [P, CHUNK, PACK], BF16)
+        round_planes(nc.scalar.copy, wtd_bf[0], wtd_raw[0])
+        got_s[0] = placed(shared, "got_s0", [P, HALF], U8, 5 * RESULT_BYTES // 2)
         gather(got_s[0][:], tab_s[:], 0)
-        quantise(wtd_w, wtd_s, 0, part_bf[0])
-        got_w[0] = placed(shared, "got_w0", [P, HALF], U32, RESULT_BYTES // 2)
+        quantise(wtd_w, wtd_s, 0, wtd_bf[0])
+        got_w[0] = placed(shared, "got_w0", [P, HALF], U32, 3 * RESULT_BYTES // 2)
         table_words = tab_w[:].bitcast(U32)
         for first in (0, CHUNK):
             gather(got_w[0][:, first : first + CHUNK], table_words, first)
         got_s[HALF] = placed(shared, "got_s1", [P, HALF], U8, 0)
         gather(got_s[HALF][:], tab_s[:], HALF)
-        round_planes(nc.scalar.copy, part_bf[1], wtd_part[1])
-        quantise(wtd_w, wtd_s, P, part_bf[1])
-        got_w[HALF] = placed(on_part1, "got_w2", [P, CHUNK], U32, 0)
+        got_w[HALF] = placed(shared, "got_w2", [P, CHUNK], U32, RESULT_BYTES // 2)
         gather(got_w[HALF][:], table_words, HALF)
 
         for first in (0, CHUNK):
             for n in range(SPLIT_TILES):
                 products(("wt4",), wide[n], part=(first, CHUNK))
-        products(("wtd",), wide[0], closes=True)
+            products(("wtd",), wide[0], closes=first > 0, part=(first, CHUNK))
+        products(("wtd",), wide[1], closes=True)
         for n in range(SPLIT_TILES, TILES):
             products(("wt4",), wide[n])
-        products(("wtd",), wide[1], closes=True)
         round_chunk(nc.scalar.copy, wtd_bf, wtd_raw, "wtd_bf", 1)
         for n in (0, 1):
             finish(wide[n], placed(on_chunk1, "res%d" % n, [P, 1, HALF], F32, n * RESULT_BYTES))
@@ -342,7 +338,7 @@ def tile_list_tiert_xdl_silu_kernel(
         for piece in (6, 7):
             rounded[piece] = tile("rounded%d" % piece, [P, P, PACK], BF16)
             round_planes(nc.scalar.copy, rounded[piece], raw_piece(piece))
-        rest_bf[2] = tile("wtd_bf2", [P, CHUNK, PACK], BF16)
+        rest_bf[2] = tile("wtd_raw2", [P, CHUNK, PACK], BF16)
         for piece in (4, 5):
             residual(piece)
         quantise(xq_w, xq_s, 6 * P, rounded[6])

@@ -344,7 +344,7 @@ def tile_list_tiert_xdl_silu_kernel(
         quantise(xq_w, xq_s, 6 * P, rounded[6])
         quantise(xr_w, xr_s, 2 * CHUNK, rest_bf[2])
         quantise(xq_w, xq_s, 7 * P, rounded[7])
-        wtd_bf[3] = placed(on_last, "wtd_bf3", [P, CHUNK, PACK], BF16, 0)
+        wtd_bf[3] = placed(on_last, "wtd_bf3", [P, CHUNK, PACK], BF16, RESULT_BYTES // 2)
         round_planes(nc.scalar.copy, wtd_bf[3], wtd_raw[3])
         finish(wide[4], placed(on_chunk3, "res4", [P, 1, HALF], F32, 0))
         finish(wide[5], placed(on_chunk3, "res5", [P, 1, HALF], F32, 2 * RESULT_BYTES + ALIGN))
@@ -357,11 +357,11 @@ def tile_list_tiert_xdl_silu_kernel(
             products(("xr",), third[m], closes=True)
             finish(third[m], bias=b_late)
         dequantise(7, free_banks.pop(0))
-        rest_bf[3] = placed(on_chunk3, "rest_bf3", [P, CHUNK, PACK], BF16, RESULT_BYTES)
-        residual(6)
-        got_w[fourth] = placed(on_last, "got_w3", [P, CHUNK], U32, 0)
+        got_w[fourth] = placed(on_last, "got_w3", [P, CHUNK], U32, RESULT_BYTES // 2)
         gather(got_w[fourth][:], table_words, fourth)
-        residual(7)
+        rest_bf[3] = placed(on_last, "rest_bf3", [P, CHUNK, PACK], BF16, RESULT_BYTES)
+        for piece in (6, 7):
+            residual(piece)
         quantise(xr_w, xr_s, 3 * CHUNK, rest_bf[3])
         for n in (6, 7):
             products(("wtd",), wide[n], closes=True)

@@ -163,7 +163,6 @@ def tile_list_tiert_xdl_silu_kernel(
             skip, span = part if part else (0, width)
             h, x_first_token = divmod(j0 + skip, HALF)
             run = max(r for r in got_w if r <= j0 + skip) if terms[0] in table_terms else 0
-            scale_first = x_first_token
             passes = [(term, n) for term in terms for n in range(n0, n0 + count)]
             for i, (term, n) in enumerate(passes):
                 rows = slice(n * P, (n + 1) * P)
@@ -171,9 +170,9 @@ def tile_list_tiert_xdl_silu_kernel(
                 c, lo = divmod(n * P, CHUNK)
                 if term == "wt4":
                     half, at = divmod(2 * n * P, N)
-                    w, w_s, a, a_s = wt4_w[half][:, at : at + 2 * P].bitcast(FP4X4), wt4_s[:, rows], got_w[run], got_s[h * HALF]
+                    w, w_s, a, a_s = wt4_w[half][:, at : at + 2 * P].bitcast(FP4X4), wt4_s[:, rows], got_w[run], got_s[run]
                 elif term == "wtd":
-                    w, w_s, a, a_s = wtd_w[c][:, lo : lo + P].bitcast(FP8X4), wtd_s[c][:, lo : lo + P], got_w[run], got_s[h * HALF]
+                    w, w_s, a, a_s = wtd_w[c][:, lo : lo + P].bitcast(FP8X4), wtd_s[c][:, lo : lo + P], got_w[run], got_s[run]
                 elif term == "xq":
                     w, w_s, a, a_s = wx_w[:, fp4_bytes].bitcast(FP4X4), wx_s[:, rows], xq_w[h], xq_s[h]
                 else:
@@ -182,7 +181,7 @@ def tile_list_tiert_xdl_silu_kernel(
                 first = j0 + skip - run if term in table_terms else x_first_token
                 nc.tensor.matmul_mx(
                     out=sums[block][0][:, at : at + span], lhsT=w, lhsT_scale=w_s,
-                    rhs=a[:, first : first + span].bitcast(FP8X4), rhs_scale=a_s[:, scale_first : scale_first + span],
+                    rhs=a[:, first : first + span].bitcast(FP8X4), rhs_scale=a_s[:, first : first + span],
                     start=opens_bank is not None and i == 0, stop=closes and i == len(passes) - 1,
                 )
 
@@ -302,24 +301,28 @@ def tile_list_tiert_xdl_silu_kernel(
         quantise(wtd_w, wtd_s, 0, wtd_bf[0])
         got_w[0] = placed(shared, "got_w0", [P, HALF], U32, 3 * RESULT_BYTES // 2)
         table_words = tab_w[:].bitcast(U32)
-        for first in (0, CHUNK):
-            gather(got_w[0][:, first : first + CHUNK], table_words, first)
-        got_s[HALF] = placed(shared, "got_s1", [P, HALF], U8, 0)
+        first_runs = ((0, P), (P, P), (CHUNK, CHUNK))
+        for first, span in first_runs:
+            gather(got_w[0][:, first : first + span], table_words, first)
+        got_s[HALF] = placed(shared, "got_s2", [P, CHUNK], U8, 0)
         gather(got_s[HALF][:], tab_s[:], HALF)
         got_w[HALF] = placed(shared, "got_w2", [P, CHUNK], U32, RESULT_BYTES // 2)
         gather(got_w[HALF][:], table_words, HALF)
 
-        for first in (0, CHUNK):
+        for run in first_runs:
+            for n in (0, 1):
+                products(("wtd",), wide[n], part=run)
             for n in range(SPLIT_TILES):
-                products(("wt4",), wide[n], part=(first, CHUNK))
-            products(("wtd",), wide[0], closes=first > 0, part=(first, CHUNK))
-        products(("wtd",), wide[1], closes=True)
+                products(("wt4",), wide[n], closes=n < 2 and run == first_runs[-1], part=run)
         for n in range(SPLIT_TILES, TILES):
             products(("wt4",), wide[n])
-        round_chunk(nc.scalar.copy, wtd_bf, wtd_raw, "wtd_bf", 1)
+        part_bf = tiles("part_bf", 2, [P, P, PACK], BF16)
+        for part in (0, 1):
+            round_planes(nc.scalar.copy, part_bf[part], wtd_raw[1][:, :, part * P : (part + 1) * P])
         for n in (0, 1):
             finish(wide[n], placed(on_chunk1, "res%d" % n, [P, 1, HALF], F32, n * RESULT_BYTES))
-        quantise(wtd_w, wtd_s, CHUNK, wtd_bf[1])
+        for part in (0, 1):
+            quantise(wtd_w, wtd_s, CHUNK + part * P, part_bf[part])
         round_chunk(nc.vector.tensor_copy, x_bf, x_raw, "x_bf", 2)
         quantise(xq_w, xq_s, 2 * CHUNK, x_bf[2])
         round_chunk(nc.vector.tensor_copy, wtd_bf, wtd_raw, "wtd_bf", 2)
@@ -357,9 +360,11 @@ def tile_list_tiert_xdl_silu_kernel(
             products(("xr",), third[m], closes=True)
             finish(third[m], bias=b_late)
         dequantise(7, free_banks.pop(0))
-        got_w[fourth] = placed(on_last, "got_w3", [P, CHUNK], U32, RESULT_BYTES // 2)
+        got_s[fourth] = placed(on_last, "got_s3", [P, CHUNK], U8, RESULT_BYTES // 2)
+        gather(got_s[fourth][:], tab_s[:], fourth)
+        got_w[fourth] = placed(on_last, "got_w3", [P, CHUNK], U32, RESULT_BYTES // 2 + CHUNK)
         gather(got_w[fourth][:], table_words, fourth)
-        rest_bf[3] = placed(on_last, "rest_bf3", [P, CHUNK, PACK], BF16, RESULT_BYTES)
+        rest_bf[3] = placed(on_last, "rest_bf3", [P, CHUNK, PACK], BF16, RESULT_BYTES + CHUNK)
         for piece in (6, 7):
             residual(piece)
         quantise(xr_w, xr_s, 3 * CHUNK, rest_bf[3])

@@ -76,7 +76,7 @@ def tile_list_tiert_xdl_silu_kernel(
         wtd_raw = {2: tile("wtd_raw2", [P, PACK, CHUNK], F32)}
         wtd_raw[3] = placed(on_chunk3, "wtd_raw3", [P, PACK, CHUNK], F32, RESULT_BYTES // 2)
         wtd_raw[0] = placed(shared, "wtd_raw0", [P, PACK, CHUNK], F32, 0)
-        wtd_raw[1] = placed(on_chunk1, "wtd_raw1", [P, PACK, CHUNK], F32, 0)
+        wtd_raw[1] = placed(on_chunk1, "wtd_raw1", [P, PACK, CHUNK], F32, RESULT_BYTES // 2)
         xq_w, xq_s = tiles("xq_w", 2, [P, HALF], U32), tiles("xq_s", 2, [P, HALF], U8)
         xr_w, xr_s = tiles("xr_w", 2, [P, HALF], U32), tiles("xr_s", 2, [P, HALF], U8)
         wtd_w, wtd_s = tiles("wtd_w", N // CHUNK, [P, CHUNK], U32), tiles("wtd_s", N // CHUNK, [P, CHUNK], U8)
@@ -306,8 +306,6 @@ def tile_list_tiert_xdl_silu_kernel(
             gather(got_w[0][:, first : first + span], table_words, first)
         got_s[HALF] = placed(shared, "got_s2", [P, CHUNK], U8, 0)
         gather(got_s[HALF][:], tab_s[:], HALF)
-        got_w[HALF] = placed(shared, "got_w2", [P, CHUNK], U32, RESULT_BYTES // 2)
-        gather(got_w[HALF][:], table_words, HALF)
 
         for run in first_runs:
             for n in (0, 1):
@@ -317,12 +315,14 @@ def tile_list_tiert_xdl_silu_kernel(
         for n in range(SPLIT_TILES, TILES):
             products(("wt4",), wide[n])
         part_bf = tiles("part_bf", 2, [P, P, PACK], BF16)
-        for part in (0, 1):
-            round_planes(nc.scalar.copy, part_bf[part], wtd_raw[1][:, :, part * P : (part + 1) * P])
+        for part, copy in enumerate((nc.vector.tensor_copy, nc.scalar.copy)):
+            round_planes(copy, part_bf[part], wtd_raw[1][:, :, part * P : (part + 1) * P])
         for n in (0, 1):
-            finish(wide[n], placed(on_chunk1, "res%d" % n, [P, 1, HALF], F32, n * RESULT_BYTES))
+            finish(wide[n], placed(on_chunk1, "res%d" % n, [P, 1, HALF], F32, n * 3 * RESULT_BYTES // 2))
         for part in (0, 1):
             quantise(wtd_w, wtd_s, CHUNK + part * P, part_bf[part])
+        got_w[HALF] = placed(on_chunk1, "got_w2", [P, CHUNK], U32, RESULT_BYTES)
+        gather(got_w[HALF][:], table_words, HALF)
         round_chunk(nc.vector.tensor_copy, x_bf, x_raw, "x_bf", 2)
         quantise(xq_w, xq_s, 2 * CHUNK, x_bf[2])
         round_chunk(nc.vector.tensor_copy, wtd_bf, wtd_raw, "wtd_bf", 2)
@@ -347,12 +347,14 @@ def tile_list_tiert_xdl_silu_kernel(
         quantise(xq_w, xq_s, 6 * P, rounded[6])
         quantise(xr_w, xr_s, 2 * CHUNK, rest_bf[2])
         quantise(xq_w, xq_s, 7 * P, rounded[7])
-        wtd_bf[3] = placed(on_last, "wtd_bf3", [P, CHUNK, PACK], BF16, RESULT_BYTES // 2)
-        round_planes(nc.scalar.copy, wtd_bf[3], wtd_raw[3])
-        finish(wide[4], placed(on_chunk3, "res4", [P, 1, HALF], F32, 0))
-        finish(wide[5], placed(on_chunk3, "res5", [P, 1, HALF], F32, 2 * RESULT_BYTES + ALIGN))
+        last_bf = [placed(on_last, "last_bf0", [P, P, PACK], BF16, RESULT_BYTES), tile("last_bf1", [P, P, PACK], BF16)]
+        for part, copy in enumerate((nc.scalar.copy, nc.vector.tensor_copy)):
+            round_planes(copy, last_bf[part], wtd_raw[3][:, :, part * P : (part + 1) * P])
+        finish(wide[4])
+        finish(wide[5])
         b_late = placed(on_chunk3, "b_late", [P, TILES], F32, 2 * RESULT_BYTES)
-        quantise(wtd_w, wtd_s, 3 * CHUNK, wtd_bf[3])
+        for part in (0, 1):
+            quantise(wtd_w, wtd_s, 3 * CHUNK + part * P, last_bf[part])
         nc.vector.tensor_copy(out=b_late[:], in_=b_cols[:])
         products(table_terms + ("xq",), third[2], opens_bank=free_banks.pop(0))
         dequantise(6, free_banks.pop(0))
@@ -360,11 +362,11 @@ def tile_list_tiert_xdl_silu_kernel(
             products(("xr",), third[m], closes=True)
             finish(third[m], bias=b_late)
         dequantise(7, free_banks.pop(0))
-        got_s[fourth] = placed(on_last, "got_s3", [P, CHUNK], U8, RESULT_BYTES // 2)
+        got_s[fourth] = placed(on_last, "got_s3", [P, CHUNK], U8, RESULT_BYTES + ALIGN)
         gather(got_s[fourth][:], tab_s[:], fourth)
-        got_w[fourth] = placed(on_last, "got_w3", [P, CHUNK], U32, RESULT_BYTES // 2 + CHUNK)
+        got_w[fourth] = placed(on_last, "got_w3", [P, CHUNK], U32, RESULT_BYTES + 2 * ALIGN)
         gather(got_w[fourth][:], table_words, fourth)
-        rest_bf[3] = placed(on_last, "rest_bf3", [P, CHUNK, PACK], BF16, RESULT_BYTES + CHUNK)
+        rest_bf[3] = placed(on_last, "rest_bf3", [P, CHUNK, PACK], BF16, ALIGN)
         for piece in (6, 7):
             residual(piece)
         quantise(xr_w, xr_s, 3 * CHUNK, rest_bf[3])

@@ -75,7 +75,7 @@ def tile_list_tiert_xdl_silu_kernel(
         x_raw = {c: tile("x_raw%d" % c, [P, PACK, CHUNK], F32) for c in (2, 3)}
         wtd_raw = {2: tile("wtd_raw2", [P, PACK, CHUNK], F32)}
         wtd_raw[3] = placed(on_chunk3, "wtd_raw3", [P, PACK, CHUNK], F32, RESULT_BYTES // 2)
-        wtd_raw[0] = placed(shared, "wtd_raw0", [P, PACK, CHUNK], F32, 0)
+        wtd_raw[0] = tile("wtd_raw0", [P, PACK, CHUNK], F32)
         wtd_raw[1] = placed(on_chunk1, "wtd_raw1", [P, PACK, CHUNK], F32, RESULT_BYTES // 2)
         xq_w, xq_s = tiles("xq_w", 2, [P, HALF], U32), tiles("xq_s", 2, [P, HALF], U8)
         xr_w, xr_s = tiles("xr_w", 2, [P, HALF], U32), tiles("xr_s", 2, [P, HALF], U8)
@@ -170,9 +170,9 @@ def tile_list_tiert_xdl_silu_kernel(
                 c, lo = divmod(n * P, CHUNK)
                 if term == "wt4":
                     half, at = divmod(2 * n * P, N)
-                    w, w_s, a, a_s = wt4_w[half][:, at : at + 2 * P].bitcast(FP4X4), wt4_s[:, rows], got_w[run], got_s[run]
+                    w, w_s, a, a_s = wt4_w[half][:, at : at + 2 * P].bitcast(FP4X4), wt4_s[:, rows], got_w[run], got_s[h * HALF]
                 elif term == "wtd":
-                    w, w_s, a, a_s = wtd_w[c][:, lo : lo + P].bitcast(FP8X4), wtd_s[c][:, lo : lo + P], got_w[run], got_s[run]
+                    w, w_s, a, a_s = wtd_w[c][:, lo : lo + P].bitcast(FP8X4), wtd_s[c][:, lo : lo + P], got_w[run], got_s[h * HALF]
                 elif term == "xq":
                     w, w_s, a, a_s = wx_w[:, fp4_bytes].bitcast(FP4X4), wx_s[:, rows], xq_w[h], xq_s[h]
                 else:
@@ -181,7 +181,7 @@ def tile_list_tiert_xdl_silu_kernel(
                 first = j0 + skip - run if term in table_terms else x_first_token
                 nc.tensor.matmul_mx(
                     out=sums[block][0][:, at : at + span], lhsT=w, lhsT_scale=w_s,
-                    rhs=a[:, first : first + span].bitcast(FP8X4), rhs_scale=a_s[:, first : first + span],
+                    rhs=a[:, first : first + span].bitcast(FP8X4), rhs_scale=a_s[:, x_first_token : x_first_token + span],
                     start=opens_bank is not None and i == 0, stop=closes and i == len(passes) - 1,
                 )
 
@@ -223,20 +223,20 @@ def tile_list_tiert_xdl_silu_kernel(
         for plane in (wx_s, tab_s, wt4_s):
             nc.vector.memset(plane[:].bitcast(I32), 0)
 
+        nc.sync.dma_start(offsets[:], offs)
         nc.sync.dma_start(out=x_first[0][:], in_=x_planes[:, :, 0:P])
         nc.sync.dma_start(out=b_rows[0:TILES, :], in_=b.rearrange("(c p) -> c p", p=P))
         for piece in range(1, PIECES):
             nc.sync.dma_start(out=x_first[piece][:], in_=x_planes[:, :, piece * P : (piece + 1) * P])
         load_scales(wx_s, wx_scales)
         nc.sync.dma_start(out=wx_w[:].bitcast(I32), in_=wx_words[0].bitcast(I32))
-        load_chunk(wtd_raw, wtd_planes, 0)
-        nc.sync.dma_start(offsets[:], offs)
+        load_wt4(0)
         load_scales(tab_s, tab_scales)
         nc.sync.dma_start(out=tab_w[:], in_=tab_words[0].rearrange("p n t -> p (n t)").bitcast(I32))
         load_scales(wt4_s, wt4_scales)
-        load_wt4(0)
-        load_chunk(wtd_raw, wtd_planes, 1)
+        load_chunk(wtd_raw, wtd_planes, 0)
         load_wt4(1)
+        load_chunk(wtd_raw, wtd_planes, 1)
         load_chunk(x_raw, x_planes, 2)
         load_chunk(wtd_raw, wtd_planes, 2)
         load_chunk(x_raw, x_planes, 3)
@@ -294,26 +294,27 @@ def tile_list_tiert_xdl_silu_kernel(
         for n in range(SPLIT_TILES, TILES):
             products(("xr",), wide[n])
 
-        wtd_bf[0] = tile("rest_bf0", [P, CHUNK, PACK], BF16)
-        round_planes(nc.scalar.copy, wtd_bf[0], wtd_raw[0])
         got_s[0] = placed(shared, "got_s0", [P, HALF], U8, 5 * RESULT_BYTES // 2)
         gather(got_s[0][:], tab_s[:], 0)
-        quantise(wtd_w, wtd_s, 0, wtd_bf[0])
         got_w[0] = placed(shared, "got_w0", [P, HALF], U32, 3 * RESULT_BYTES // 2)
         table_words = tab_w[:].bitcast(U32)
         first_runs = ((0, P), (P, P), (CHUNK, CHUNK))
         for first, span in first_runs:
             gather(got_w[0][:, first : first + span], table_words, first)
-        got_s[HALF] = placed(shared, "got_s2", [P, CHUNK], U8, 0)
+        got_s[HALF] = placed(shared, "got_s1", [P, HALF], U8, 5 * RESULT_BYTES // 2 + HALF)
         gather(got_s[HALF][:], tab_s[:], HALF)
+        first_bf = tiles("first_bf", 2, [P, P, PACK], BF16)
+        for part in (0, 1):
+            round_planes(nc.scalar.copy, first_bf[part], wtd_raw[0][:, :, part * P : (part + 1) * P])
+            quantise(wtd_w, wtd_s, part * P, first_bf[part])
 
         for run in first_runs:
-            for n in (0, 1):
-                products(("wtd",), wide[n], part=run)
             for n in range(SPLIT_TILES):
-                products(("wt4",), wide[n], closes=n < 2 and run == first_runs[-1], part=run)
+                products(("wt4",), wide[n], part=run)
         for n in range(SPLIT_TILES, TILES):
             products(("wt4",), wide[n])
+            if n in (SPLIT_TILES + 1, SPLIT_TILES + 2):
+                products(("wtd",), wide[n - SPLIT_TILES - 1], closes=True)
         part_bf = tiles("part_bf", 2, [P, P, PACK], BF16)
         for part, copy in enumerate((nc.vector.tensor_copy, nc.scalar.copy)):
             round_planes(copy, part_bf[part], wtd_raw[1][:, :, part * P : (part + 1) * P])
@@ -362,8 +363,6 @@ def tile_list_tiert_xdl_silu_kernel(
             products(("xr",), third[m], closes=True)
             finish(third[m], bias=b_late)
         dequantise(7, free_banks.pop(0))
-        got_s[fourth] = placed(on_last, "got_s3", [P, CHUNK], U8, RESULT_BYTES + ALIGN)
-        gather(got_s[fourth][:], tab_s[:], fourth)
         got_w[fourth] = placed(on_last, "got_w3", [P, CHUNK], U32, RESULT_BYTES + 2 * ALIGN)
         gather(got_w[fourth][:], table_words, fourth)
         rest_bf[3] = placed(on_last, "rest_bf3", [P, CHUNK, PACK], BF16, ALIGN)

@@ -23,7 +23,7 @@ TILES = N // P
 PIECES = HALF // P
 RUN = 2
 ALIGN = 256
-RESULT_BUFS = 20
+RESULT_BUFS = 14
 SPLIT_TILES = 4
 WARM_PASSES = 10
 WARM_BANK = PIECES - 1
@@ -76,7 +76,7 @@ def tile_list_tiert_xdl_silu_kernel(
         wtd_raw = {2: tile("wtd_raw2", [P, PACK, CHUNK], F32)}
         wtd_raw[3] = placed(on_chunk3, "wtd_raw3", [P, PACK, CHUNK], F32, RESULT_BYTES // 2)
         wtd_raw[0] = tile("wtd_raw0", [P, PACK, CHUNK], F32)
-        wtd_raw[1] = placed(on_chunk1, "wtd_raw1", [P, PACK, CHUNK], F32, RESULT_BYTES // 2)
+        wtd_raw[1] = placed(on_chunk1, "wtd_raw1", [P, PACK, CHUNK], F32, 3 * RESULT_BYTES)
         xq_w, xq_s = tiles("xq_w", 2, [P, HALF], U32), tiles("xq_s", 2, [P, HALF], U8)
         xr_w, xr_s = tiles("xr_w", 2, [P, HALF], U32), tiles("xr_s", 2, [P, HALF], U8)
         wtd_w, wtd_s = tiles("wtd_w", N // CHUNK, [P, CHUNK], U32), tiles("wtd_s", N // CHUNK, [P, CHUNK], U8)
@@ -185,19 +185,24 @@ def tile_list_tiert_xdl_silu_kernel(
                     start=opens_bank is not None and i == 0, stop=closes and i == len(passes) - 1,
                 )
 
-        def finish(block, res=None, bias=b_cols):
-            n0, count, j0, width = block
-            acc, bank_index = sums[block]
+        def finish(*blocks, res=None, bias=b_cols, n0=None, stores=True):
+            n0 = blocks[0][0] if n0 is None else n0
+            j0, width = blocks[0][2], blocks[0][3]
             if res is None:
-                res = results.tile([P, count, width], F32, name="res")
-            for i in range(count):
-                nc.scalar.activation(
-                    out=res[:, i, :], in_=acc[:, i * width : (i + 1) * width], func=SILU,
-                    bias=bias[:, n0 + i : n0 + i + 1],
-                )
-            rows = out[n0 * P : (n0 + count) * P, j0 : j0 + width]
-            nc.sync.dma_start(out=rows.rearrange("(i p) j -> p i j", p=P), in_=res[:])
-            free_banks.append(bank_index)
+                res = results.tile([P, sum(block[1] for block in blocks), width], F32, name="res")
+            total = res.shape[1]
+            for block in blocks:
+                acc, bank_index = sums[block]
+                for i in range(block[1]):
+                    n = block[0] + i
+                    nc.scalar.activation(
+                        out=res[:, n - n0, :], in_=acc[:, i * width : (i + 1) * width], func=SILU,
+                        bias=bias[:, n : n + 1],
+                    )
+                free_banks.append(bank_index)
+            if stores:
+                rows = out[n0 * P : (n0 + total) * P, j0 : j0 + width]
+                nc.sync.dma_start(out=rows.rearrange("(i p) j -> p i j", p=P), in_=res[:])
 
         wide = [(n, 1, 0, HALF) for n in range(TILES)]
         third = [(2 * m, 2, HALF, CHUNK) for m in range(TILES // 2)]
@@ -298,7 +303,7 @@ def tile_list_tiert_xdl_silu_kernel(
         gather(got_s[0][:], tab_s[:], 0)
         got_w[0] = placed(shared, "got_w0", [P, HALF], U32, 3 * RESULT_BYTES // 2)
         table_words = tab_w[:].bitcast(U32)
-        first_runs = ((0, P), (P, P), (CHUNK, CHUNK))
+        first_runs = ((0, CHUNK), (CHUNK, CHUNK))
         for first, span in first_runs:
             gather(got_w[0][:, first : first + span], table_words, first)
         got_s[HALF] = placed(shared, "got_s1", [P, HALF], U8, 5 * RESULT_BYTES // 2 + HALF)
@@ -318,11 +323,11 @@ def tile_list_tiert_xdl_silu_kernel(
         part_bf = tiles("part_bf", 2, [P, P, PACK], BF16)
         for part, copy in enumerate((nc.vector.tensor_copy, nc.scalar.copy)):
             round_planes(copy, part_bf[part], wtd_raw[1][:, :, part * P : (part + 1) * P])
-        for n in (0, 1):
-            finish(wide[n], placed(on_chunk1, "res%d" % n, [P, 1, HALF], F32, n * 3 * RESULT_BYTES // 2))
+        upper_rows = placed(on_chunk1, "upper_rows", [P, 4, HALF], F32, 0)
+        finish(wide[0], wide[1], res=upper_rows, stores=False)
         for part in (0, 1):
             quantise(wtd_w, wtd_s, CHUNK + part * P, part_bf[part])
-        got_w[HALF] = placed(on_chunk1, "got_w2", [P, CHUNK], U32, RESULT_BYTES)
+        got_w[HALF] = placed(on_chunk1, "got_w2", [P, CHUNK], U32, 4 * RESULT_BYTES)
         gather(got_w[HALF][:], table_words, HALF)
         round_chunk(nc.vector.tensor_copy, x_bf, x_raw, "x_bf", 2)
         quantise(xq_w, xq_s, 2 * CHUNK, x_bf[2])
@@ -331,7 +336,7 @@ def tile_list_tiert_xdl_silu_kernel(
 
         for n in (2, 3):
             products(("wtd",), wide[n], closes=True)
-            finish(wide[n])
+        finish(wide[2], wide[3], res=upper_rows, n0=0)
         for m in (0, 1):
             products(table_terms, third[m], opens_bank=free_banks.pop(0))
         for m in (0, 1):
@@ -351,8 +356,7 @@ def tile_list_tiert_xdl_silu_kernel(
         last_bf = [placed(on_last, "last_bf0", [P, P, PACK], BF16, RESULT_BYTES), tile("last_bf1", [P, P, PACK], BF16)]
         for part, copy in enumerate((nc.scalar.copy, nc.vector.tensor_copy)):
             round_planes(copy, last_bf[part], wtd_raw[3][:, :, part * P : (part + 1) * P])
-        finish(wide[4])
-        finish(wide[5])
+        finish(wide[4], wide[5])
         b_late = placed(on_chunk3, "b_late", [P, TILES], F32, 2 * RESULT_BYTES)
         for part in (0, 1):
             quantise(wtd_w, wtd_s, 3 * CHUNK + part * P, last_bf[part])
@@ -361,7 +365,8 @@ def tile_list_tiert_xdl_silu_kernel(
         dequantise(6, free_banks.pop(0))
         for m in range(3):
             products(("xr",), third[m], closes=True)
-            finish(third[m], bias=b_late)
+        finish(third[0], third[1], bias=b_late)
+        finish(third[2], bias=b_late)
         dequantise(7, free_banks.pop(0))
         got_w[fourth] = placed(on_last, "got_w3", [P, CHUNK], U32, RESULT_BYTES + 2 * ALIGN)
         gather(got_w[fourth][:], table_words, fourth)
@@ -371,7 +376,7 @@ def tile_list_tiert_xdl_silu_kernel(
         quantise(xr_w, xr_s, 3 * CHUNK, rest_bf[3])
         for n in (6, 7):
             products(("wtd",), wide[n], closes=True)
-            finish(wide[n])
+        finish(wide[6], wide[7])
         products(table_terms + x_terms, third[3], opens_bank=free_banks.pop(0), closes=True)
         finish(third[3])
         for n0 in (0, 2):
@@ -379,6 +384,9 @@ def tile_list_tiert_xdl_silu_kernel(
             products(table_terms + x_terms, pair, opens_bank=free_banks.pop(0), closes=True)
             finish(pair)
         blocks = [(n, 1, fourth, CHUNK) for n in (4, 5, 6)] + [(7, 1, fourth, P), (7, 1, fourth + P, P)]
-        for block in blocks:
+        for block in blocks[:2]:
+            products(table_terms + x_terms, block, opens_bank=free_banks.pop(0), closes=True)
+        finish(*blocks[:2])
+        for block in blocks[2:]:
             products(table_terms + x_terms, block, opens_bank=free_banks.pop(0), closes=True)
             finish(block)

@@ -303,7 +303,7 @@ def tile_list_tiert_xdl_silu_kernel(
         gather(got_s[0][:], tab_s[:], 0)
         got_w[0] = placed(shared, "got_w0", [P, HALF], U32, 3 * RESULT_BYTES // 2)
         table_words = tab_w[:].bitcast(U32)
-        first_runs = ((0, CHUNK), (CHUNK, CHUNK))
+        first_runs = ((0, P), (P, P), (CHUNK, CHUNK))
         for first, span in first_runs:
             gather(got_w[0][:, first : first + span], table_words, first)
         got_s[HALF] = placed(shared, "got_s1", [P, HALF], U8, 5 * RESULT_BYTES // 2 + HALF)

@@ -25,6 +25,7 @@ RUN = 2
 ALIGN = 256
 RESULT_BUFS = 14
 SPLIT_TILES = 4
+WT4_FIRST = 6 * 2 * P
 WARM_PASSES = 10
 WARM_BANK = PIECES - 1
 RESULT_BYTES = 4 * HALF
@@ -68,7 +69,8 @@ def tile_list_tiert_xdl_silu_kernel(
 
         offsets = keep.tile([P, J // 16], U16, name="offsets")
         tab_w, tab_s = tile("tab_w", [P, T], I32), tile("tab_s", [P, T], U8)
-        wt4_w, wt4_s = tiles("wt4_w", 2, [P, N], U8), tile("wt4_s", [P, N], U8)
+        wt4_w = [tile("wt4_w0", [P, WT4_FIRST], U8), tile("wt4_w1", [P, 2 * N - WT4_FIRST], U8)]
+        wt4_s = tile("wt4_s", [P, N], U8)
         wx_w, wx_s = tile("wx_w", [P, 2 * N], U8), tile("wx_s", [P, N], U8)
         x_first = tiles("x_first", PIECES - 1, [P, PACK, P], F32)
         x_first.append(placed(shared, "x_first3", [P, PACK, P], F32, 2 * RESULT_BYTES))
@@ -101,7 +103,7 @@ def tile_list_tiert_xdl_silu_kernel(
             nc.sync.dma_start(out=raw[c][:], in_=planes[:, :, c * CHUNK : (c + 1) * CHUNK])
 
         def load_wt4(part):
-            words = wt4_words[0][:, part * N : (part + 1) * N]
+            words = wt4_words[0][:, (0, WT4_FIRST)[part] : (WT4_FIRST, 2 * N)[part]]
             nc.sync.dma_start(out=wt4_w[part][:].bitcast(I32), in_=words.bitcast(I32))
 
         def round_planes(copy, dst, src):
@@ -169,7 +171,7 @@ def tile_list_tiert_xdl_silu_kernel(
                 fp4_bytes = slice(2 * n * P, 2 * (n + 1) * P)
                 c, lo = divmod(n * P, CHUNK)
                 if term == "wt4":
-                    half, at = divmod(2 * n * P, N)
+                    half, at = divmod(2 * n * P, WT4_FIRST)
                     w, w_s, a, a_s = wt4_w[half][:, at : at + 2 * P].bitcast(FP4X4), wt4_s[:, rows], got_w[run], got_s[h * HALF]
                 elif term == "wtd":
                     w, w_s, a, a_s = wtd_w[c][:, lo : lo + P].bitcast(FP8X4), wtd_s[c][:, lo : lo + P], got_w[run], got_s[h * HALF]
@@ -240,8 +242,8 @@ def tile_list_tiert_xdl_silu_kernel(
         nc.sync.dma_start(out=tab_w[:], in_=tab_words[0].rearrange("p n t -> p (n t)").bitcast(I32))
         load_scales(wt4_s, wt4_scales)
         load_chunk(wtd_raw, wtd_planes, 0)
-        load_wt4(1)
         load_chunk(wtd_raw, wtd_planes, 1)
+        load_wt4(1)
         load_chunk(x_raw, x_planes, 2)
         load_chunk(wtd_raw, wtd_planes, 2)
         load_chunk(x_raw, x_planes, 3)
@@ -303,7 +305,7 @@ def tile_list_tiert_xdl_silu_kernel(
         gather(got_s[0][:], tab_s[:], 0)
         got_w[0] = placed(shared, "got_w0", [P, HALF], U32, 3 * RESULT_BYTES // 2)
         table_words = tab_w[:].bitcast(U32)
-        first_runs = ((0, P), (P, P), (CHUNK, CHUNK))
+        first_runs = ((0, CHUNK), (CHUNK, CHUNK))
         for first, span in first_runs:
             gather(got_w[0][:, first : first + span], table_words, first)
         got_s[HALF] = placed(shared, "got_s1", [P, HALF], U8, 5 * RESULT_BYTES // 2 + HALF)
@@ -318,8 +320,9 @@ def tile_list_tiert_xdl_silu_kernel(
                 products(("wt4",), wide[n], part=run)
         for n in range(SPLIT_TILES, TILES):
             products(("wt4",), wide[n])
-            if n in (SPLIT_TILES + 1, SPLIT_TILES + 2):
-                products(("wtd",), wide[n - SPLIT_TILES - 1], closes=True)
+            if n == SPLIT_TILES + 1:
+                for early in (0, 1):
+                    products(("wtd",), wide[early], closes=True)
         part_bf = tiles("part_bf", 2, [P, P, PACK], BF16)
         for part, copy in enumerate((nc.vector.tensor_copy, nc.scalar.copy)):
             round_planes(copy, part_bf[part], wtd_raw[1][:, :, part * P : (part + 1) * P])

from contextlib import ExitStack

import concourse.mybir as mybir

K, L, N, T, J = 512, 512, 1024, 2048, 1024
FLOPS = 4 * 2 * K * N * J + 2 * L * L * J

F32 = mybir.dt.float32
BF16 = mybir.dt.bfloat16
I32 = mybir.dt.int32
U32 = mybir.dt.uint32
U16 = mybir.dt.uint16
U8 = mybir.dt.uint8
FP8X4 = mybir.dt.float8_e4m3fn_x4
FP4X4 = mybir.dt.float4_e2m1fn_x4
SILU = mybir.ActivationFunctionType.Silu

P = 128
PACK = 4
HALF = 512
CHUNK = 256
TILES = N // P
PIECES = HALF // P
RUN = 2
ALIGN = 256
RESULT_BUFS = 14
SPLIT_TILES = 4
WT4_FIRST = 6 * 2 * P
WARM_PASSES = 10
WARM_BANK = PIECES - 1
RESULT_BYTES = 4 * HALF
PIECE_BYTES = 2 * PACK * P


def packed_by_runs(ap):
    return ap.rearrange("p (c i) t -> p c t i", i=RUN)


def planes_by_runs(ap):
    return ap.rearrange("p t (c i) -> p c t i", i=RUN)


def tile_list_tiert_xdl_silu_kernel(
    tc, tab_words, tab_scales, wt4_words, wt4_scales, wtd, x, wx_words, wx_scales, b, offs, out
):
    nc = tc.nc
    with ExitStack() as ctx:
        keep = ctx.enter_context(tc.tile_pool(name="keep", bufs=1))
        shared = ctx.enter_context(tc.tile_pool(name="shared", bufs=1))
        on_eyes = ctx.enter_context(tc.tile_pool(name="on_eyes", bufs=1))
        on_diagonal = ctx.enter_context(tc.tile_pool(name="on_diagonal", bufs=1))
        on_chunk1 = ctx.enter_context(tc.tile_pool(name="on_chunk1", bufs=1))
        on_chunk3 = ctx.enter_context(tc.tile_pool(name="on_chunk3", bufs=1))
        on_last = ctx.enter_context(tc.tile_pool(name="on_last", bufs=1))
        results = ctx.enter_context(tc.tile_pool(name="results", bufs=RESULT_BUFS))
        psum = ctx.enter_context(tc.psum_pool(name="psum", bufs=1))

        def bank(i):
            return psum.tile([P, HALF], F32, name="bank%d" % i)

        def tile(name, shape, dtype):
            return keep.tile(shape, dtype, name=name, align_bytes=ALIGN)

        def placed(pool, name, shape, dtype, offset):
            return pool.tile(shape, dtype, name=name, align_bytes=ALIGN, offset=offset)

        def tiles(name, count, shape, dtype):
            return [tile("%s%d" % (name, i), shape, dtype) for i in range(count)]

        offsets = keep.tile([P, J // 16], U16, name="offsets")
        tab_w, tab_s = tile("tab_w", [P, T], I32), tile("tab_s", [P, T], U8)
        wt4_w = [tile("wt4_w0", [P, WT4_FIRST], U8), tile("wt4_w1", [P, 2 * N - WT4_FIRST], U8)]
        wt4_s = tile("wt4_s", [P, N], U8)
        wx_w, wx_s = tile("wx_w", [P, 2 * N], U8), tile("wx_s", [P, N], U8)
        x_first = tiles("x_first", PIECES - 1, [P, PACK, P], F32)
        x_first.append(placed(shared, "x_first3", [P, PACK, P], F32, 2 * RESULT_BYTES))
        x_raw = {c: tile("x_raw%d" % c, [P, PACK, CHUNK], F32) for c in (2, 3)}
        wtd_raw = {2: tile("wtd_raw2", [P, PACK, CHUNK], F32)}
        wtd_raw[3] = placed(on_chunk3, "wtd_raw3", [P, PACK, CHUNK], F32, RESULT_BYTES // 2)
        wtd_raw[0] = tile("wtd_raw0", [P, PACK, CHUNK], F32)
        wtd_raw[1] = placed(on_chunk1, "wtd_raw1", [P, PACK, CHUNK], F32, 3 * RESULT_BYTES)
        xq_w, xq_s = tiles("xq_w", 2, [P, HALF], U32), tiles("xq_s", 2, [P, HALF], U8)
        xr_w, xr_s = tiles("xr_w", 2, [P, HALF], U32), tiles("xr_s", 2, [P, HALF], U8)
        wtd_w, wtd_s = tiles("wtd_w", N // CHUNK, [P, CHUNK], U32), tiles("wtd_s", N // CHUNK, [P, CHUNK], U8)
        eye_w, eye_s = tile("eye_w", [P, PACK * P], U32), tile("eye_s", [P, PACK * P], U8)
        eye_f32 = keep.tile([P, P], F32, name="eye_f32")
        eye_bf = placed(on_eyes, "eye_bf", [P, PACK - 1, P * PACK], BF16, 0)
        diagonal = placed(on_diagonal, "diagonal", [P, P * PACK + PACK], BF16, 0)
        b_rows = tile("b_rows", [P, P], F32)
        b_cols = keep.tile([P, TILES], F32, name="b_cols")
        table_warm = keep.tile([P, 8], F32, name="table_warm")
        rounded, x_bf, wtd_bf, rest_bf, got_w, got_s, back, sums = {}, {}, {}, {}, {}, {}, {}, {}
        free_banks = []

        x_planes = x.rearrange("(p t) j -> p t j", t=PACK)
        wtd_planes = wtd.rearrange("(p t) n -> p t n", t=PACK)

        def load_scales(plane, rows):
            for r in range(4):
                nc.sync.dma_start(out=plane[r:P:32, :].bitcast(I32), in_=rows[0, r:16:4, :].bitcast(I32))

        def load_chunk(raw, planes, c):
            nc.sync.dma_start(out=raw[c][:], in_=planes[:, :, c * CHUNK : (c + 1) * CHUNK])

        def load_wt4(part):
            words = wt4_words[0][:, (0, WT4_FIRST)[part] : (WT4_FIRST, 2 * N)[part]]
            nc.sync.dma_start(out=wt4_w[part][:].bitcast(I32), in_=words.bitcast(I32))

        def round_planes(copy, dst, src):
            copy(out=packed_by_runs(dst[:, :, :]), in_=planes_by_runs(src[:, :, :]))

        def raw_piece(piece):
            c, lo = divmod(piece * P, CHUNK)
            return x_first[piece][:] if piece < PIECES else x_raw[c][:, :, lo : lo + P]

        def round_piece(piece, copy, pool, offset):
            rounded[piece] = placed(pool, "rounded%d" % piece, [P, P, PACK], BF16, offset)
            round_planes(copy, rounded[piece], raw_piece(piece))

        def round_chunk(copy, dst, raw, name, c):
            dst[c] = tile("%s%d" % (name, c), [P, CHUNK, PACK], BF16)
            round_planes(copy, dst[c], raw[c])

        def quantise(words, scales, first, src):
            i, lo = divmod(first, words[0].shape[1])
            columns = slice(lo, lo + src.shape[1])
            nc.vector.quantize_mx(
                out=words[i][:, columns].bitcast(FP8X4), scales=scales[i][:, columns],
                in_=src[:].rearrange("p c t -> p (c t)"),
            )

        def dequantise(piece, bank_index):
            h, lo = divmod(piece * P, HALF)
            back[piece] = (bank(bank_index), bank_index)
            for t in range(PACK):
                columns = slice(t * P, (t + 1) * P)
                nc.tensor.matmul_mx(
                    out=back[piece][0][:, columns],
                    lhsT=eye_w[:, columns].bitcast(FP8X4), lhsT_scale=eye_s[:, columns],
                    rhs=xq_w[h][:, lo : lo + P].bitcast(FP8X4), rhs_scale=xq_s[h][:, lo : lo + P],
                    start=True, stop=True,
                )

        def residual(piece):
            c, lo = divmod(piece * P, CHUNK)
            if c not in rest_bf:
                rest_bf[c] = tile("rest_bf%d" % c, [P, CHUNK, PACK], BF16)
            values, bank_index = back[piece]
            nc.vector.tensor_tensor(
                out=packed_by_runs(rest_bf[c][:, lo : lo + P, :]),
                in0=planes_by_runs(raw_piece(piece)),
                in1=values[:].rearrange("p (t c i) -> p c t i", t=PACK, i=RUN),
                op=mybir.AluOpType.subtract,
            )
            free_banks.append(bank_index)

        def gather(dst, table, j0):
            entries = offsets[:, j0 // 16 : (j0 + dst.shape[1]) // 16]
            nc.vector.tensor_copy(out=dst, in_=table.indirect(entries))

        def products(terms, block, opens_bank=None, closes=False, part=None):
            n0, count, j0, width = block
            if opens_bank is not None:
                sums[block] = (bank(opens_bank), opens_bank)
            skip, span = part if part else (0, width)
            h, x_first_token = divmod(j0 + skip, HALF)
            run = max(r for r in got_w if r <= j0 + skip) if terms[0] in table_terms else 0
            passes = [(term, n) for term in terms for n in range(n0, n0 + count)]
            for i, (term, n) in enumerate(passes):
                rows = slice(n * P, (n + 1) * P)
                fp4_bytes = slice(2 * n * P, 2 * (n + 1) * P)
                c, lo = divmod(n * P, CHUNK)
                if term == "wt4":
                    half, at = divmod(2 * n * P, WT4_FIRST)
                    w, w_s, a, a_s = wt4_w[half][:, at : at + 2 * P].bitcast(FP4X4), wt4_s[:, rows], got_w[run], got_s[h * HALF]
                elif term == "wtd":
                    w, w_s, a, a_s = wtd_w[c][:, lo : lo + P].bitcast(FP8X4), wtd_s[c][:, lo : lo + P], got_w[run], got_s[h * HALF]
                elif term == "xq":
                    w, w_s, a, a_s = wx_w[:, fp4_bytes].bitcast(FP4X4), wx_s[:, rows], xq_w[h], xq_s[h]
                else:
                    w, w_s, a, a_s = wx_w[:, fp4_bytes].bitcast(FP4X4), wx_s[:, rows], xr_w[h], xr_s[h]
                at = (n - n0) * width + skip
                first = j0 + skip - run if term in table_terms else x_first_token
                nc.tensor.matmul_mx(
                    out=sums[block][0][:, at : at + span], lhsT=w, lhsT_scale=w_s,
                    rhs=a[:, first : first + span].bitcast(FP8X4), rhs_scale=a_s[:, x_first_token : x_first_token + span],
                    start=opens_bank is not None and i == 0, stop=closes and i == len(passes) - 1,
                )

        def finish(*blocks, res=None, bias=b_cols, n0=None, stores=True):
            n0 = blocks[0][0] if n0 is None else n0
            j0, width = blocks[0][2], blocks[0][3]
            if res is None:
                res = results.tile([P, sum(block[1] for block in blocks), width], F32, name="res")
            total = res.shape[1]
            for block in blocks:
                acc, bank_index = sums[block]
                for i in range(block[1]):
                    n = block[0] + i
                    nc.scalar.activation(
                        out=res[:, n - n0, :], in_=acc[:, i * width : (i + 1) * width], func=SILU,
                        bias=bias[:, n : n + 1],
                    )
                free_banks.append(bank_index)
            if stores:
                rows = out[n0 * P : (n0 + total) * P, j0 : j0 + width]
                nc.sync.dma_start(out=rows.rearrange("(i p) j -> p i j", p=P), in_=res[:])

        wide = [(n, 1, 0, HALF) for n in range(TILES)]
        third = [(2 * m, 2, HALF, CHUNK) for m in range(TILES // 2)]
        fourth = HALF + CHUNK
        table_terms, x_terms = ("wt4", "wtd"), ("xq", "xr")

        nc.gpsimd.memset(b_rows[:], 0.0)
        last = PACK - 1
        nc.gpsimd.memset(diagonal[:].bitcast(I32), 0)
        pairs = diagonal[:].bitcast(F32)
        nc.gpsimd.affine_select(
            out=pairs, in_=pairs, pattern=[[1, (P * PACK + PACK) // 2]], compare_op=mybir.AluOpType.not_equal,
            fill=1.0, base=-1, channel_multiplier=-2,
        )
        last_eye = slice(last * P, PACK * P)
        nc.vector.quantize_mx(
            out=eye_w[:, last_eye].bitcast(FP8X4), scales=eye_s[:, last_eye], in_=diagonal[:, 0 : P * PACK]
        )

        nc.vector.memset(table_warm[:], 0.0)
        nc.scalar.activation(out=table_warm[:], in_=table_warm[:], func=SILU)

        for plane in (wx_s, tab_s, wt4_s):
            nc.vector.memset(plane[:].bitcast(I32), 0)

        nc.sync.dma_start(offsets[:], offs)
        nc.sync.dma_start(out=x_first[0][:], in_=x_planes[:, :, 0:P])
        nc.sync.dma_start(out=b_rows[0:TILES, :], in_=b.rearrange("(c p) -> c p", p=P))
        for piece in range(1, PIECES):
            nc.sync.dma_start(out=x_first[piece][:], in_=x_planes[:, :, piece * P : (piece + 1) * P])
        load_scales(wx_s, wx_scales)
        nc.sync.dma_start(out=wx_w[:].bitcast(I32), in_=wx_words[0].bitcast(I32))
        load_wt4(0)
        load_scales(tab_s, tab_scales)
        nc.sync.dma_start(out=tab_w[:], in_=tab_words[0].rearrange("p n t -> p (n t)").bitcast(I32))
        load_scales(wt4_s, wt4_scales)
        load_chunk(wtd_raw, wtd_planes, 0)
        load_chunk(wtd_raw, wtd_planes, 1)
        load_wt4(1)
        load_chunk(x_raw, x_planes, 2)
        load_chunk(wtd_raw, wtd_planes, 2)
        load_chunk(x_raw, x_planes, 3)
        load_chunk(wtd_raw, wtd_planes, 3)

        for t in (2, 1):
            nc.vector.tensor_copy(out=eye_bf[:, t, :], in_=diagonal[:, last - t : last - t + P * PACK])
        eye_row = eye_bf[:].rearrange("p t c -> p (t c)")
        nc.scalar.copy(out=eye_bf[:, 0, :], in_=eye_row[:, P * PACK + 1 : 2 * P * PACK + 1])
        nc.scalar.copy(out=eye_f32[:], in_=eye_bf[:, 2, 2 : P * PACK : PACK])
        round_piece(0, nc.vector.tensor_copy, on_diagonal, 0)
        for lo, hi in ((1, last), (0, 1)):
            columns = slice(lo * P, hi * P)
            nc.vector.quantize_mx(
                out=eye_w[:, columns].bitcast(FP8X4), scales=eye_s[:, columns],
                in_=eye_bf[:, lo:hi, :].rearrange("p t c -> p (t c)"),
            )

        idle = bank(WARM_BANK)
        for warm_pass in range(WARM_PASSES):
            nc.tensor.matmul_mx(
                out=idle[:, 0:P],
                lhsT=eye_w[:, last_eye].bitcast(FP8X4), lhsT_scale=eye_s[:, last_eye],
                rhs=eye_w[:, last_eye].bitcast(FP8X4), rhs_scale=eye_s[:, last_eye],
                start=True, stop=True,
            )

        b_turned = bank(WARM_BANK)
        nc.tensor.transpose(b_turned[:, 0:P], b_rows[:], eye_f32[:])

        later_pieces = {
            1: (nc.scalar.copy, on_diagonal, PIECE_BYTES),
            2: (nc.vector.tensor_copy, on_diagonal, 0),
            3: (nc.scalar.copy, on_eyes, 0),
        }
        for piece in range(PIECES):
            if piece in later_pieces:
                round_piece(piece, *later_pieces[piece])
            quantise(xq_w, xq_s, piece * P, rounded[piece])
            dequantise(piece, PIECES + piece)
            if piece == 1:
                residual(0)
        for piece in range(1, PIECES):
            residual(piece)
        nc.scalar.copy(out=b_cols[:], in_=b_turned[:, 0:TILES])
        for n in range(PIECES):
            products(("xq",), wide[n], opens_bank=n)
        for c in (0, 1):
            quantise(xr_w, xr_s, c * CHUNK, rest_bf[c])
        for n in range(PIECES, TILES):
            products(("xq",), wide[n], opens_bank=free_banks.pop(0))
        for first in (0, CHUNK):
            for n in range(SPLIT_TILES):
                products(("xr",), wide[n], part=(first, CHUNK))
        for n in range(SPLIT_TILES, TILES):
            products(("xr",), wide[n])

        got_s[0] = placed(shared, "got_s0", [P, HALF], U8, 5 * RESULT_BYTES // 2)
        gather(got_s[0][:], tab_s[:], 0)
        got_w[0] = placed(shared, "got_w0", [P, HALF], U32, 3 * RESULT_BYTES // 2)
        table_words = tab_w[:].bitcast(U32)
        first_runs = ((0, CHUNK), (CHUNK, CHUNK))
        for first, span in first_runs:
            gather(got_w[0][:, first : first + span], table_words, first)
        got_s[HALF] = placed(shared, "got_s1", [P, HALF], U8, 5 * RESULT_BYTES // 2 + HALF)
        gather(got_s[HALF][:], tab_s[:], HALF)
        first_bf = tiles("first_bf", 2, [P, P, PACK], BF16)
        for part in (0, 1):
            round_planes(nc.scalar.copy, first_bf[part], wtd_raw[0][:, :, part * P : (part + 1) * P])
            quantise(wtd_w, wtd_s, part * P, first_bf[part])

        for run in first_runs:
            for n in range(SPLIT_TILES):
                products(("wt4",), wide[n], part=run)
        for n in range(SPLIT_TILES, TILES):
            products(("wt4",), wide[n])
            if n == SPLIT_TILES + 1:
                for early in (0, 1):
                    products(("wtd",), wide[early], closes=True)
        part_bf = tiles("part_bf", 2, [P, P, PACK], BF16)
        for part, copy in enumerate((nc.vector.tensor_copy, nc.scalar.copy)):
            round_planes(copy, part_bf[part], wtd_raw[1][:, :, part * P : (part + 1) * P])
        upper_rows = placed(on_chunk1, "upper_rows", [P, 4, HALF], F32, 0)
        finish(wide[0], wide[1], res=upper_rows, stores=False)
        for part in (0, 1):
            quantise(wtd_w, wtd_s, CHUNK + part * P, part_bf[part])
        got_w[HALF] = placed(on_chunk1, "got_w2", [P, CHUNK], U32, 4 * RESULT_BYTES)
        gather(got_w[HALF][:], table_words, HALF)
        round_chunk(nc.vector.tensor_copy, x_bf, x_raw, "x_bf", 2)
        quantise(xq_w, xq_s, 2 * CHUNK, x_bf[2])
        round_chunk(nc.vector.tensor_copy, wtd_bf, wtd_raw, "wtd_bf", 2)
        quantise(wtd_w, wtd_s, 2 * CHUNK, wtd_bf[2])

        for n in (2, 3):
            products(("wtd",), wide[n], closes=True)
        finish(wide[2], wide[3], res=upper_rows, n0=0)
        for m in (0, 1):
            products(table_terms, third[m], opens_bank=free_banks.pop(0))
        for m in (0, 1):
            dequantise(4 + m, free_banks.pop(0))
            products(("xq",), third[m])
        for n in (4, 5):
            products(("wtd",), wide[n], closes=True)
        for piece in (6, 7):
            rounded[piece] = tile("rounded%d" % piece, [P, P, PACK], BF16)
            round_planes(nc.scalar.copy, rounded[piece], raw_piece(piece))
        rest_bf[2] = tile("wtd_raw2", [P, CHUNK, PACK], BF16)
        for piece in (4, 5):
            residual(piece)
        quantise(xq_w, xq_s, 6 * P, rounded[6])
        quantise(xr_w, xr_s, 2 * CHUNK, rest_bf[2])
        quantise(xq_w, xq_s, 7 * P, rounded[7])
        last_bf = [placed(on_last, "last_bf0", [P, P, PACK], BF16, RESULT_BYTES), tile("last_bf1", [P, P, PACK], BF16)]
        for part, copy in enumerate((nc.scalar.copy, nc.vector.tensor_copy)):
            round_planes(copy, last_bf[part], wtd_raw[3][:, :, part * P : (part + 1) * P])
        finish(wide[4], wide[5])
        b_late = placed(on_chunk3, "b_late", [P, TILES], F32, 2 * RESULT_BYTES)
        for part in (0, 1):
            quantise(wtd_w, wtd_s, 3 * CHUNK + part * P, last_bf[part])
        nc.vector.tensor_copy(out=b_late[:], in_=b_cols[:])
        products(table_terms + ("xq",), third[2], opens_bank=free_banks.pop(0))
        dequantise(6, free_banks.pop(0))
        for m in range(3):
            products(("xr",), third[m], closes=True)
        finish(third[0], third[1], bias=b_late)
        finish(third[2], bias=b_late)
        dequantise(7, free_banks.pop(0))
        got_w[fourth] = placed(on_last, "got_w3", [P, CHUNK], U32, RESULT_BYTES + 2 * ALIGN)
        gather(got_w[fourth][:], table_words, fourth)
        rest_bf[3] = placed(on_last, "rest_bf3", [P, CHUNK, PACK], BF16, ALIGN)
        for piece in (6, 7):
            residual(piece)
        quantise(xr_w, xr_s, 3 * CHUNK, rest_bf[3])
        for n in (6, 7):
            products(("wtd",), wide[n], closes=True)
        finish(wide[6], wide[7])
        products(table_terms + x_terms, third[3], opens_bank=free_banks.pop(0), closes=True)
        finish(third[3])
        for n0 in (0, 2):
            pair = (n0, 2, fourth, CHUNK)
            products(table_terms + x_terms, pair, opens_bank=free_banks.pop(0), closes=True)
            finish(pair)
        blocks = [(n, 1, fourth, CHUNK) for n in (4, 5, 6)] + [(7, 1, fourth, P), (7, 1, fourth + P, P)]
        for block in blocks[:2]:
            products(table_terms + x_terms, block, opens_bank=free_banks.pop(0), closes=True)
        finish(*blocks[:2])
        for block in blocks[2:]:
            products(table_terms + x_terms, block, opens_bank=free_banks.pop(0), closes=True)
            finish(block)
